import numpy as np, ml_dtypes
CORES = [2,3,42,43,82,83,122,123]
N = 8
import mx_ref
BF = ml_dtypes.bfloat16
def pick(q, e):
    c = np.concatenate([q[0].reshape(128, -1, 4), np.zeros((128, 1, 4), np.uint8)], axis=1); s = np.concatenate([q[1], np.ones((16, 1), np.uint8)], axis=1)
    return (np.ascontiguousarray(c[:, e].reshape(128, -1)), np.ascontiguousarray(s[:, e]))
def join(*qs):
    return (np.concatenate([q[0] for q in qs], axis=1), np.concatenate([q[1] for q in qs], axis=1))
def put(q, e, v):
    c, s = q[0].reshape(128, -1, 4).copy(), q[1].copy(); c[:, e] = v[0].reshape(128, -1, 4); s[:, e] = v[1]
    return (c.reshape(128, -1), s)
def pk(c, s):
    return (np.ascontiguousarray(c), mx_ref.live(s))
def emit(q):
    return q[0], q[1]
def decode(q):
    o = []
    for b in range(4):
        e = np.zeros((128, 128, 4), np.float32); e[np.arange(128), np.arange(128), b] = 1
        o.append(mx_ref.matmul(mx_ref.quantize(e.reshape(128, 512).astype(BF)), q))
    return np.stack(o, axis=2).reshape(128, -1)
def cut(t, i, w=512):
    return t[:, w * i:w * i + w]
def f(rng, *shape):
    return mx_ref.flush((rng.standard_normal(shape, dtype=np.float32) * np.exp2(rng.integers(-2, 3, shape[:-1] + (1,)))).astype(BF))
def wide(rng, *shape, cols=0):
    v = rng.standard_normal(shape, dtype=np.float32) * np.exp2(rng.integers(-12, 13, shape)).astype(np.float32)
    if cols: v *= np.repeat(np.exp2(rng.integers(-cols, cols + 1, shape[:-2] + (1, shape[-1] // 4))) * (rng.random(shape[:-2] + (1, shape[-1] // 4)) > 0.0625), 4, axis=-1).astype(np.float32)
    return mx_ref.flush(v.astype(BF))
P, K, O, L = 512, 128, 1, 3
def times(t, v):
    v = t.astype(np.float32) * np.asarray(v, np.float32)
    return np.where(np.abs(v) < 2.0 ** -16, 0, v).astype(np.float32).astype(BF)
def loud(u, e):
    v = u.astype(np.float32) * np.float32(2.0 ** e)
    return np.where(np.abs(v) < 2.0 ** -30, 0, v).astype(np.float32).astype(BF)
def strong(rng, u, n):
    return np.sign(u[0, :, None, :4].astype(np.float32)) * (1 + rng.random((128, n, 4))) * 128
def near(rng, u):
    ku, v = mx_ref.quantize(np.ascontiguousarray(u[0])), np.repeat(strong(rng, u, 1), 12, axis=1).astype(np.float32)
    v[127] = 0
    z = size(ku, mx_ref.quantize(np.ascontiguousarray(v.reshape(128, -1).astype(BF))))
    v[127, 1:, 0] = np.exp2(np.floor(np.log2(z[0])) - 23 + np.arange(11))
    z = size(ku, mx_ref.quantize(np.ascontiguousarray(v.reshape(128, -1).astype(BF))))
    return v[:, [0, int(np.argmax(z > z[0]))]]
def plain(rng):
    k = np.exp2(6 * rng.random(P) - 3) * np.exp2(rng.random((N, P)) - 0.5)
    u = np.zeros((N, 128, 512), BF)
    u[:, :, :4] = f(rng, 128, 4)
    return {"gr": times(f(rng, N, 128, 4 * P), np.repeat(k, 4, axis=1)[:, None]), "u": u, "w": f(rng, N, 128, 512 * O)}
def setup_inputs(rng):
    return plain(rng)
def setup_inputs_apart(rng):
    d, h = plain(rng), K // 2
    d["u"][:, :8] = 0
    d["u"][:, 120:] = 0
    d["u"][:, 127, 0] = 1
    g = d["gr"].astype(np.float32).reshape(N, 128, P, 4) * np.float32(2.0 ** -8)
    x = rng.permutation(P)[:N // 2 * K].reshape(N // 2, 2, h)
    c = near(rng, d["u"])
    for j in range(N // 2):
        rest = rng.permutation(np.setdiff1d(np.arange(P), x[j].reshape(-1)))[:K].reshape(2, h)
        for i in range(2):
            v = c[:, (x[j, i] >= P // 2).astype(int)]
            v[:8] = (1 + rng.random((8, h, 4))) * 128 * rng.choice([-1.0, 1.0], (8, h, 4))
            g[2 * j + i][:, x[j, i]] = v * np.exp2(rng.integers(0, 3, h))[:, None]
            g[2 * j + i][:, rest[i]] = strong(rng, d["u"], h) * 2.0 ** -4
    d["gr"] = times(g.reshape(N, 128, -1), 1)
    return d
def setup_inputs_cancel(rng):
    d, m = plain(rng), K // 8
    g = d["gr"].astype(np.float32).reshape(N, 128, P, 4)
    e = rng.permutation(P)[:3 * L * m].reshape(L, 3, m)
    g[:, :, e.reshape(-1)] = 0
    for b in range(L):
        for r in range(N):
            h = (r >> b) & 1
            g[r][:, e[b, 1 + h]] = strong(rng, d["u"], m)
            if r % (1 << b) == 0:
                g[r][:, e[b, 0]] = -g[r - (1 << b)][:, e[b, 0]] if h else strong(rng, d["u"], m)
    d["gr"] = times(g.reshape(N, 128, -1), 2.0 ** -10)
    d["u"] = loud(d["u"], -26)
    return d
def setup_inputs_few(rng):
    d, m, h = plain(rng), K // 8, N // 2
    d["u"][:, :64] = 0
    g = d["gr"].astype(np.float32).reshape(N, 128, P, 4)
    g[:, 64:] = 0
    g *= (np.arange(P) % 4 != rng.integers(0, 4, (N, 1)))[:, None, :, None]
    low, e = rng.permutation(K // 4)[:m], K + rng.permutation(P - K)[:(h + 3) * m].reshape(h + 3, m)
    c = np.concatenate([low, e[0]])
    for r in range(N):
        own = e[3 + r] if r < h else e[1:3].reshape(-1)
        g[r][:, own] += strong(rng, d["u"], own.size)
        if r % 2: g[r][:, c] = -g[r - 1][:, c]
        else: g[r][:, c] += strong(rng, d["u"], c.size)
    d["gr"] = times(g.reshape(N, 128, -1), 1)
    d["u"] = loud(d["u"], 24)
    return d
def setup_inputs_spread(rng):
    d = plain(rng)
    e = rng.permutation(P)[:K]
    k = np.exp2(rng.integers(-12, -5, (N, P))) * (rng.random((N, P)) > 0.0625)
    k[:, e] = np.exp2(rng.integers(0, 7, (N, K))) * rng.choice([-1.0, 1.0], (N, K))
    g = wide(rng, N, 128, 4 * P).astype(np.float32).reshape(N, 128, P, 4)
    g[:, :, e] = np.abs(g[:, :, e]) * np.sign(d["u"][0, :, None, :4].astype(np.float32))
    d["gr"] = times(g.reshape(N, 128, -1), np.repeat(k, 4, axis=1)[:, None])
    return d
def setup_inputs_ties(rng):
    d = plain(rng)
    x = f(rng, 128, 24).astype(np.float32).reshape(128, 6, 4)
    h = np.stack([rng.permutation(P) % 6 for r in range(N)])
    sign = rng.choice([-1.0, 1.0], (N, 1, P, 1))
    d["gr"] = times((np.moveaxis(x[:, h], 1, 0) * sign).reshape(N, 128, -1), 1)
    return d
def check_inputs(d):
    b = []
    for k, lo, hi in (("gr", -16, 24), ("u", -30, 30), ("w", -30, 30)):
        v = np.abs(d[k].astype(np.float32))
        if not (np.isfinite(v).all() and ((v == 0) | (v >= 2.0 ** lo) & (v <= 2.0 ** hi)).all()): b.append("a value of " + k)
    v = d["u"].astype(np.float32)
    if (v[:, :, 4:] != 0).any(): b.append("u has numbers behind its column 0")
    if (v != v[:1]).any(): b.append("u isn't the same on all ranks")
    return b
def size(ku, q):
    return np.abs(mx_ref.matmul(ku, q)[0])
def best(s):
    return np.sort(np.argsort(-s, kind="stable")[:K])
def merge(ku, a, b):
    i, j = np.intersect1d(a[0], b[0], return_indices=True)[1:]
    q = join(a[1], b[1])
    v = decode(q).reshape(128, 2 * K, 4)
    v[:, i] = v[:, i] + v[:, K + j]
    q = put(q, i, pick(mx_ref.quantize(np.ascontiguousarray(v.reshape(128, -1).astype(BF))), i))
    n = np.concatenate([a[0], b[0]])
    e = np.setdiff1d(np.arange(2 * K), K + j)
    e = e[np.argsort(n[e])]
    e = e[best(size(ku, q)[e])]
    return n[e], pick(q, e)
def reference(gr, u, w):
    ku, S = [mx_ref.quantize(np.ascontiguousarray(u[r])) for r in range(N)], []
    for r in range(N):
        q = mx_ref.quantize(np.ascontiguousarray(gr[r]))
        e = best(size(ku[r], q))
        S.append((e, pick(q, e)))
    for b in range(L):
        new = list(S)
        for r in range(N):
            p = r ^ (1 << b)
            if r < p: new[r] = new[p] = merge(ku[r], S[r], S[p])
        S = new
    oc, osc = np.zeros((N, 128, 4 * K), np.uint8), np.zeros((N, 16, K), np.uint8)
    nb, y = np.zeros((N, 1, K), np.float32), np.zeros((N, 128, O * K), np.float32)
    for r in range(N):
        oc[r], osc[r] = emit(S[r][1])
        nb[r, 0] = S[r][0]
        for o in range(O): y[r, :, o * K:o * K + K] = mx_ref.matmul(mx_ref.quantize(np.ascontiguousarray(cut(w[r], o))), S[r][1])
    return {"oc": oc, "osc": osc, "nb": nb, "y": y}

@@ -1,0 +1,451 @@
+from concourse.mybir import dt, AluOpType as Op, AxisListType, ActivationFunctionType as Act
+
+K, P, L = 128, 512, 3
+A0, B0, M0 = 256, 384, 128
+TINY = 2.0 ** -100
+ULP = 2.0 ** -24
+NONE = 255.0
+SNAP = 1.5 * 2.0 ** 27
+
+SCRATCH = {}
+
+
+def _buf(name, cols, dtype, where="sbuf"):
+    SCRATCH[name] = (where, [128, cols], dtype)
+
+
+def _codes(name, cols):
+    _buf(name, cols, "float8_e4m3fn_x4")
+    _buf(name + "s", cols, "uint8")
+
+
+for _n, _c in (("ones", 512), ("ident", 128), ("tri", 128), ("tbn", 128), ("m16", 128), ("rs16", 128), ("i128", 128), ("iN", 512),
+               ("u4", 4), ("ut", 4 * 264), ("grt", 2048), ("wt", 512), ("cwt", 1536), ("et", 2560), ("dg", 512), ("ot0", 512), ("otr", 512),
+               ("tk", 512), ("nlt", 1024), ("sg0", 512), ("sg1", 512), ("c0", 512), ("c1", 512), ("rs", 1024), ("ye", 512), ("yj", 128),
+               ("xm", 128), ("sc", 128), ("xd", 128), ("xp", 128), ("xj", 128), ("posr", 128), ("mk", 128), ("um", 128), ("hm", 512),
+               ("ca", 256), ("cb", 256), ("lta", 128), ("ltb", 256), ("sca", 128), ("scb", 128), ("nw0", 512), ("nw1", 512), ("nw2", 512),
+               ("flag", 6), ("ta0", 512), ("ta1", 512), ("ta2", 512)):
+    _buf(_n, _c, "bfloat16")
+for _n, _c in (("ij", 128), ("idf", 128), ("pi", 2), ("tj", 128), ("td", 128), ("tp", 4)):
+    _buf(_n, _c, "int32")
+for _n, _c in (("pf", 4), ("f0", 128), ("t0", 128), ("ar", 512), ("small", 40), ("absa", 128), ("arow", 256), ("sbs", 128), ("sbm", 128),
+               ("absm", 128), ("ta", 128), ("tb", 256), ("nbo", 128), ("yw", 512), ("yo", 128)):
+    _buf(_n, _c, "float32")
+for _n in ("lw0", "lw1", "lw2", "lw3", "na1", "na2", "nb0", "nb1", "nb2", "off0", "off1", "off2"):
+    _buf(_n, 8, "uint16")
+for _n, _c in (("cu", 264), ("qg", 512), ("qw", 128), ("cw", 384), ("ce", 640), ("nq", 128), ("nl", 128), ("qo0", 128), ("qor", 128),
+               ("qe", 128), ("qtk", 128), ("qlt", 256), ("w0", 512), ("w1", 512), ("w2", 512), ("w3", 128), ("ap0", 128), ("ap1", 128), ("ap2", 128)):
+    _codes(_n, _c)
+SMALL = {"acol": (0, 8)}
+for _i, _n in enumerate(("aac", "ada", "sbt", "sbd", "acb", "acd", "nac", "nbc", "unc", "umc", "mkc", "tka", "tkb", "tku", "tkm")):
+    SMALL[_n] = (8 + 2 * _i, 2)
+for _i in range(8):
+    _buf("p%d" % _i, 512, "float32", "psum")
+SEMAPHORES = ["sv", "sa", "st", "sp", "sent", "ac0", "ac1", "ac2", "an0", "an1", "an2", "ready"] + ["d%d" % i for i in range(16)]
+
+
+def rank_program(g, core, T, topo):
+    rank = T.rank_of(core)
+    if rank is None:
+        return
+    Q = {"v": g.vector, "a": g.scalar, "t": g.tensor, "p": g, "s": g.sync}
+    ESEM = {"v": "sv", "a": "sa", "t": "st", "p": "sp"}
+    total, known, hist, recs = {}, {e: {} for e in Q}, {}, {}
+
+    def meet(x, y):
+        if x[1] >= y[2] or y[1] >= x[2]:
+            return False
+        return not (x[3] == y[3] and x[3] > 1 and (x[1] - y[1]) % x[3])
+
+    def waits(e, outs, ins):
+        need = {}
+        for regs, isw in ((ins, False), (outs, True)):
+            for r in regs:
+                ps = SCRATCH[r[0]][0] == "psum"
+                for q, w, s, c, e2 in recs.get(r[0], []):
+                    if ps:
+                        if e2 == e and (e == "t" or not (w or isw)):
+                            continue
+                    elif not (w or isw) or not meet(r, q):
+                        continue
+                    need[s] = max(need.get(s, 0), c)
+        for s in sorted(need):
+            c = need[s]
+            if known[e].get(s, 0) < c:
+                Q[e].wait_ge(T.sem[s], c)
+                known[e][s] = c
+                for s2, c2 in hist.get((s, c), {}).items():
+                    if known[e].get(s2, 0) < c2:
+                        known[e][s2] = c2
+
+    def note(s, c, e, outs, ins):
+        for regs, w in ((ins, False), (outs, True)):
+            for r in regs:
+                recs.setdefault(r[0], []).append((r, w, s, c, e))
+
+    def op(e, call, outs, ins):
+        waits(e, outs, ins)
+        s = ESEM[e]
+        total[s] = total.get(s, 0) + 1
+        call(Q[e]).then_inc(T.sem[s], 1)
+        hist[(s, total[s])] = dict(known[e])
+        hist[(s, total[s])][s] = total[s]
+        note(s, total[s], e, outs, ins)
+
+    nd = [0]
+
+    def dma(e, out, in_, outs, ins):
+        waits(e, outs, ins)
+        s = "d%d" % nd[0]
+        nd[0] += 1
+        total[s] = 16
+        Q[e].dma_start(out, in_).then_inc(T.sem[s], 16)
+        hist[(s, 16)] = dict(known[e])
+        note(s, 16, "dma", outs, ins)
+
+    def R(n, a=0, b=None, st=1):
+        if n in SMALL:
+            o, width = SMALL[n]
+            return ("small", o + a, o + (width if b is None else b), st)
+        return (n, a, SCRATCH[n][1][1] if b is None else b, st)
+
+    def ap(r):
+        if r[3] == 1:
+            return T[r[0]][:, r[1]:r[2]]
+        return T[r[0]][:, r[1]:r[2]:r[3]]
+
+    def S(r):
+        return (r[0] + "s",) + r[1:]
+
+    def isr(x):
+        return isinstance(x, tuple)
+
+    def sap(x):
+        return ap(x) if isr(x) else x
+
+    def fill(r, c):
+        op("v", lambda q: q.memset(ap(r), c), [r], [])
+
+    def copy(o, i, e="v"):
+        if e == "v":
+            op("v", lambda q: q.tensor_copy(ap(o), ap(i)), [o], [i])
+        else:
+            op("a", lambda q: q.activation(ap(o), ap(i), Act.Copy), [o], [i])
+
+    def act(o, i, f, bias=0.0, scale=1.0, acc=None):
+        ins = [i] + [x for x in (bias, scale) if isr(x)]
+        if acc is None:
+            op("a", lambda q: q.activation(ap(o), ap(i), f, bias=sap(bias), scale=sap(scale)), [o], ins)
+        else:
+            op("a", lambda q: q.activation(ap(o), ap(i), f, accum_out=ap(acc)), [o, acc], ins)
+
+    def tt(o, a, b, f):
+        op("v", lambda q: q.tensor_tensor(ap(o), ap(a), ap(b), f), [o], [a, b])
+
+    def ts(o, i, s1, f1, s2=None, f2=None):
+        ins = [i] + [x for x in (s1, s2) if isr(x)]
+        if f2 is None:
+            op("v", lambda q: q.tensor_scalar(ap(o), ap(i), sap(s1), None, f1), [o], ins)
+        else:
+            op("v", lambda q: q.tensor_scalar(ap(o), ap(i), sap(s1), sap(s2), f1, f2), [o], ins)
+
+    def scan(o, a, b, f0, f1):
+        op("v", lambda q: q.tensor_tensor_scan(ap(o), ap(a), ap(b), 0.0, f0, f1), [o], [a, b])
+
+    def iota(o, pat, base, cm, flag=False):
+        if flag:
+            op("p", lambda q: q.iota(ap(o), pat, base, cm, allow_small_or_imprecise_dtypes=True), [o], [])
+        else:
+            op("p", lambda q: q.iota(ap(o), pat, base, cm), [o], [])
+
+    def aselect(o, i, n, f, base, cm):
+        op("p", lambda q: q.affine_select(ap(o), ap(i), [[-1, n]], f, 0.0, base, cm), [o], [i])
+
+    def gather(o, win, off, e="v"):
+        if e == "v":
+            op("v", lambda q: q.tensor_copy(ap(o), ap(win).indirect(ap(off))), [o], [win, off])
+        else:
+            op("a", lambda q: q.activation(ap(o), ap(win).indirect(ap(off)), Act.Copy), [o], [win, off])
+
+    def pick(o, win, off):
+        op("v", lambda q: q.tensor_copy(ap(o).bitcast(dt.uint32), ap(win).bitcast(dt.uint32).indirect(ap(off))), [o], [win, off])
+        gather(S(o), S(win), off, "a")
+
+    def quant(o, i):
+        op("v", lambda q: q.quantize_mx(ap(o), ap(S(o)), ap(i)), [o, S(o)], [i])
+
+    def mm(o, a, b, start=True, stop=True):
+        op("t", lambda q: q.matmul_mx(ap(o), ap(a), ap(S(a)), ap(b), ap(S(b)), start, stop), [o], [a, S(a), b, S(b)])
+
+    def wrap(row):
+        tt(R("xm"), row, R("m16"), Op.mult)
+        scan(R("sc"), R("rs16"), R("xm"), Op.mult, Op.add)
+    WR = R("sc", 15, 128, 16)
+
+    partner = [T.cores[rank ^ (1 << b)] for b in range(L)]
+
+    def route(b):
+        rid, pid, _se = topo.addr(partner[b])
+        e = topo.engines(core, partner[b])
+        return pid, rid, sum(1 << x for x in e), len(e)
+
+    def sent(sem, n):
+        total["sent"] = total.get("sent", 0) + n
+        total[sem] = total.get(sem, 0) + n
+
+    def send(b, o, i, sem, raw=False):
+        waits("p", [], [i])
+        pid, rid, mask, n = route(b)
+        x, y = (ap(o), ap(i)) if raw else (ap(o).bitcast(dt.uint8), ap(i).bitcast(dt.uint8))
+        g.remote_dma(x, y, T.sem[sem], T.sem["sent"], pid, rid, mask)
+        sent(sem, n)
+
+    def arrive(b, sem, outs):
+        note(sem, total[sem], "far", outs, [])
+
+    def send_codes(b):
+        send(b, R("w%d" % b, B0, 512), R("w%d" % b, A0, B0), "ac%d" % b)
+
+    def send_scales(b):
+        send(b, R("w%ds" % b, B0, 512), R("w%ds" % b, A0, B0), "ac%d" % b, True)
+        arrive(b, "ac%d" % b, [R("w%d" % b, B0, 512), R("w%ds" % b, B0, 512)])
+
+    UB = R("cu", 0, 128)
+
+    def UZ(q):
+        return R("cu", 128 + 6 - 2 * q, 256 + 6 - 2 * q)
+
+    def E(t):
+        return R("ce", 128 * t, 128 * t + 128)
+
+    LO, HI, WU = R("cw", 0, 128), R("cw", 128, 256), R("cw", 256, 384)
+
+    def pb(i, n=128, a=0):
+        return R("p%d" % i, a, n)
+
+    dma("s", ap(R("u4")), T.u[:, 0:4], [R("u4")], [])
+    for q in range(4):
+        r = R("grt", 512 * q, 512 * q + 512)
+        dma("a" if q % 2 else "s", ap(r), T.gr[:, 512 * q:512 * q + 512], [r], [])
+    dma("s", ap(R("wt")), T.w[:, 0:512], [R("wt")], [])
+
+    o128 = R("ones", 0, 128)
+    fill(R("ones"), 1.0)
+    fill(R("dg"), 0.0)
+    iota(R("pi", 0, 1), [[1, 1]], 0, 1)
+    iota(R("idf"), [[1, 128]], 128, -1)
+    iota(R("ij"), [[1, 128]], 0, 0)
+    aselect(R("tri"), o128, 128, Op.is_gt, 0, 1)
+    iota(R("i128"), [[1, 128]], 0, 0, True)
+    aselect(R("ident"), o128, 128, Op.is_equal, 0, 1)
+    for b in range(4):
+        aselect(R("et", 512 * b, 512 * b + 512), R("ones"), 512, Op.is_equal, b, 4)
+    iota(R("iN"), [[1, 512]], -256, 0, True)
+    quant(R("nl"), R("dg"))
+    waits("p", [R("nl"), R("nls")], [])
+    pid, rid, mask, nready = route(0)
+    g.remote_sem_update(T.sem["ready"], T.sem["sent"], pid, rid, mask)
+    sent("ready", nready)
+    ts(R("tp", 0, 1), R("pi", 0, 1), 15, Op.bitwise_and)
+    ts(R("tp", 1, 2), R("pi", 0, 1), 112, Op.bitwise_and)
+    copy(R("pf", 0, 2), R("tp", 0, 2))
+    fill(R("cwt", 1024, 1536), 0.0)
+    act(R("cwt", 0, 512), R("ones"), Act.Copy, 0.0, R("pf", 0, 1))
+    for t in range(4):
+        act(R("cwt", 512 + t, 1024, 4), o128, Act.Copy, 128.0 * (t - 2), R("pf", 1, 2))
+    act(R("cwt", 1024, 1536, 4), o128, Act.Copy, 0.0, -1.0)
+    act(R("cwt", 1025, 1536, 4), o128, Act.Copy, 0.0, 2.0 ** -7)
+    fill(R("ut", 512, 1056), 0.0)
+    fill(R("et", 2048, 2560), 0.0)
+    copy(R("et", 2048, 2560, 4), R("ident"), "a")
+    copy(R("et", 2049, 2560, 4), R("ident"), "a")
+    fill(R("ta0"), NONE)
+    for t in range(4):
+        ts(R("ut", t, 512, 4), o128, R("u4", t, t + 1), Op.mult)
+    copy(R("ut", 4 * 134, 4 * 135), R("u4"))
+    quant(R("cu"), R("ut"))
+
+    for q in range(4):
+        a, b = 128 * q, 128 * q + 128
+        quant(R("qg", a, b), R("grt", 4 * a, 4 * b))
+        mm(pb(q), UB, R("qg", a, b))
+        mm(pb(4), R("qg", a, b), UZ(q), q == 0, q == 3)
+        act(R("ar", a, b), pb(q), Act.Abs, TINY)
+    act(R("acol"), pb(4, 8), Act.Abs, TINY)
+    ts(R("f0"), R("tri"), -ULP, Op.mult, 1.0, Op.add)
+    ts(R("tbn"), R("tri"), 0.5, Op.subtract)
+    ts(R("td"), R("idf"), 15, Op.bitwise_and)
+    ts(R("tj"), R("ij"), 15, Op.bitwise_and)
+    ts(R("m16"), R("td"), 0.0, Op.is_equal)
+    ts(R("rs16"), R("tj"), 0.0, Op.is_gt)
+    quant(R("cw"), R("cwt"))
+    for q in range(4):
+        sg, c = "sg%d" % (q % 2), "c%d" % (q % 2)
+        a, b = 128 * q, 128 * q + 128
+        aj = R("acol", 2 * q, 2 * q + 1)
+        if q == 0:
+            ts(R("t0"), R("f0"), aj, Op.mult)
+            ts(R(c, b, 512), R("ar", b, 512), aj, Op.is_gt)
+            tt(R(c, a, b), R("ar", a, b), R("t0"), Op.is_gt)
+        else:
+            act(R(sg), R("ar"), Act.Sign, aj, -1.0)
+            ts(R(c, 0, a), R(sg, 0, a), 0.0, Op.is_le)
+            if q < 3:
+                ts(R(c, b, 512), R(sg, b, 512), 0.0, Op.is_lt)
+            tt(R(c, a, b), R(sg, a, b), R("tbn"), Op.is_lt)
+        scan(R("rs", 256 * q, 256 * q + 256), R(c, 0, 256), R(c, 256, 512), Op.add, Op.add)
+        ts(R("ot0", q, 512, 4), R("i128"), R("rs", 256 * q + 255, 256 * q + 256), Op.is_equal)
+    quant(R("qo0"), R("ot0"))
+    quant(R("ce", 0, 512), R("et", 0, 2048))
+    mm(pb(5), LO, R("qo0"), True, False)
+    mm(pb(5), HI, R("qo0"), False, True)
+    wrap(pb(5))
+    ts(R("lw0"), WR, 256.0, Op.add)
+    pick(R("w0", A0, B0), R("qg"), R("lw0"))
+    send_codes(0)
+    ts(R("dg", 0, 32, 4), WR, SNAP, Op.add, SNAP, Op.subtract)
+    tt(R("dg", 1, 32, 4), WR, R("dg", 0, 32, 4), Op.subtract)
+    quant(R("nq"), R("dg"))
+    g.wait_ge(T.sem["ready"], nready)
+    send(0, R("nl", 0, 16), R("nq", 0, 16), "an0")
+    send(0, R("nls", 0, 16), R("nqs", 0, 16), "an0", True)
+    arrive(0, "an0", [R("nl", 0, 16), R("nls", 0, 16)])
+    send_scales(0)
+    copy(R("nw0", A0, B0), pb(5), "a")
+    quant(R("ce", 512, 640), R("et", 2048, 2560))
+
+    mine = ["lw0", "na1", "na2"]
+    for b in range(L):
+        w, nw, ta, nb, off, apn = ["%s%d" % (x, b) for x in ("w", "nw", "ta", "nb", "off", "ap")]
+        last = b == L - 1
+        own, far, mrg = R(w, A0, B0), R(w, B0, 512), R(w, M0, A0)
+        na = R(mine[b])
+        if b:
+            fill(R(ta), NONE)
+        op("v", lambda q: q.tensor_copy(ap(R(ta)).indirect(ap(na)), ap(R("i128"))), [R(ta)], [na, R("i128")])
+        mm(pb(4), UB, own)
+        mm(pb(5), own, UZ(0))
+        act(R("absa"), pb(4), Act.Abs, TINY)
+        act(R("aac", 0, 1), pb(5, 1), Act.Abs, TINY)
+        act(R("ada", 0, 1), R("aac", 0, 1), Act.Copy, 0.0, ULP)
+        nar, nbr = R(nw, A0, B0), R(nw, B0, 512)
+        nac, nbc, unc, umc, mkc = [R(x, 0, 1) for x in ("nac", "nbc", "unc", "umc", "mkc")]
+        unb, umb, mkb = [R("flag", i, i + 1) for i in (0, 2, 4)]
+        tt(R("xd"), nar, R("ident"), Op.mult)
+        act(R("xj"), R("xd"), Act.Copy, acc=nac)
+        fill(R(nw, 0, 128), 0.0)
+        if b == 0:
+            fill(R("ye"), 0.0)
+            ts(R("ye", 1, 512, 4), o128, 1.0, Op.mult)
+            fill(R("otr"), 0.0)
+        if b == 1:
+            quant(R("qw"), R("wt"))
+        if last:
+            fill(R("yw", 0, 128), 0.0)
+            fill(R("tk"), 0.0)
+            fill(R("nlt"), 0.0)
+        if b == 0:
+            mm(pb(6), E(4), R("nl"))
+            ts(R(nb), pb(6, 8), 256.0, Op.add)
+        gather(nbr, R("iN"), R(nb), "a")
+        aselect(R("xp"), nbr, 128, Op.is_equal, 0, 1)
+        gather(R("posr"), R(ta), R(nb))
+        wrap(R("posr"))
+        ts(R(off), WR, 127.0, Op.min)
+        pick(R(apn), own, R(off))
+        act(R("xj"), R("xp"), Act.Copy, acc=nbc)
+        ts(R("mk"), R("posr"), 200.0, Op.is_lt)
+        act(R("um"), R("mk"), Act.Identity, 1.0, -1.0)
+        first, second = (far, R(apn)) if b == 0 else (R(apn), far)
+        for t in range(4):
+            mm(pb(t), E(t), first, True, False)
+        for t in range(4):
+            mm(pb(t), E(t), second, False, True)
+        mm(pb(6), UB, far)
+        mm(pb(7), far, UZ(0))
+        ts(R("lta"), nbr, nac, Op.is_lt, -1.0, Op.mult)
+        ts(R("ye", 0, 512, 4), nar, nbc, Op.is_equal)
+        quant(R("qe"), R("ye"))
+        mm(pb(4), WU, R("qe"))
+        ts(R("ltb"), R(nw, A0, 512), nbc, Op.is_lt, -1.0, Op.mult)
+        act(R("ta"), R("lta"), Act.Identity, R("aac", 0, 1), R("ada", 0, 1))
+        act(R("yj"), R("ye", 0, 512, 4), Act.Copy, acc=mkc)
+        act(umc, mkc, Act.Identity, 1.0, -1.0)
+        copy(umb, umc, "a")
+        copy(mkb, mkc, "a")
+        copy(R(nw, M0, A0), nbr, "a")
+        act(R("sbt", 0, 1), pb(7, 1), Act.Identity, TINY, umc)
+        act(R("sbd", 0, 1), R("sbt", 0, 1), Act.Copy, 0.0, ULP)
+        if last:
+            ts(R("nlt", 2, 1024, 4), R(nw, A0, 512), nac, Op.is_gt)
+            ts(R("nlt", 3, 1024, 4), R(nw, A0, 512), nbc, Op.is_gt)
+            quant(R("qlt"), R("nlt"))
+        for t in range(4):
+            tt(R("hm", t, 512, 4), pb(t), R("mk"), Op.mult)
+        quant(mrg, R("hm"))
+        tt(R("sbs"), pb(6), R("um"), Op.mult)
+        act(R("sbm"), R("sbs"), Act.Abs)
+        tt(R("arow", 0, 128), R("absa"), pb(4), Op.mult)
+        tt(R("ca", 0, 128), R("tri"), pb(4), Op.mult)
+        mm(pb(0), UB, mrg)
+        mm(pb(1), mrg, UZ(0))
+        mm(pb(5), R("qe"), WU)
+        if last:
+            mm(pb(3, 384), R("qw"), R(w, M0, 512))
+        acb, acd = R("acb", 0, 1), R("acd", 0, 1)
+        act(R("absm"), pb(0), Act.Abs, TINY)
+        act(acb, pb(1, 1), Act.Abs, R("sbt", 0, 1))
+        act(acd, pb(1, 1), Act.Abs, R("sbd", 0, 1), ULP)
+        act(R("tb"), R("ltb"), Act.Identity, acb, acd)
+        copy(unb, pb(5, 1), "a")
+        copy(unc, pb(5, 1), "a")
+        if last:
+            copy(R("yw", M0, 512), pb(3, 384), "a")
+        tt(R("arow", 128, 256), R("absm"), R("sbm"), Op.max)
+        tt(R("ca", 128, 256), R("arow", 128, 256), R("ta"), Op.is_gt)
+        tt(R("cb"), R("arow"), R("tb"), Op.is_gt)
+        scan(R("sca"), R("ca", 0, 128), R("ca", 128, 256), Op.add, Op.add)
+        scan(R("scb"), R("cb", 0, 128), R("cb", 128, 256), Op.add, Op.add)
+        ra, rb = R("sca", 127, 128), R("scb", 127, 128)
+        oa, ou, om = unb, umb, mkb
+        if last:
+            oa, ou, om = [R(x, 0, 1) for x in ("tka", "tku", "tkm")]
+            ts(R("tk", 2, 3), ra, 128.0, Op.is_lt, unc, Op.mult)
+            ts(R("tk", 3, 4), rb, 128.0, Op.is_lt)
+            quant(R("qtk"), R("tk"))
+            mm(pb(6), R("qlt", 0, 128), R("qtk"))
+            mm(pb(7), R("qlt", 128, 256), R("qtk"))
+            ts(oa, ra, 128.0, Op.is_lt, unc, Op.mult)
+            ts(ou, rb, 128.0, Op.is_lt, umc, Op.mult)
+            ts(om, rb, 128.0, Op.is_lt, mkc, Op.mult)
+            ra, rb = pb(6, 1), pb(7, 1)
+        ts(R("otr", 2, 512, 4), R("i128"), ra, Op.is_equal, oa, Op.mult)
+        ts(R("otr", 3, 512, 4), R("i128"), rb, Op.is_equal, ou, Op.mult)
+        ts(R("otr", 1, 512, 4), R("i128"), rb, Op.is_equal, om, Op.mult)
+        quant(R("qor"), R("otr"))
+        mm(pb(2), LO, R("qor"), True, False)
+        mm(pb(2), HI, R("qor"), False, True)
+        wrap(pb(2))
+        lw = R("lw%d" % (b + 1))
+        ts(lw, WR, 256.0, Op.add)
+        if not last:
+            n1 = "nw%d" % (b + 1)
+            gather(R(n1, A0, B0), R(nw), lw, "a")
+            pick(R("w%d" % (b + 1), A0, B0), R(w), lw)
+            wrap(R(n1, A0, B0))
+            ts(R(mine[b + 1]), WR, 256.0, Op.add)
+            send_codes(b + 1)
+            send(b + 1, R("nb%d" % (b + 1)), R(mine[b + 1]), "an%d" % (b + 1), True)
+            arrive(b + 1, "an%d" % (b + 1), [R("nb%d" % (b + 1))])
+            send_scales(b + 1)
+        else:
+            pick(R("w3"), R(w), lw)
+            dma("s", T.oc[:, 0:512], ap(R("w3")).bitcast(dt.uint8), [], [R("w3")])
+            gather(R("yo"), R("yw"), lw, "a")
+            dma("a", T.y[:, 0:128], ap(R("yo")), [], [R("yo")])
+            for k in range(4):
+                dma("a" if k % 2 else "s", T.osc[4 * k:4 * k + 4, 0:128], T["w3s"][32 * k:32 * k + 4, 0:128], [], [R("w3s")])
+            op("v", lambda q: q.tensor_scalar(ap(R("nbo")), ap(R(nw)).indirect(ap(lw)), 256.0, None, Op.add), [R("nbo")], [R(nw), lw])
+            dma("s", T.nb[0:1, 0:128], T.nbo[0:1, 0:128], [], [R("nbo")])
+    for s in sorted(total):
+        g.wait_ge(T.sem[s], total[s])

@@ -6,6 +6,7 @@ TINY = 2.0 ** -100
 ULP = 2.0 ** -24
 NONE = 255.0
 SNAP = 1.5 * 2.0 ** 27
+HALF = 7.5
 
 SCRATCH = {}
 
@@ -19,26 +20,27 @@ def _codes(name, cols):
     _buf(name + "s", cols, "uint8")
 
 
-for _n, _c in (("ones", 512), ("ident", 128), ("tri", 128), ("tbn", 128), ("m16", 128), ("rs16", 128), ("i128", 128), ("iN", 512),
-               ("u4", 4), ("ut", 4 * 264), ("grt", 2048), ("wt", 512), ("cwt", 1536), ("et", 2560), ("dg", 512), ("ot0", 512), ("otr", 512),
-               ("tk", 512), ("nlt", 1024), ("sg0", 512), ("sg1", 512), ("c0", 512), ("c1", 512), ("rs", 1024), ("ye", 512), ("yj", 128),
-               ("xm", 128), ("sc", 128), ("xd", 128), ("xp", 128), ("xj", 128), ("posr", 128), ("mk", 128), ("um", 128), ("hm", 512),
-               ("ca", 256), ("cb", 256), ("lta", 128), ("ltb", 256), ("sca", 128), ("scb", 128), ("nw0", 512), ("nw1", 512), ("nw2", 512),
-               ("flag", 6), ("ta0", 512), ("ta1", 512), ("ta2", 512)):
+for _n, _c in (("ones", 512), ("ident", 128), ("tri", 128), ("m16", 128), ("rs16", 128), ("i128", 128), ("jm", 128), ("jm2", 256), ("c32", 32),
+               ("iN", 512), ("m8", 8), ("neg", 16), ("u4", 4), ("ut", 512), ("grt", 2048), ("wt", 512), ("cwt", 1536), ("et", 520), ("dg", 512),
+               ("ot0", 512), ("wx", 576), ("ex", 64), ("dv", 64), ("tk", 520), ("nlt", 1024), ("sg", 768), ("cc", 1536),
+               ("rs", 768), ("ye", 512), ("yj", 128), ("xm", 128), ("sc", 128), ("xp", 128), ("xj", 128), ("x8", 8), ("mk", 128), ("um", 128),
+               ("hm", 512), ("ca", 256), ("cb", 256), ("lta", 128), ("ltb", 256), ("rk", 256), ("nw0", 512), ("nw1", 512), ("nw2", 512),
+               ("ta0", 512), ("ta1", 512), ("ta2", 512)):
     _buf(_n, _c, "bfloat16")
-for _n, _c in (("ij", 128), ("idf", 128), ("pi", 2), ("tj", 128), ("td", 128), ("tp", 4)):
-    _buf(_n, _c, "int32")
-for _n, _c in (("pf", 4), ("f0", 128), ("t0", 128), ("ar", 512), ("small", 40), ("absa", 128), ("arow", 256), ("sbs", 128), ("sbm", 128),
-               ("absm", 128), ("ta", 128), ("tb", 256), ("nbo", 128), ("yw", 512), ("yo", 128)):
+for _n, _c in (("f0", 128), ("t0", 512), ("ar", 512), ("small", 64), ("absa", 128), ("arow", 128), ("za", 128), ("sbs", 128), ("xb", 128),
+               ("rowb", 128), ("ta", 128), ("fb", 256), ("tb", 128), ("nbo", 128), ("yw", 512), ("yo", 128)):
     _buf(_n, _c, "float32")
-for _n in ("lw0", "lw1", "lw2", "lw3", "na1", "na2", "nb0", "nb1", "nb2", "off0", "off1", "off2"):
+for _n in ("lw0", "lw1", "lw2", "lw3"):
+    _buf(_n, 16, "uint16")
+for _n in ("nb0", "nb1", "nb2", "off1", "off2"):
     _buf(_n, 8, "uint16")
-for _n, _c in (("cu", 264), ("qg", 512), ("qw", 128), ("cw", 384), ("ce", 640), ("nq", 128), ("nl", 128), ("qo0", 128), ("qor", 128),
-               ("qe", 128), ("qtk", 128), ("qlt", 256), ("w0", 512), ("w1", 512), ("w2", 512), ("w3", 128), ("ap0", 128), ("ap1", 128), ("ap2", 128)):
+for _n, _c in (("cu", 128), ("qg", 512), ("qw", 128), ("cw", 384), ("ce", 512), ("nq", 128), ("nl", 128), ("qo0", 128), ("qwx", 144),
+               ("qe", 128), ("qtk", 130), ("qlt", 256), ("w0", 512), ("w1", 512), ("w2", 512), ("w3", 128), ("ap0", 128), ("ap1", 128), ("ap2", 128)):
     _codes(_n, _c)
-SMALL = {"acol": (0, 8)}
-for _i, _n in enumerate(("aac", "ada", "sbt", "sbd", "acb", "acd", "nac", "nbc", "unc", "umc", "mkc", "tka", "tkb", "tku", "tkm")):
-    SMALL[_n] = (8 + 2 * _i, 2)
+SMALL = {}
+for _i, _n in enumerate(("p", "ph", "pl", "pb", "a0", "a1", "a2", "a3", "s0", "s1", "s2", "s3", "aac", "ada", "sbt", "thr", "nac", "nbc", "nah", "nbh",
+                         "ini", "umc", "mkc", "h0", "h1")):
+    SMALL[_n] = 2 * _i
 for _i in range(8):
     _buf("p%d" % _i, 512, "float32", "psum")
 SEMAPHORES = ["sv", "sa", "st", "sp", "sent", "ac0", "ac1", "ac2", "an0", "an1", "an2", "ready"] + ["d%d" % i for i in range(16)]
@@ -104,10 +106,10 @@ def rank_program(g, core, T, topo):
         note(s, 16, "dma", outs, ins)
 
     def R(n, a=0, b=None, st=1):
-        if n in SMALL:
-            o, width = SMALL[n]
-            return ("small", o + a, o + (width if b is None else b), st)
         return (n, a, SCRATCH[n][1][1] if b is None else b, st)
+
+    def C(n):
+        return ("small", SMALL[n], SMALL[n] + 1, 1)
 
     def ap(r):
         if r[3] == 1:
@@ -123,6 +125,9 @@ def rank_program(g, core, T, topo):
     def sap(x):
         return ap(x) if isr(x) else x
 
+    def by(win, off):
+        return ap(win) if off is None else ap(win).indirect(ap(off))
+
     def fill(r, c):
         op("v", lambda q: q.memset(ap(r), c), [r], [])
 
@@ -132,15 +137,15 @@ def rank_program(g, core, T, topo):
         else:
             op("a", lambda q: q.activation(ap(o), ap(i), Act.Copy), [o], [i])
 
-    def act(o, i, f, bias=0.0, scale=1.0, acc=None):
-        ins = [i] + [x for x in (bias, scale) if isr(x)]
+    def act(o, i, f, bias=0.0, scale=1.0, acc=None, off=None):
+        ins = [i] + [x for x in (bias, scale, off) if isr(x)]
         if acc is None:
-            op("a", lambda q: q.activation(ap(o), ap(i), f, bias=sap(bias), scale=sap(scale)), [o], ins)
+            op("a", lambda q: q.activation(ap(o), by(i, off), f, bias=sap(bias), scale=sap(scale)), [o], ins)
         else:
-            op("a", lambda q: q.activation(ap(o), ap(i), f, accum_out=ap(acc)), [o, acc], ins)
+            op("a", lambda q: q.activation(ap(o), ap(i), f, bias=sap(bias), scale=sap(scale), accum_out=ap(acc)), [o, acc], ins)
 
-    def tt(o, a, b, f):
-        op("v", lambda q: q.tensor_tensor(ap(o), ap(a), ap(b), f), [o], [a, b])
+    def tt(o, a, b, f, off=None):
+        op("v", lambda q: q.tensor_tensor(ap(o), by(a, off), ap(b), f), [o], [a, b] + ([off] if off else []))
 
     def ts(o, i, s1, f1, s2=None, f2=None):
         ins = [i] + [x for x in (s1, s2) if isr(x)]
@@ -149,14 +154,14 @@ def rank_program(g, core, T, topo):
         else:
             op("v", lambda q: q.tensor_scalar(ap(o), ap(i), sap(s1), sap(s2), f1, f2), [o], ins)
 
-    def scan(o, a, b, f0, f1):
-        op("v", lambda q: q.tensor_tensor_scan(ap(o), ap(a), ap(b), 0.0, f0, f1), [o], [a, b])
+    def scan(o, a, b, f0, f1, first=0.0):
+        op("v", lambda q: q.tensor_tensor_scan(ap(o), ap(a), ap(b), sap(first), f0, f1), [o], [a, b] + ([first] if isr(first) else []))
 
-    def iota(o, pat, base, cm, flag=False):
-        if flag:
-            op("p", lambda q: q.iota(ap(o), pat, base, cm, allow_small_or_imprecise_dtypes=True), [o], [])
-        else:
-            op("p", lambda q: q.iota(ap(o), pat, base, cm), [o], [])
+    def rsum(o, i):
+        op("v", lambda q: q.tensor_reduce(ap(o), ap(i), AxisListType.X, Op.add), [o], [i])
+
+    def iota(o, pat, base, cm):
+        op("p", lambda q: q.iota(ap(o), pat, base, cm, allow_small_or_imprecise_dtypes=True), [o], [])
 
     def aselect(o, i, n, f, base, cm):
         op("p", lambda q: q.affine_select(ap(o), ap(i), [[-1, n]], f, 0.0, base, cm), [o], [i])
@@ -167,9 +172,11 @@ def rank_program(g, core, T, topo):
         else:
             op("a", lambda q: q.activation(ap(o), ap(win).indirect(ap(off)), Act.Copy), [o], [win, off])
 
-    def pick(o, win, off):
+    def pickc(o, win, off):
         op("v", lambda q: q.tensor_copy(ap(o).bitcast(dt.uint32), ap(win).bitcast(dt.uint32).indirect(ap(off))), [o], [win, off])
-        gather(S(o), S(win), off, "a")
+
+    def picks(o, win, off, e="a"):
+        gather(S(o), S(win), off, e)
 
     def quant(o, i):
         op("v", lambda q: q.quantize_mx(ap(o), ap(S(o)), ap(i)), [o, S(o)], [i])
@@ -177,8 +184,8 @@ def rank_program(g, core, T, topo):
     def mm(o, a, b, start=True, stop=True):
         op("t", lambda q: q.matmul_mx(ap(o), ap(a), ap(S(a)), ap(b), ap(S(b)), start, stop), [o], [a, S(a), b, S(b)])
 
-    def wrap(row):
-        tt(R("xm"), row, R("m16"), Op.mult)
+    def wrap(row, off=None):
+        tt(R("xm"), row, R("m16"), Op.mult, off)
         scan(R("sc"), R("rs16"), R("xm"), Op.mult, Op.add)
     WR = R("sc", 15, 128, 16)
 
@@ -200,252 +207,303 @@ def rank_program(g, core, T, topo):
         g.remote_dma(x, y, T.sem[sem], T.sem["sent"], pid, rid, mask)
         sent(sem, n)
 
-    def arrive(b, sem, outs):
+    def arrive(sem, outs):
         note(sem, total[sem], "far", outs, [])
 
-    def send_codes(b):
+    def send_set(b):
         send(b, R("w%d" % b, B0, 512), R("w%d" % b, A0, B0), "ac%d" % b)
-
-    def send_scales(b):
         send(b, R("w%ds" % b, B0, 512), R("w%ds" % b, A0, B0), "ac%d" % b, True)
-        arrive(b, "ac%d" % b, [R("w%d" % b, B0, 512), R("w%ds" % b, B0, 512)])
+        arrive("ac%d" % b, [R("w%d" % b, B0, 512), R("w%ds" % b, B0, 512)])
 
-    UB = R("cu", 0, 128)
-
-    def UZ(q):
-        return R("cu", 128 + 6 - 2 * q, 256 + 6 - 2 * q)
+    UB = R("cu")
 
     def E(t):
         return R("ce", 128 * t, 128 * t + 128)
 
     LO, HI, WU = R("cw", 0, 128), R("cw", 128, 256), R("cw", 256, 384)
 
-    def pb(i, n=128, a=0):
-        return R("p%d" % i, a, n)
+    def pb(i, n=128, a=0, st=1):
+        return R("p%d" % i, a, n, st)
+
+    def D(t, c):
+        return R("dv", 32 * c + t, 32 * c + 32, 4)
 
     dma("s", ap(R("u4")), T.u[:, 0:4], [R("u4")], [])
     for q in range(4):
         r = R("grt", 512 * q, 512 * q + 512)
-        dma("a" if q % 2 else "s", ap(r), T.gr[:, 512 * q:512 * q + 512], [r], [])
+        dma("s" if q % 2 else "a", ap(r), T.gr[:, 512 * q:512 * q + 512], [r], [])
     dma("s", ap(R("wt")), T.w[:, 0:512], [R("wt")], [])
 
-    o128 = R("ones", 0, 128)
+    o128, o8 = R("ones", 0, 128), R("ones", 0, 8)
+    iota(C("p"), [[1, 1]], 0, 1)
+    iota(R("i128"), [[1, 128]], 0, 0)
+    iota(R("jm"), [[0, 8], [1, 16]], 0, 0)
     fill(R("ones"), 1.0)
+    ts(C("pb"), C("p"), HALF, Op.subtract)
     fill(R("dg"), 0.0)
-    iota(R("pi", 0, 1), [[1, 1]], 0, 1)
-    iota(R("idf"), [[1, 128]], 128, -1)
-    iota(R("ij"), [[1, 128]], 0, 0)
-    aselect(R("tri"), o128, 128, Op.is_gt, 0, 1)
-    iota(R("i128"), [[1, 128]], 0, 0, True)
-    aselect(R("ident"), o128, 128, Op.is_equal, 0, 1)
-    for b in range(4):
-        aselect(R("et", 512 * b, 512 * b + 512), R("ones"), 512, Op.is_equal, b, 4)
-    iota(R("iN"), [[1, 512]], -256, 0, True)
+    ts(C("ph"), C("pb"), SNAP, Op.add, SNAP, Op.subtract)
     quant(R("nl"), R("dg"))
     waits("p", [R("nl"), R("nls")], [])
     pid, rid, mask, nready = route(0)
     g.remote_sem_update(T.sem["ready"], T.sem["sent"], pid, rid, mask)
     sent("ready", nready)
-    ts(R("tp", 0, 1), R("pi", 0, 1), 15, Op.bitwise_and)
-    ts(R("tp", 1, 2), R("pi", 0, 1), 112, Op.bitwise_and)
-    copy(R("pf", 0, 2), R("tp", 0, 2))
-    fill(R("cwt", 1024, 1536), 0.0)
-    act(R("cwt", 0, 512), R("ones"), Act.Copy, 0.0, R("pf", 0, 1))
+    iota(R("c32"), [[0, 2], [16, 8], [0, 2]], 0, 0)
+    iota(R("jm2"), [[0, 8], [1, 16], [0, 2]], 0, 0)
+    tt(C("pl"), C("p"), C("ph"), Op.subtract)
     for t in range(4):
-        act(R("cwt", 512 + t, 1024, 4), o128, Act.Copy, 128.0 * (t - 2), R("pf", 1, 2))
-    act(R("cwt", 1024, 1536, 4), o128, Act.Copy, 0.0, -1.0)
-    act(R("cwt", 1025, 1536, 4), o128, Act.Copy, 0.0, 2.0 ** -7)
-    fill(R("ut", 512, 1056), 0.0)
-    fill(R("et", 2048, 2560), 0.0)
-    copy(R("et", 2048, 2560, 4), R("ident"), "a")
-    copy(R("et", 2049, 2560, 4), R("ident"), "a")
-    fill(R("ta0"), NONE)
+        act(R("cwt", 512 + t, 1024, 4), o128, Act.Copy, 128.0 * (t - 2), C("ph"))
+    act(R("cwt", 0, 512), R("ones"), Act.Copy, 0.0, C("pl"))
+    fill(R("et"), 0.0)
+    ts(R("tri"), R("i128"), C("p"), Op.is_lt)
+    ts(R("et", 3, 515, 4), R("i128"), C("p"), Op.is_equal)
+    ts(R("f0"), R("tri"), -ULP, Op.mult, 1.0, Op.add)
     for t in range(4):
+        quant(E(t), R("et", 3 - t, 515 - t))
+    quant(R("cw", 0, 256), R("cwt", 0, 1024))
+    for t in range(3):
         ts(R("ut", t, 512, 4), o128, R("u4", t, t + 1), Op.mult)
-    copy(R("ut", 4 * 134, 4 * 135), R("u4"))
+    act(R("ut", 3, 512, 4), o128, Act.Identity, R("u4", 3, 4), 0.0)
     quant(R("cu"), R("ut"))
+
+    def blk(q, n=1):
+        return R("ar", 128 * q, 128 * (q + n))
 
     for q in range(4):
         a, b = 128 * q, 128 * q + 128
         quant(R("qg", a, b), R("grt", 4 * a, 4 * b))
+        mm(pb(4 + q), R("qg", a, b), UB)
         mm(pb(q), UB, R("qg", a, b))
-        mm(pb(4), R("qg", a, b), UZ(q), q == 0, q == 3)
-        act(R("ar", a, b), pb(q), Act.Abs, TINY)
-    act(R("acol"), pb(4, 8), Act.Abs, TINY)
-    ts(R("f0"), R("tri"), -ULP, Op.mult, 1.0, Op.add)
-    ts(R("tbn"), R("tri"), 0.5, Op.subtract)
-    ts(R("td"), R("idf"), 15, Op.bitwise_and)
-    ts(R("tj"), R("ij"), 15, Op.bitwise_and)
-    ts(R("m16"), R("td"), 0.0, Op.is_equal)
-    ts(R("rs16"), R("tj"), 0.0, Op.is_gt)
-    quant(R("cw"), R("cwt"))
-    for q in range(4):
-        sg, c = "sg%d" % (q % 2), "c%d" % (q % 2)
-        a, b = 128 * q, 128 * q + 128
-        aj = R("acol", 2 * q, 2 * q + 1)
-        if q == 0:
-            ts(R("t0"), R("f0"), aj, Op.mult)
-            ts(R(c, b, 512), R("ar", b, 512), aj, Op.is_gt)
-            tt(R(c, a, b), R("ar", a, b), R("t0"), Op.is_gt)
+        act(C("a%d" % q), pb(4 + q, 1), Act.Abs, TINY)
+        act(blk(q), pb(q), Act.Abs, TINY)
+    plan = ((1, 2, 3, 1, 0), (0, 1, 2, 2, 128), (3, 1, 0, 2, 384), (1, 2, 0, 1, 640))
+
+    def limit(q, e):
+        o = R("t0", 128 * q, 128 * q + 128)
+        if e == "v":
+            ts(o, R("f0"), C("a%d" % q), Op.mult)
         else:
-            act(R(sg), R("ar"), Act.Sign, aj, -1.0)
-            ts(R(c, 0, a), R(sg, 0, a), 0.0, Op.is_le)
-            if q < 3:
-                ts(R(c, b, 512), R(sg, b, 512), 0.0, Op.is_lt)
-            tt(R(c, a, b), R(sg, a, b), R("tbn"), Op.is_lt)
-        scan(R("rs", 256 * q, 256 * q + 256), R(c, 0, 256), R(c, 256, 512), Op.add, Op.add)
-        ts(R("ot0", q, 512, 4), R("i128"), R("rs", 256 * q + 255, 256 * q + 256), Op.is_equal)
+            act(o, R("f0"), Act.Copy, 0.0, C("a%d" % q))
+
+    def signs(q):
+        _v0, _vn, s0, sn, at = plan[q]
+        act(R("sg", at, at + 128 * sn), blk(s0, sn), Act.Sign, C("a%d" % q), -1.0)
+
+    def count(q):
+        _v0, _vn, s0, sn, at = plan[q]
+        r = R("sg", at, at + 128 * sn)
+        act(r, r, Act.Sign if s0 < q else Act.Relu, 1.0 if s0 < q else 0.0, -1.0, acc=C("s%d" % q))
+
+    def diag(q):
+        tt(R("cc", 384 * q, 384 * q + 128), blk(q), R("t0", 128 * q, 128 * q + 128), Op.is_gt)
+
+    def side(q):
+        v0, vn = plan[q][:2]
+        ts(R("cc", 384 * q + 128, 384 * q + 128 * (vn + 1)), blk(v0, vn), C("a%d" % q), Op.is_ge if v0 < q else Op.is_gt)
+
+    def place(q):
+        n, a = 64 * (plan[q][1] + 1), 384 * q
+        scan(R("rs", 192 * q, 192 * q + n), R("cc", a, a + n), R("cc", a + n, a + 2 * n), Op.add, Op.add, C("s%d" % q))
+
+    def onehot(q):
+        n = 192 * q + 64 * (plan[q][1] + 1)
+        ts(R("ot0", q, 512, 4), R("i128"), R("rs", n - 1, n), Op.is_equal)
+
+    limit(0, "v"), limit(1, "v"), diag(0), side(1), diag(1), side(0)
+    limit(2, "a"), signs(0), signs(1), limit(3, "a"), count(0), count(1), signs(2), signs(3), count(2), count(3)
+    diag(2), side(2), place(0), place(1), diag(3), onehot(0), onehot(1), side(3), place(2), place(3), onehot(2), onehot(3)
     quant(R("qo0"), R("ot0"))
-    quant(R("ce", 0, 512), R("et", 0, 2048))
     mm(pb(5), LO, R("qo0"), True, False)
     mm(pb(5), HI, R("qo0"), False, True)
+    for t in range(4):
+        act(R("iN", 128 * t, 128 * t + 128), R("i128"), Act.Copy, 128.0 * (t - 2))
+    ts(R("m16"), R("jm"), C("pl"), Op.is_equal)
+    ts(R("rs16"), R("jm"), 0.0, Op.is_gt)
     wrap(pb(5))
-    ts(R("lw0"), WR, 256.0, Op.add)
-    pick(R("w0", A0, B0), R("qg"), R("lw0"))
-    send_codes(0)
+    lw = R("lw0", 0, 8)
     ts(R("dg", 0, 32, 4), WR, SNAP, Op.add, SNAP, Op.subtract)
+    ts(lw, WR, 256.0, Op.add)
     tt(R("dg", 1, 32, 4), WR, R("dg", 0, 32, 4), Op.subtract)
+    picks(R("w0", A0, B0), R("qg"), lw)
     quant(R("nq"), R("dg"))
+    pickc(R("w0", A0, B0), R("qg"), lw)
     g.wait_ge(T.sem["ready"], nready)
     send(0, R("nl", 0, 16), R("nq", 0, 16), "an0")
     send(0, R("nls", 0, 16), R("nqs", 0, 16), "an0", True)
-    arrive(0, "an0", [R("nl", 0, 16), R("nls", 0, 16)])
-    send_scales(0)
+    arrive("an0", [R("nl", 0, 16), R("nls", 0, 16)])
+    send_set(0)
     copy(R("nw0", A0, B0), pb(5), "a")
-    quant(R("ce", 512, 640), R("et", 2048, 2560))
+    ts(R("m8"), R("c32", 0, 16, 2), C("ph"), Op.is_equal)
+    mine, wrapped = lw, WR
 
-    mine = ["lw0", "na1", "na2"]
+    nac, nbc, nah, nbh, umc, mkc, thr = [C(x) for x in ("nac", "nbc", "nah", "nbh", "umc", "mkc", "thr")]
     for b in range(L):
         w, nw, ta, nb, off, apn = ["%s%d" % (x, b) for x in ("w", "nw", "ta", "nb", "off", "ap")]
         last = b == L - 1
         own, far, mrg = R(w, A0, B0), R(w, B0, 512), R(w, M0, A0)
-        na = R(mine[b])
-        if b:
-            fill(R(ta), NONE)
-        op("v", lambda q: q.tensor_copy(ap(R(ta)).indirect(ap(na)), ap(R("i128"))), [R(ta)], [na, R("i128")])
-        mm(pb(4), UB, own)
-        mm(pb(5), own, UZ(0))
-        act(R("absa"), pb(4), Act.Abs, TINY)
-        act(R("aac", 0, 1), pb(5, 1), Act.Abs, TINY)
-        act(R("ada", 0, 1), R("aac", 0, 1), Act.Copy, 0.0, ULP)
         nar, nbr = R(nw, A0, B0), R(nw, B0, 512)
-        nac, nbc, unc, umc, mkc = [R(x, 0, 1) for x in ("nac", "nbc", "unc", "umc", "mkc")]
-        unb, umb, mkb = [R("flag", i, i + 1) for i in (0, 2, 4)]
-        tt(R("xd"), nar, R("ident"), Op.mult)
-        act(R("xj"), R("xd"), Act.Copy, acc=nac)
-        fill(R(nw, 0, 128), 0.0)
+        tt(R("x8"), wrapped, R("m8"), Op.mult)
+        fill(R(ta), NONE)
+        if b:
+            gather(nar, R("iN"), mine, "a")
+        rsum(nac, R("x8"))
+        op("v", lambda q: q.tensor_copy(ap(R(ta)).indirect(ap(mine)), ap(R("i128"))), [R(ta)], [mine, R("i128")])
+        ts(nah, nac, SNAP, Op.add, SNAP, Op.subtract)
+        mm(pb(4), UB, own)
+        mm(pb(5), own, UB)
+        act(R("absa"), pb(4), Act.Abs, TINY)
+        act(C("aac"), pb(5, 1), Act.Abs, TINY)
+        act(C("ada"), C("aac"), Act.Copy, 0.0, ULP)
         if b == 0:
+            fill(R("cwt", 1024, 1536), 0.0)
             fill(R("ye"), 0.0)
+            fill(R("neg", 0, 8), -1.0)
+            fill(R("neg", 8, 16), -256.0)
+            ts(R("cwt", 1024, 1536, 4), o128, -1.0, Op.mult)
+            ts(R("cwt", 1025, 1536, 4), o128, 2.0 ** -7, Op.mult)
             ts(R("ye", 1, 512, 4), o128, 1.0, Op.mult)
-            fill(R("otr"), 0.0)
+            quant(WU, R("cwt", 1024, 1536))
+            ts(R("jm2"), R("jm2"), HALF, Op.subtract)
+            ts(C("pb"), C("ph"), 128.0, Op.add)
+            act(D(0, 0), o8, Act.Copy, 0.0, C("pl"))
+            act(D(1, 0), o8, Act.Copy, 0.0, C("pl"))
+            act(D(2, 0), o8, Act.Copy, 0.0, C("ph"))
+        act(D(2, 1), o8, Act.Copy, 0.0, nah)
+        act(D(0, 1), R("neg", 0, 8), Act.Identity, nac, nah)
         if b == 1:
             quant(R("qw"), R("wt"))
-        if last:
-            fill(R("yw", 0, 128), 0.0)
             fill(R("tk"), 0.0)
             fill(R("nlt"), 0.0)
+            ts(R("ident"), R("i128"), C("p"), Op.is_equal, -240.0, Op.mult)
+            copy(R("nlt", 0, 512, 4), R("ident"), "a")
+            copy(R("nlt", 513, 1024, 4), R("ident"), "a")
+        if last:
+            fill(R(nw, 0, 128), 0.0)
+            fill(R("yw", 0, 128), 0.0)
         if b == 0:
-            mm(pb(6), E(4), R("nl"))
+            mm(pb(6), E(0), R("nl"), True, False)
+            mm(pb(6), E(1), R("nl"), False, True)
             ts(R(nb), pb(6, 8), 256.0, Op.add)
-        gather(nbr, R("iN"), R(nb), "a")
-        aselect(R("xp"), nbr, 128, Op.is_equal, 0, 1)
-        gather(R("posr"), R(ta), R(nb))
-        wrap(R("posr"))
-        ts(R(off), WR, 127.0, Op.min)
-        pick(R(apn), own, R(off))
-        act(R("xj"), R("xp"), Act.Copy, acc=nbc)
-        ts(R("mk"), R("posr"), 200.0, Op.is_lt)
+            pickc(R(apn), R("qg"), R(nb))
+            picks(R(apn), R("qg"), R(nb))
+            act(R("mk"), R(ta), Act.Sign, NONE, -1.0, off=R(nb))
+            gather(nbr, R("iN"), R(nb))
+            tt(R("x8"), pb(6, 8), R("m8"), Op.mult)
+            rsum(nbc, R("x8"))
+        else:
+            gather(nbr, R("iN"), R(nb), "a")
+            wrap(R(ta), R(nb))
+            act(R("mk"), R(ta), Act.Sign, NONE, -1.0, off=R(nb))
+            ts(R(off), WR, 127.0, Op.min)
+            pickc(R(apn), own, R(off))
+            picks(R(apn), own, R(off))
+            aselect(R("xp"), nbr, 128, Op.is_equal, 0, 1)
+            act(R("xj"), R("xp"), Act.Copy, acc=nbc)
         act(R("um"), R("mk"), Act.Identity, 1.0, -1.0)
-        first, second = (far, R(apn)) if b == 0 else (R(apn), far)
         for t in range(4):
-            mm(pb(t), E(t), first, True, False)
-        for t in range(4):
-            mm(pb(t), E(t), second, False, True)
-        mm(pb(6), UB, far)
-        mm(pb(7), far, UZ(0))
+            mm(pb(t), E(t), R(apn), True, False)
+
+        def merge():
+            for t in range(4):
+                tt(R("hm", t, 512, 4), pb(t), R("mk"), Op.mult)
+            quant(mrg, R("hm"))
+
+        def alive():
+            tt(R("za"), R("arow"), R("fb", 0, 128), Op.mult)
+            tt(R("ca", 0, 128), R("tri"), pb(4), Op.mult)
+
+        if b == 0:
+            for t in range(4):
+                mm(pb(t), E(t), far, False, True)
         ts(R("lta"), nbr, nac, Op.is_lt, -1.0, Op.mult)
         ts(R("ye", 0, 512, 4), nar, nbc, Op.is_equal)
+        ts(R("ltb", 0, 128), nar, nbc, Op.is_gt, -ULP, Op.mult)
+        ts(R("ltb", 128, 256), nbr, nbc, Op.is_lt, -ULP, Op.mult)
         quant(R("qe"), R("ye"))
+        ts(nbh, nbc, SNAP, Op.add, SNAP, Op.subtract)
         mm(pb(4), WU, R("qe"))
-        ts(R("ltb"), R(nw, A0, 512), nbc, Op.is_lt, -1.0, Op.mult)
-        act(R("ta"), R("lta"), Act.Identity, R("aac", 0, 1), R("ada", 0, 1))
+        mm(pb(5), R("qe"), WU)
         act(R("yj"), R("ye", 0, 512, 4), Act.Copy, acc=mkc)
+        act(R("fb"), R("ltb"), Act.Identity, 1.0)
         act(umc, mkc, Act.Identity, 1.0, -1.0)
-        copy(umb, umc, "a")
-        copy(mkb, mkc, "a")
-        copy(R(nw, M0, A0), nbr, "a")
-        act(R("sbt", 0, 1), pb(7, 1), Act.Identity, TINY, umc)
-        act(R("sbd", 0, 1), R("sbt", 0, 1), Act.Copy, 0.0, ULP)
+        act(R("ta"), R("lta"), Act.Identity, C("aac"), C("ada"))
+        act(C("ini"), pb(5, 1), Act.Identity, 128.0 - HALF, -128.0)
+        if b == 0:
+            merge()
+        else:
+            tt(R("arow"), R("absa"), pb(4), Op.mult)
+            alive()
+        act(D(3, 0), R("neg", 8, 16), Act.Identity, C("pb"), mkc)
+        act(D(3, 1), o8, Act.Copy, 0.0, nbh)
+        act(D(1, 1), R("neg", 0, 8), Act.Identity, nbc, nbh)
         if last:
             ts(R("nlt", 2, 1024, 4), R(nw, A0, 512), nac, Op.is_gt)
             ts(R("nlt", 3, 1024, 4), R(nw, A0, 512), nbc, Op.is_gt)
+            copy(R(nw, M0, A0), nbr, "a")
             quant(R("qlt"), R("nlt"))
-        for t in range(4):
-            tt(R("hm", t, 512, 4), pb(t), R("mk"), Op.mult)
-        quant(mrg, R("hm"))
+        if b:
+            for t in range(4):
+                mm(pb(t), E(t), far, False, True)
+        mm(pb(6), UB, far)
+        mm(pb(7), far, UB)
+        act(C("sbt"), pb(7, 1), Act.Identity, TINY, umc)
+        if b:
+            merge()
         tt(R("sbs"), pb(6), R("um"), Op.mult)
-        act(R("sbm"), R("sbs"), Act.Abs)
-        tt(R("arow", 0, 128), R("absa"), pb(4), Op.mult)
-        tt(R("ca", 0, 128), R("tri"), pb(4), Op.mult)
+        if b == 0:
+            tt(R("arow"), R("absa"), pb(4), Op.mult)
+        mm(pb(1), mrg, UB)
         mm(pb(0), UB, mrg)
-        mm(pb(1), mrg, UZ(0))
-        mm(pb(5), R("qe"), WU)
         if last:
             mm(pb(3, 384), R("qw"), R(w, M0, 512))
-        acb, acd = R("acb", 0, 1), R("acd", 0, 1)
-        act(R("absm"), pb(0), Act.Abs, TINY)
-        act(acb, pb(1, 1), Act.Abs, R("sbt", 0, 1))
-        act(acd, pb(1, 1), Act.Abs, R("sbd", 0, 1), ULP)
-        act(R("tb"), R("ltb"), Act.Identity, acb, acd)
-        copy(unb, pb(5, 1), "a")
-        copy(unc, pb(5, 1), "a")
+        act(thr, pb(1, 1), Act.Abs, C("sbt"))
+        tt(R("xb"), pb(0), R("sbs"), Op.add)
+        if b == 0:
+            alive()
+        act(R("rowb"), R("xb"), Act.Abs, TINY)
+        act(R("tb"), R("fb", 128, 256), Act.Copy, 0.0, thr)
+        ts(R("cb", 0, 128), R("za"), thr, Op.is_ge)
+        tt(R("ca", 128, 256), R("rowb"), R("ta"), Op.is_gt)
+        tt(R("cb", 128, 256), R("rowb"), R("tb"), Op.is_gt)
         if last:
             copy(R("yw", M0, 512), pb(3, 384), "a")
-        tt(R("arow", 128, 256), R("absm"), R("sbm"), Op.max)
-        tt(R("ca", 128, 256), R("arow", 128, 256), R("ta"), Op.is_gt)
-        tt(R("cb"), R("arow"), R("tb"), Op.is_gt)
-        scan(R("sca"), R("ca", 0, 128), R("ca", 128, 256), Op.add, Op.add)
-        scan(R("scb"), R("cb", 0, 128), R("cb", 128, 256), Op.add, Op.add)
-        ra, rb = R("sca", 127, 128), R("scb", 127, 128)
-        oa, ou, om = unb, umb, mkb
+        scan(R("rk", 0, 128), R("ca", 0, 128), R("ca", 128, 256), Op.add, Op.add, C("ini"))
+        scan(R("rk", 128, 256), R("cb", 0, 128), R("cb", 128, 256), Op.add, Op.add, -HALF)
+        both, ra, rb = R("rk", 127, 256, 128), R("rk", 127, 128), R("rk", 255, 256)
         if last:
-            oa, ou, om = [R(x, 0, 1) for x in ("tka", "tku", "tkm")]
-            ts(R("tk", 2, 3), ra, 128.0, Op.is_lt, unc, Op.mult)
-            ts(R("tk", 3, 4), rb, 128.0, Op.is_lt)
+            ts(R("tk", 8, 10), both, 128.0 - 8, Op.is_lt, 31.0 / 32, Op.subtract)
+            ts(R("tk", 10, 12), both, 128.0 - 8, Op.is_lt)
             quant(R("qtk"), R("tk"))
-            mm(pb(6), R("qlt", 0, 128), R("qtk"))
-            mm(pb(7), R("qlt", 128, 256), R("qtk"))
-            ts(oa, ra, 128.0, Op.is_lt, unc, Op.mult)
-            ts(ou, rb, 128.0, Op.is_lt, umc, Op.mult)
-            ts(om, rb, 128.0, Op.is_lt, mkc, Op.mult)
-            ra, rb = pb(6, 1), pb(7, 1)
-        ts(R("otr", 2, 512, 4), R("i128"), ra, Op.is_equal, oa, Op.mult)
-        ts(R("otr", 3, 512, 4), R("i128"), rb, Op.is_equal, ou, Op.mult)
-        ts(R("otr", 1, 512, 4), R("i128"), rb, Op.is_equal, om, Op.mult)
-        quant(R("qor"), R("otr"))
-        mm(pb(2), LO, R("qor"), True, False)
-        mm(pb(2), HI, R("qor"), False, True)
-        wrap(pb(2))
-        lw = R("lw%d" % (b + 1))
-        ts(lw, WR, 256.0, Op.add)
+            mm(pb(6), R("qlt", 0, 128), R("qtk", 2, 130), True, False)
+            mm(pb(6), R("qlt", 128, 256), R("qtk", 0, 128), False, True)
+            both, ra, rb = pb(6, 3, 0, 2), pb(6, 1), pb(6, 3, 2)
+        ha, hb = (C("h0"), C("h1")) if last else (R("rk", 0, 1), R("rk", 2, 3))
+        ts(ha[:2] + (ha[1] + 3, 2), both, SNAP, Op.add, SNAP, Op.subtract)
+        ts(R("ex", 0, 64, 2), R("c32"), ha, Op.is_equal)
+        ts(R("ex", 1, 64, 2), R("c32"), hb, Op.is_equal)
+        ts(R("wx", 64, 576, 2), R("jm2"), ha, Op.add, ra, Op.is_equal)
+        tt(R("wx", 0, 64), R("ex"), R("dv"), Op.mult)
+        ts(R("wx", 65, 576, 2), R("jm2"), hb, Op.add, rb, Op.is_equal)
+        quant(R("qwx"), R("wx"))
+        mm(pb(2), R("qwx", 16, 144), R("qwx", 0, 128))
+        ln = "lw%d" % (b + 1)
+        ts(R(ln), pb(2, 16), 256.0, Op.add)
+        lw, mine, wrapped = R(ln, 0, 8), R(ln, 8, 16), pb(2, 16, 8)
         if not last:
-            n1 = "nw%d" % (b + 1)
-            gather(R(n1, A0, B0), R(nw), lw, "a")
-            pick(R("w%d" % (b + 1), A0, B0), R(w), lw)
-            wrap(R(n1, A0, B0))
-            ts(R(mine[b + 1]), WR, 256.0, Op.add)
-            send_codes(b + 1)
-            send(b + 1, R("nb%d" % (b + 1)), R(mine[b + 1]), "an%d" % (b + 1), True)
-            arrive(b + 1, "an%d" % (b + 1), [R("nb%d" % (b + 1))])
-            send_scales(b + 1)
+            nxt = R("w%d" % (b + 1), A0, B0)
+            pickc(nxt, R(w), lw)
+            picks(nxt, R(w), lw)
+            send(b + 1, R("nb%d" % (b + 1)), mine, "an%d" % (b + 1), True)
+            arrive("an%d" % (b + 1), [R("nb%d" % (b + 1))])
+            send_set(b + 1)
         else:
-            pick(R("w3"), R(w), lw)
+            pickc(R("w3"), R(w), lw)
             dma("s", T.oc[:, 0:512], ap(R("w3")).bitcast(dt.uint8), [], [R("w3")])
             gather(R("yo"), R("yw"), lw, "a")
             dma("a", T.y[:, 0:128], ap(R("yo")), [], [R("yo")])
+            picks(R("w3"), R(w), lw, "v")
+            act(R("nbo"), R(nw), Act.Identity, 256.0, off=lw)
+            dma("a", T.nb[0:1, 0:128], T.nbo[0:1, 0:128], [], [R("nbo")])
             for k in range(4):
                 dma("a" if k % 2 else "s", T.osc[4 * k:4 * k + 4, 0:128], T["w3s"][32 * k:32 * k + 4, 0:128], [], [R("w3s")])
-            op("v", lambda q: q.tensor_scalar(ap(R("nbo")), ap(R(nw)).indirect(ap(lw)), 256.0, None, Op.add), [R("nbo")], [R(nw), lw])
-            dma("s", T.nb[0:1, 0:128], T.nbo[0:1, 0:128], [], [R("nbo")])
     for s in sorted(total):
         g.wait_ge(T.sem[s], total[s])

@@ -1,3 +1,4 @@
+from concourse.bass import DstId, RemoteDMATransfer
 from concourse.mybir import dt, AluOpType as Op, AxisListType, ActivationFunctionType as Act
 
 K, P, L = 128, 512, 3
@@ -20,26 +21,26 @@ def _codes(name, cols):
     _buf(name + "s", cols, "uint8")
 
 
-for _n, _c in (("ones", 512), ("ident", 128), ("tri", 128), ("m16", 128), ("rs16", 128), ("i128", 128), ("jm", 128), ("jm2", 256), ("c32", 32),
-               ("iN", 512), ("m8", 8), ("neg", 16), ("u4", 4), ("ut", 512), ("grt", 2048), ("wt", 512), ("cwt", 1536), ("et", 520), ("dg", 512),
-               ("ot0", 512), ("wx", 576), ("ex", 64), ("dv", 64), ("tk", 520), ("nlt", 1024), ("sg", 768), ("cc", 1536),
-               ("rs", 768), ("ye", 512), ("yj", 128), ("xm", 128), ("sc", 128), ("xp", 128), ("xj", 128), ("x8", 8), ("mk", 128), ("um", 128),
-               ("hm", 512), ("ca", 256), ("cb", 256), ("lta", 128), ("ltb", 256), ("rk", 256), ("nw0", 512), ("nw1", 512), ("nw2", 512),
+for _n, _c in (("ones", 512), ("tri", 128), ("m16", 128), ("rs16", 128), ("i128", 128), ("hq", 4), ("d0", 64), ("jm2", 256), ("c32", 32),
+               ("iN", 512), ("m8", 8), ("neg", 16), ("u4", 4), ("ut", 512), ("grt", 2048), ("wt", 512), ("cwt", 512), ("et", 520), ("dg", 544),
+               ("wx", 576), ("ex", 64), ("dv", 64), ("tk", 520), ("nlt", 1024), ("sg", 768), ("cc", 1600),
+               ("rs", 800), ("ye", 512), ("yj", 128), ("xm", 128), ("sc", 128), ("xp", 128), ("xj", 128), ("x8", 8), ("mk", 128), ("um", 128),
+               ("hm", 512), ("ca", 256), ("cb", 256), ("lta", 128), ("idn", 128), ("rk", 256), ("nw0", 512), ("nw1", 512), ("nw2", 512),
                ("ta0", 512), ("ta1", 512), ("ta2", 512)):
     _buf(_n, _c, "bfloat16")
 for _n, _c in (("f0", 128), ("t0", 512), ("ar", 512), ("small", 64), ("absa", 128), ("arow", 128), ("za", 128), ("sbs", 128), ("xb", 128),
-               ("rowb", 128), ("ta", 128), ("fb", 256), ("tb", 128), ("nbo", 128), ("yw", 512), ("yo", 128)):
+               ("rowb", 128), ("ta", 128), ("fb", 256), ("tb", 128), ("nbo", 128), ("snap", 8), ("yw", 512), ("yo", 128)):
     _buf(_n, _c, "float32")
 for _n in ("lw0", "lw1", "lw2", "lw3"):
     _buf(_n, 16, "uint16")
 for _n in ("nb0", "nb1", "nb2", "off1", "off2"):
     _buf(_n, 8, "uint16")
-for _n, _c in (("cu", 128), ("qg", 512), ("qw", 128), ("cw", 384), ("ce", 512), ("nq", 128), ("nl", 128), ("qo0", 128), ("qwx", 144),
+for _n, _c in (("cu", 128), ("qg", 512), ("qw", 128), ("cw", 128), ("ce", 512), ("nq", 128), ("nl", 136), ("qwx", 144),
                ("qe", 128), ("qtk", 130), ("qlt", 256), ("w0", 512), ("w1", 512), ("w2", 512), ("w3", 128), ("ap0", 128), ("ap1", 128), ("ap2", 128)):
     _codes(_n, _c)
 SMALL = {}
-for _i, _n in enumerate(("p", "ph", "pl", "pb", "a0", "a1", "a2", "a3", "s0", "s1", "s2", "s3", "aac", "ada", "sbt", "thr", "nac", "nbc", "nah", "nbh",
-                         "ini", "umc", "mkc", "h0", "h1")):
+for _i, _n in enumerate(("p", "ph", "pl", "pb", "a0", "a1", "a2", "a3", "s0", "s1", "s2", "s3", "aac", "ada", "sbt", "thr", "nac", "nbc",
+                         "ini", "umc", "h0", "h1")):
     SMALL[_n] = 2 * _i
 for _i in range(8):
     _buf("p%d" % _i, 512, "float32", "psum")
@@ -57,7 +58,7 @@ def rank_program(g, core, T, topo):
     def meet(x, y):
         if x[1] >= y[2] or y[1] >= x[2]:
             return False
-        return not (x[3] == y[3] and x[3] > 1 and (x[1] - y[1]) % x[3])
+        return x[3] == y[3] == 1 or not set(range(*x[1:])).isdisjoint(range(*y[1:]))
 
     def waits(e, outs, ins):
         need = {}
@@ -147,12 +148,12 @@ def rank_program(g, core, T, topo):
     def tt(o, a, b, f, off=None):
         op("v", lambda q: q.tensor_tensor(ap(o), by(a, off), ap(b), f), [o], [a, b] + ([off] if off else []))
 
-    def ts(o, i, s1, f1, s2=None, f2=None):
-        ins = [i] + [x for x in (s1, s2) if isr(x)]
+    def ts(o, i, s1, f1, s2=None, f2=None, off=None):
+        ins = [i] + [x for x in (s1, s2, off) if isr(x)]
         if f2 is None:
-            op("v", lambda q: q.tensor_scalar(ap(o), ap(i), sap(s1), None, f1), [o], ins)
+            op("v", lambda q: q.tensor_scalar(ap(o), by(i, off), sap(s1), None, f1), [o], ins)
         else:
-            op("v", lambda q: q.tensor_scalar(ap(o), ap(i), sap(s1), sap(s2), f1, f2), [o], ins)
+            op("v", lambda q: q.tensor_scalar(ap(o), by(i, off), sap(s1), sap(s2), f1, f2), [o], ins)
 
     def scan(o, a, b, f0, f1, first=0.0):
         op("v", lambda q: q.tensor_tensor_scan(ap(o), ap(a), ap(b), sap(first), f0, f1), [o], [a, b] + ([first] if isr(first) else []))
@@ -162,9 +163,6 @@ def rank_program(g, core, T, topo):
 
     def iota(o, pat, base, cm):
         op("p", lambda q: q.iota(ap(o), pat, base, cm, allow_small_or_imprecise_dtypes=True), [o], [])
-
-    def aselect(o, i, n, f, base, cm):
-        op("p", lambda q: q.affine_select(ap(o), ap(i), [[-1, n]], f, 0.0, base, cm), [o], [i])
 
     def gather(o, win, off, e="v"):
         if e == "v":
@@ -183,11 +181,6 @@ def rank_program(g, core, T, topo):
 
     def mm(o, a, b, start=True, stop=True):
         op("t", lambda q: q.matmul_mx(ap(o), ap(a), ap(S(a)), ap(b), ap(S(b)), start, stop), [o], [a, S(a), b, S(b)])
-
-    def wrap(row, off=None):
-        tt(R("xm"), row, R("m16"), Op.mult, off)
-        scan(R("sc"), R("rs16"), R("xm"), Op.mult, Op.add)
-    WR = R("sc", 15, 128, 16)
 
     partner = [T.cores[rank ^ (1 << b)] for b in range(L)]
 
@@ -210,17 +203,27 @@ def rank_program(g, core, T, topo):
     def arrive(sem, outs):
         note(sem, total[sem], "far", outs, [])
 
+    def fused(b, sem, pieces):
+        waits("p", [], [i for _o, i, _raw, _n in pieces])
+        rid, pid, _se = topo.addr(partner[b])
+        e, at, xs = topo.engines(core, partner[b]), 0, []
+        for o, i, raw, n in pieces:
+            x, y = (ap(o), ap(i)) if raw else (ap(o).bitcast(dt.uint8), ap(i).bitcast(dt.uint8))
+            xs.append(RemoteDMATransfer(dst_ids=[DstId(rid=rid, pnc=pid)], dma_engine_mask=sum(1 << z for z in e[at:at + n]), remote_sem=T.sem[sem], src=y, dst=x))
+            at += n
+        g.remote_dma_fused(xs, local_sem=T.sem["sent"])
+        sent(sem, at)
+        arrive(sem, [o for o, _i, _raw, _n in pieces])
+
     def send_set(b):
         send(b, R("w%d" % b, B0, 512), R("w%d" % b, A0, B0), "ac%d" % b)
         send(b, R("w%ds" % b, B0, 512), R("w%ds" % b, A0, B0), "ac%d" % b, True)
         arrive("ac%d" % b, [R("w%d" % b, B0, 512), R("w%ds" % b, B0, 512)])
 
-    UB = R("cu")
+    UB, WU, WX = R("cu"), R("cw"), R("qwx", 16, 144)
 
     def E(t):
         return R("ce", 128 * t, 128 * t + 128)
-
-    LO, HI, WU = R("cw", 0, 128), R("cw", 128, 256), R("cw", 256, 384)
 
     def pb(i, n=128, a=0, st=1):
         return R("p%d" % i, a, n, st)
@@ -237,29 +240,30 @@ def rank_program(g, core, T, topo):
     o128, o8 = R("ones", 0, 128), R("ones", 0, 8)
     iota(C("p"), [[1, 1]], 0, 1)
     iota(R("i128"), [[1, 128]], 0, 0)
-    iota(R("jm"), [[0, 8], [1, 16]], 0, 0)
-    fill(R("ones"), 1.0)
-    ts(C("pb"), C("p"), HALF, Op.subtract)
+    iota(R("jm2"), [[0, 8], [1, 16], [0, 2]], 0, 0)
     fill(R("dg"), 0.0)
-    ts(C("ph"), C("pb"), SNAP, Op.add, SNAP, Op.subtract)
+    ts(C("pb"), C("p"), HALF, Op.subtract)
+    fill(R("ones"), 1.0)
     quant(R("nl"), R("dg"))
     waits("p", [R("nl"), R("nls")], [])
     pid, rid, mask, nready = route(0)
     g.remote_sem_update(T.sem["ready"], T.sem["sent"], pid, rid, mask)
     sent("ready", nready)
     iota(R("c32"), [[0, 2], [16, 8], [0, 2]], 0, 0)
-    iota(R("jm2"), [[0, 8], [1, 16], [0, 2]], 0, 0)
-    tt(C("pl"), C("p"), C("ph"), Op.subtract)
-    for t in range(4):
-        act(R("cwt", 512 + t, 1024, 4), o128, Act.Copy, 128.0 * (t - 2), C("ph"))
-    act(R("cwt", 0, 512), R("ones"), Act.Copy, 0.0, C("pl"))
+    iota(R("d0", 32, 64), [[0, 8], [128, 4]], -256, 0)
+    ts(C("ph"), C("pb"), SNAP, Op.add, SNAP, Op.subtract)
     fill(R("et"), 0.0)
     ts(R("tri"), R("i128"), C("p"), Op.is_lt)
+    tt(C("pl"), C("p"), C("ph"), Op.subtract)
     ts(R("et", 3, 515, 4), R("i128"), C("p"), Op.is_equal)
     ts(R("f0"), R("tri"), -ULP, Op.mult, 1.0, Op.add)
+    fill(R("cc", 7, 1600, 400), -HALF)
+    fill(R("cc", 392, 1600, 1200), 0.0)
+    fill(R("cc", 664, 1200, 400), 0.0)
     for t in range(4):
-        quant(E(t), R("et", 3 - t, 515 - t))
-    quant(R("cw", 0, 256), R("cwt", 0, 1024))
+        act(R("iN", 128 * t, 128 * t + 128), R("i128"), Act.Copy, 128.0 * (t - 2))
+    act(R("jm2"), R("jm2"), Act.Identity, -HALF)
+    act(R("d0", 0, 32), R("ones", 0, 32), Act.Copy, 0.0, C("pl"))
     for t in range(3):
         ts(R("ut", t, 512, 4), o128, R("u4", t, t + 1), Op.mult)
     act(R("ut", 3, 512, 4), o128, Act.Identity, R("u4", 3, 4), 0.0)
@@ -275,6 +279,8 @@ def rank_program(g, core, T, topo):
         mm(pb(q), UB, R("qg", a, b))
         act(C("a%d" % q), pb(4 + q, 1), Act.Abs, TINY)
         act(blk(q), pb(q), Act.Abs, TINY)
+    for t in range(4):
+        quant(E(t), R("et", 3 - t, 515 - t))
     plan = ((1, 2, 3, 1, 0), (0, 1, 2, 2, 128), (3, 1, 0, 2, 384), (1, 2, 0, 1, 640))
 
     def limit(q, e):
@@ -294,184 +300,166 @@ def rank_program(g, core, T, topo):
         act(r, r, Act.Sign if s0 < q else Act.Relu, 1.0 if s0 < q else 0.0, -1.0, acc=C("s%d" % q))
 
     def diag(q):
-        tt(R("cc", 384 * q, 384 * q + 128), blk(q), R("t0", 128 * q, 128 * q + 128), Op.is_gt)
+        tt(R("cc", 400 * q + 8, 400 * q + 136), blk(q), R("t0", 128 * q, 128 * q + 128), Op.is_gt)
 
     def side(q):
         v0, vn = plan[q][:2]
-        ts(R("cc", 384 * q + 128, 384 * q + 128 * (vn + 1)), blk(v0, vn), C("a%d" % q), Op.is_ge if v0 < q else Op.is_gt)
+        ts(R("cc", 400 * q + 136, 400 * q + 136 + 128 * vn), blk(v0, vn), C("a%d" % q), Op.is_ge if v0 < q else Op.is_gt)
 
     def place(q):
-        n, a = 64 * (plan[q][1] + 1), 384 * q
-        scan(R("rs", 192 * q, 192 * q + n), R("cc", a, a + n), R("cc", a + n, a + 2 * n), Op.add, Op.add, C("s%d" % q))
+        n, a = 64 * (plan[q][1] + 1) + 1, 400 * q + 7
+        scan(R("rs", 200 * q + 200 - n, 200 * q + 200), R("cc", a, a + n), R("cc", a + n, a + 2 * n), Op.add, Op.add, C("s%d" % q))
 
-    def onehot(q):
-        n = 192 * q + 64 * (plan[q][1] + 1)
-        ts(R("ot0", q, 512, 4), R("i128"), R("rs", n - 1, n), Op.is_equal)
+    def high(q, n):
+        ts(R("hq", q, q + n), R("rs", 200 * q + 199, 200 * (q + n), 200), SNAP, Op.add, SNAP, Op.subtract)
+
+    def col(q):
+        ts(R("ex", q, 64, 4), R("c32", 0, 32, 2), R("hq", q, q + 1), Op.is_equal)
+
+    def row(q):
+        ts(R("wx", 64 + q, 576, 4), R("jm2", 0, 256, 2), R("hq", q, q + 1), Op.add, R("rs", 200 * q + 199, 200 * q + 200), Op.is_equal)
 
     limit(0, "v"), limit(1, "v"), diag(0), side(1), diag(1), side(0)
     limit(2, "a"), signs(0), signs(1), limit(3, "a"), count(0), count(1), signs(2), signs(3), count(2), count(3)
-    diag(2), side(2), place(0), place(1), diag(3), onehot(0), onehot(1), side(3), place(2), place(3), onehot(2), onehot(3)
-    quant(R("qo0"), R("ot0"))
-    mm(pb(5), LO, R("qo0"), True, False)
-    mm(pb(5), HI, R("qo0"), False, True)
-    for t in range(4):
-        act(R("iN", 128 * t, 128 * t + 128), R("i128"), Act.Copy, 128.0 * (t - 2))
-    ts(R("m16"), R("jm"), C("pl"), Op.is_equal)
-    ts(R("rs16"), R("jm"), 0.0, Op.is_gt)
-    wrap(pb(5))
+    act(R("d0", 32, 64), R("d0", 32, 64), Act.Identity, C("ph"))
+    act(R("ta0"), R("ones"), Act.Copy, 0.0, NONE)
+    diag(2), side(2), place(0), diag(3), place(1), side(3), high(0, 2), place(2), place(3), col(0), col(1), row(0), row(1)
+    high(2, 2), ts(R("m8"), R("c32", 0, 16, 2), C("ph"), Op.is_equal), col(2), col(3), row(2), row(3)
+    tt(R("wx", 0, 64), R("ex"), R("d0"), Op.mult)
+    quant(R("qwx"), R("wx"))
+    mm(pb(5), WX, R("qwx", 0, 128))
+    mm(pb(2), WX, R("qwx", 0, 128), True, False)
+    mm(pb(2), WX, R("qwx", 8, 136), False, True)
     lw = R("lw0", 0, 8)
-    ts(R("dg", 0, 32, 4), WR, SNAP, Op.add, SNAP, Op.subtract)
-    ts(lw, WR, 256.0, Op.add)
-    tt(R("dg", 1, 32, 4), WR, R("dg", 0, 32, 4), Op.subtract)
+    copy(R("dg", 0, 64, 4), pb(5, 16))
+    ts(lw, pb(2, 8), 256.0, Op.add)
+    quant(R("nq"), R("dg", 0, 512))
     picks(R("w0", A0, B0), R("qg"), lw)
-    quant(R("nq"), R("dg"))
     pickc(R("w0", A0, B0), R("qg"), lw)
     g.wait_ge(T.sem["ready"], nready)
-    send(0, R("nl", 0, 16), R("nq", 0, 16), "an0")
-    send(0, R("nls", 0, 16), R("nqs", 0, 16), "an0", True)
-    arrive("an0", [R("nl", 0, 16), R("nls", 0, 16)])
+    fused(0, "an0", [(R("nl", 0, 16), R("nq", 0, 16), False, nready // 2), (R("nls", 0, 64), R("nqs", 0, 64), True, nready // 2)])
     send_set(0)
-    copy(R("nw0", A0, B0), pb(5), "a")
-    ts(R("m8"), R("c32", 0, 16, 2), C("ph"), Op.is_equal)
-    mine, wrapped = lw, WR
+    mine, wrapped = lw, pb(2, 8)
 
-    nac, nbc, nah, nbh, umc, mkc, thr = [C(x) for x in ("nac", "nbc", "nah", "nbh", "umc", "mkc", "thr")]
+    nac, nbc, umc, thr = [C(x) for x in ("nac", "nbc", "umc", "thr")]
     for b in range(L):
         w, nw, ta, nb, off, apn = ["%s%d" % (x, b) for x in ("w", "nw", "ta", "nb", "off", "ap")]
         last = b == L - 1
         own, far, mrg = R(w, A0, B0), R(w, B0, 512), R(w, M0, A0)
         nar, nbr = R(nw, A0, B0), R(nw, B0, 512)
         tt(R("x8"), wrapped, R("m8"), Op.mult)
-        fill(R(ta), NONE)
-        if b:
-            gather(nar, R("iN"), mine, "a")
-        rsum(nac, R("x8"))
         op("v", lambda q: q.tensor_copy(ap(R(ta)).indirect(ap(mine)), ap(R("i128"))), [R(ta)], [mine, R("i128")])
-        ts(nah, nac, SNAP, Op.add, SNAP, Op.subtract)
+        rsum(nac, R("x8"))
+        gather(nar, R("iN"), mine, "a")
         mm(pb(4), UB, own)
         mm(pb(5), own, UB)
-        act(R("absa"), pb(4), Act.Abs, TINY)
         act(C("aac"), pb(5, 1), Act.Abs, TINY)
+        act(R("absa"), pb(4), Act.Abs, TINY)
         act(C("ada"), C("aac"), Act.Copy, 0.0, ULP)
         if b == 0:
-            fill(R("cwt", 1024, 1536), 0.0)
+            fill(R("snap"), SNAP)
+            fill(R("cwt"), 0.0)
             fill(R("ye"), 0.0)
-            fill(R("neg", 0, 8), -1.0)
-            fill(R("neg", 8, 16), -256.0)
-            ts(R("cwt", 1024, 1536, 4), o128, -1.0, Op.mult)
-            ts(R("cwt", 1025, 1536, 4), o128, 2.0 ** -7, Op.mult)
+            fill(R("neg", 8, 16), 256.0)
+            ts(R("cwt", 0, 512, 4), o128, -1.0, Op.mult)
+            ts(R("cwt", 1, 512, 4), o128, 2.0 ** -7, Op.mult)
             ts(R("ye", 1, 512, 4), o128, 1.0, Op.mult)
-            quant(WU, R("cwt", 1024, 1536))
-            ts(R("jm2"), R("jm2"), HALF, Op.subtract)
-            ts(C("pb"), C("ph"), 128.0, Op.add)
+            ts(C("pb"), C("ph"), 128.0, Op.subtract)
+            quant(WU, R("cwt"))
             act(D(0, 0), o8, Act.Copy, 0.0, C("pl"))
             act(D(1, 0), o8, Act.Copy, 0.0, C("pl"))
             act(D(2, 0), o8, Act.Copy, 0.0, C("ph"))
-        act(D(2, 1), o8, Act.Copy, 0.0, nah)
-        act(D(0, 1), R("neg", 0, 8), Act.Identity, nac, nah)
+        ts(D(2, 1), R("snap"), nac, Op.add, SNAP, Op.subtract)
+        act(D(0, 1), D(2, 1), Act.Identity, nac, -1.0)
         if b == 1:
-            quant(R("qw"), R("wt"))
+            ts(R("idn"), R("i128"), C("p"), Op.is_equal)
+            ts(R("m16"), R("jm2", 0, 256, 2), HALF, Op.add, C("pl"), Op.is_equal)
+            ts(R("rs16"), R("jm2", 0, 256, 2), -7.0, Op.is_gt)
             fill(R("tk"), 0.0)
             fill(R("nlt"), 0.0)
-            ts(R("ident"), R("i128"), C("p"), Op.is_equal, -240.0, Op.mult)
-            copy(R("nlt", 0, 512, 4), R("ident"), "a")
-            copy(R("nlt", 513, 1024, 4), R("ident"), "a")
         if last:
+            quant(R("qw"), R("wt"))
             fill(R(nw, 0, 128), 0.0)
             fill(R("yw", 0, 128), 0.0)
+            act(R("nlt", 0, 512, 4), R("idn"), Act.Copy, 0.0, -240.0)
+            act(R("nlt", 513, 1024, 4), R("idn"), Act.Copy, 0.0, -240.0)
+        else:
+            act(R("ta%d" % (b + 1)), R("ones"), Act.Copy, 0.0, NONE)
         if b == 0:
-            mm(pb(6), E(0), R("nl"), True, False)
-            mm(pb(6), E(1), R("nl"), False, True)
+            mm(pb(6), E(0), R("nl", 0, 128), True, False)
+            mm(pb(6), E(0), R("nl", 8, 136), False, True)
             ts(R(nb), pb(6, 8), 256.0, Op.add)
+            tt(R("x8"), pb(6, 8), R("m8"), Op.mult)
             pickc(R(apn), R("qg"), R(nb))
             picks(R(apn), R("qg"), R(nb))
+            rsum(nbc, R("x8"))
             act(R("mk"), R(ta), Act.Sign, NONE, -1.0, off=R(nb))
             gather(nbr, R("iN"), R(nb))
-            tt(R("x8"), pb(6, 8), R("m8"), Op.mult)
-            rsum(nbc, R("x8"))
         else:
-            gather(nbr, R("iN"), R(nb), "a")
-            wrap(R(ta), R(nb))
+            tt(R("xm"), R(ta), R("m16"), Op.mult, R(nb))
+            tt(R("xp"), R("iN"), R("idn"), Op.mult, R(nb))
+            scan(R("sc"), R("rs16"), R("xm"), Op.mult, Op.add)
             act(R("mk"), R(ta), Act.Sign, NONE, -1.0, off=R(nb))
-            ts(R(off), WR, 127.0, Op.min)
+            act(R("xj"), R("xp"), Act.Copy, acc=nbc)
+            ts(R(off), R("sc", 15, 128, 16), 127.0, Op.min)
+            gather(nbr, R("iN"), R(nb), "a")
+            ts(R("ye", 0, 512, 4), nar, nbc, Op.is_equal)
             pickc(R(apn), own, R(off))
             picks(R(apn), own, R(off))
-            aselect(R("xp"), nbr, 128, Op.is_equal, 0, 1)
-            act(R("xj"), R("xp"), Act.Copy, acc=nbc)
-        act(R("um"), R("mk"), Act.Identity, 1.0, -1.0)
         for t in range(4):
-            mm(pb(t), E(t), R(apn), True, False)
-
-        def merge():
-            for t in range(4):
-                tt(R("hm", t, 512, 4), pb(t), R("mk"), Op.mult)
-            quant(mrg, R("hm"))
-
-        def alive():
-            tt(R("za"), R("arow"), R("fb", 0, 128), Op.mult)
-            tt(R("ca", 0, 128), R("tri"), pb(4), Op.mult)
-
+            mm(pb(t), E(t), far, True, False)
+        for t in range(4):
+            mm(pb(t), E(t), R(apn), False, True)
         if b == 0:
-            for t in range(4):
-                mm(pb(t), E(t), far, False, True)
-        ts(R("lta"), nbr, nac, Op.is_lt, -1.0, Op.mult)
-        ts(R("ye", 0, 512, 4), nar, nbc, Op.is_equal)
-        ts(R("ltb", 0, 128), nar, nbc, Op.is_gt, -ULP, Op.mult)
-        ts(R("ltb", 128, 256), nbr, nbc, Op.is_lt, -ULP, Op.mult)
+            ts(R("ye", 0, 512, 4), nar, nbc, Op.is_equal)
+        ts(R("fb", 0, 128), nar, nbc, Op.is_lt, 1.0 - ULP, Op.max)
         quant(R("qe"), R("ye"))
-        ts(nbh, nbc, SNAP, Op.add, SNAP, Op.subtract)
+        ts(R("lta"), nbr, nac, Op.is_lt, -1.0, Op.mult)
         mm(pb(4), WU, R("qe"))
-        mm(pb(5), R("qe"), WU)
-        act(R("yj"), R("ye", 0, 512, 4), Act.Copy, acc=mkc)
-        act(R("fb"), R("ltb"), Act.Identity, 1.0)
-        act(umc, mkc, Act.Identity, 1.0, -1.0)
-        act(R("ta"), R("lta"), Act.Identity, C("aac"), C("ada"))
-        act(C("ini"), pb(5, 1), Act.Identity, 128.0 - HALF, -128.0)
-        if b == 0:
-            merge()
-        else:
-            tt(R("arow"), R("absa"), pb(4), Op.mult)
-            alive()
-        act(D(3, 0), R("neg", 8, 16), Act.Identity, C("pb"), mkc)
-        act(D(3, 1), o8, Act.Copy, 0.0, nbh)
-        act(D(1, 1), R("neg", 0, 8), Act.Identity, nbc, nbh)
-        if last:
-            ts(R("nlt", 2, 1024, 4), R(nw, A0, 512), nac, Op.is_gt)
-            ts(R("nlt", 3, 1024, 4), R(nw, A0, 512), nbc, Op.is_gt)
-            copy(R(nw, M0, A0), nbr, "a")
-            quant(R("qlt"), R("nlt"))
-        if b:
-            for t in range(4):
-                mm(pb(t), E(t), far, False, True)
         mm(pb(6), UB, far)
         mm(pb(7), far, UB)
+        mm(pb(5), R("qe"), WU)
+        act(R("um"), R("mk"), Act.Identity, 1.0, -1.0)
+        act(R("yj"), R("ye", 0, 512, 4), Act.Identity, 2.0 ** -7, -1.0, acc=umc)
+        act(R("ta"), R("lta"), Act.Identity, C("aac"), C("ada"))
         act(C("sbt"), pb(7, 1), Act.Identity, TINY, umc)
-        if b:
-            merge()
+        act(C("ini"), pb(5, 1), Act.Identity, 128.0 - HALF, -128.0)
+        act(D(3, 0), R("neg", 8, 16), Act.Identity, C("pb"), umc)
+        for t in range(4):
+            tt(R("hm", t, 512, 4), pb(t), R("mk"), Op.mult)
+        tt(R("arow"), R("absa"), pb(4), Op.mult)
+        quant(mrg, R("hm"))
         tt(R("sbs"), pb(6), R("um"), Op.mult)
-        if b == 0:
-            tt(R("arow"), R("absa"), pb(4), Op.mult)
-        mm(pb(1), mrg, UB)
+        ts(R("fb", 128, 256), nbr, nbc, Op.is_ge, 1.0 - ULP, Op.max)
+        tt(R("za"), R("arow"), R("fb", 0, 128), Op.mult)
         mm(pb(0), UB, mrg)
+        mm(pb(1), mrg, UB)
         if last:
             mm(pb(3, 384), R("qw"), R(w, M0, 512))
-        act(thr, pb(1, 1), Act.Abs, C("sbt"))
         tt(R("xb"), pb(0), R("sbs"), Op.add)
-        if b == 0:
-            alive()
+        act(thr, pb(1, 1), Act.Abs, C("sbt"))
         act(R("rowb"), R("xb"), Act.Abs, TINY)
         act(R("tb"), R("fb", 128, 256), Act.Copy, 0.0, thr)
+        tt(R("ca", 0, 128), R("tri"), pb(4), Op.mult)
+        ts(D(3, 1), R("snap"), nbc, Op.add, SNAP, Op.subtract)
         ts(R("cb", 0, 128), R("za"), thr, Op.is_ge)
+        act(D(1, 1), D(3, 1), Act.Identity, nbc, -1.0)
         tt(R("ca", 128, 256), R("rowb"), R("ta"), Op.is_gt)
         tt(R("cb", 128, 256), R("rowb"), R("tb"), Op.is_gt)
         if last:
+            copy(R(nw, M0, A0), nbr, "a")
             copy(R("yw", M0, 512), pb(3, 384), "a")
         scan(R("rk", 0, 128), R("ca", 0, 128), R("ca", 128, 256), Op.add, Op.add, C("ini"))
+        if last:
+            ts(R("nlt", 2, 1024, 4), R(nw, A0, 512), nac, Op.is_gt)
         scan(R("rk", 128, 256), R("cb", 0, 128), R("cb", 128, 256), Op.add, Op.add, -HALF)
+        if last:
+            ts(R("nlt", 3, 1024, 4), R(nw, A0, 512), nbc, Op.is_gt)
         both, ra, rb = R("rk", 127, 256, 128), R("rk", 127, 128), R("rk", 255, 256)
         if last:
             ts(R("tk", 8, 10), both, 128.0 - 8, Op.is_lt, 31.0 / 32, Op.subtract)
             ts(R("tk", 10, 12), both, 128.0 - 8, Op.is_lt)
+            quant(R("qlt"), R("nlt"))
             quant(R("qtk"), R("tk"))
             mm(pb(6), R("qlt", 0, 128), R("qtk", 2, 130), True, False)
             mm(pb(6), R("qlt", 128, 256), R("qtk", 0, 128), False, True)
@@ -481,10 +469,10 @@ def rank_program(g, core, T, topo):
         ts(R("ex", 0, 64, 2), R("c32"), ha, Op.is_equal)
         ts(R("ex", 1, 64, 2), R("c32"), hb, Op.is_equal)
         ts(R("wx", 64, 576, 2), R("jm2"), ha, Op.add, ra, Op.is_equal)
-        tt(R("wx", 0, 64), R("ex"), R("dv"), Op.mult)
         ts(R("wx", 65, 576, 2), R("jm2"), hb, Op.add, rb, Op.is_equal)
+        tt(R("wx", 0, 64), R("ex"), R("dv"), Op.mult)
         quant(R("qwx"), R("wx"))
-        mm(pb(2), R("qwx", 16, 144), R("qwx", 0, 128))
+        mm(pb(2), WX, R("qwx", 0, 128))
         ln = "lw%d" % (b + 1)
         ts(R(ln), pb(2, 16), 256.0, Op.add)
         lw, mine, wrapped = R(ln, 0, 8), R(ln, 8, 16), pb(2, 16, 8)
@@ -497,13 +485,13 @@ def rank_program(g, core, T, topo):
             send_set(b + 1)
         else:
             pickc(R("w3"), R(w), lw)
-            dma("s", T.oc[:, 0:512], ap(R("w3")).bitcast(dt.uint8), [], [R("w3")])
             gather(R("yo"), R("yw"), lw, "a")
-            dma("a", T.y[:, 0:128], ap(R("yo")), [], [R("yo")])
-            picks(R("w3"), R(w), lw, "v")
-            act(R("nbo"), R(nw), Act.Identity, 256.0, off=lw)
-            dma("a", T.nb[0:1, 0:128], T.nbo[0:1, 0:128], [], [R("nbo")])
+            dma("s", T.oc[:, 0:512], ap(R("w3")).bitcast(dt.uint8), [], [R("w3")])
+            ts(R("nbo"), R(nw), 256.0, Op.add, off=lw)
+            picks(R("w3"), R(w), lw)
+            dma("s", T.y[:, 0:128], ap(R("yo")), [], [R("yo")])
+            dma("s", T.nb[0:1, 0:128], T.nbo[0:1, 0:128], [], [R("nbo")])
             for k in range(4):
-                dma("a" if k % 2 else "s", T.osc[4 * k:4 * k + 4, 0:128], T["w3s"][32 * k:32 * k + 4, 0:128], [], [R("w3s")])
+                dma("s" if k == 3 else "a", T.osc[4 * k:4 * k + 4, 0:128], T["w3s"][32 * k:32 * k + 4, 0:128], [], [R("w3s")])
     for s in sorted(total):
         g.wait_ge(T.sem[s], total[s])

@@ -2,13 +2,17 @@ from concourse.bass import DstId, RemoteDMATransfer
 from concourse.mybir import dt, AluOpType as Op, AxisListType, ActivationFunctionType as Act
 
 K, P, L = 128, 512, 3
-A0, B0, M0 = 256, 384, 128
+M0, A0, B0, W1 = 0, 128, 256, 384
 TINY = 2.0 ** -100
 ULP = 2.0 ** -24
 NONE = 255.0
 SNAP = 1.5 * 2.0 ** 27
 HALF = 7.5
+TOP = 3072.0
 
+CFG = dict(hop=220, f=1.0, load=(1500, 1900, 2300, 2700), num=(1100, 1100, 1100), set=(1100, 1400, 1400), issue=150, amin=120,
+           dual0=False, fuse0=False, fuse=False, own_first=(0, 1, 1))
+ORDER = {}
 SCRATCH = {}
 
 
@@ -21,26 +25,28 @@ def _codes(name, cols):
     _buf(name + "s", cols, "uint8")
 
 
-for _n, _c in (("ones", 512), ("tri", 128), ("m16", 128), ("rs16", 128), ("i128", 128), ("hq", 4), ("d0", 64), ("jm2", 256), ("c32", 32),
-               ("iN", 512), ("m8", 8), ("neg", 16), ("u4", 4), ("ut", 512), ("grt", 2048), ("wt", 512), ("cwt", 512), ("et", 520), ("dg", 544),
-               ("wx", 576), ("ex", 64), ("dv", 64), ("tk", 520), ("nlt", 1024), ("sg", 768), ("cc", 1600),
-               ("rs", 800), ("ye", 512), ("yj", 128), ("xm", 128), ("sc", 128), ("xp", 128), ("xj", 128), ("x8", 8), ("mk", 128), ("um", 128),
-               ("hm", 512), ("ca", 256), ("cb", 256), ("lta", 128), ("idn", 128), ("rk", 256), ("nw0", 512), ("nw1", 512), ("nw2", 512),
+for _n, _c in (("ones", 544), ("tri", 128), ("jq", 128), ("wz", 768), ("rh", 800), ("i128", 128), ("hq", 4), ("d0", 64), ("jm", 128), ("c32", 32),
+               ("iN", 512), ("m8", 8), ("neg", 8), ("u4", 4), ("ut", 512), ("grt", 2048), ("wt", 512), ("cwt", 520), ("et", 520),
+               ("wy", 576), ("wx", 640), ("ey", 64), ("ex", 64), ("dv", 64), ("tk", 520), ("nlt", 1024), ("sg", 768), ("cc", 1600),
+               ("rs", 800), ("r0", 128), ("ye", 512), ("yj", 128), ("r1", 128), ("xp", 128), ("xj", 128), ("x8", 16), ("mk", 128),
+               ("um", 128), ("hm", 512), ("cb", 128), ("idn", 128), ("rk", 256), ("nw0", W1), ("nw1", W1), ("nw2", W1),
                ("ta0", 512), ("ta1", 512), ("ta2", 512)):
     _buf(_n, _c, "bfloat16")
-for _n, _c in (("f0", 128), ("t0", 512), ("ar", 512), ("small", 64), ("absa", 128), ("arow", 128), ("za", 128), ("sbs", 128), ("xb", 128),
-               ("rowb", 128), ("ta", 128), ("fb", 256), ("tb", 128), ("nbo", 128), ("snap", 8), ("yw", 512), ("yo", 128)):
+for _n, _c in (("f0", 128), ("t0", 512), ("ar", 512), ("small", 64), ("absa", 128), ("za", 128), ("sbs", 128), ("xb", 128),
+               ("rowb", 128), ("fb", 128), ("tb", 128), ("nbo", 128), ("snap", 8), ("yw", W1), ("yo", 128), ("jf", 128)):
     _buf(_n, _c, "float32")
 for _n in ("lw0", "lw1", "lw2", "lw3"):
     _buf(_n, 16, "uint16")
-for _n in ("nb0", "nb1", "nb2", "off1", "off2"):
+for _n in ("nb0", "nb1", "nb2", "lc"):
     _buf(_n, 8, "uint16")
-for _n, _c in (("cu", 128), ("qg", 512), ("qw", 128), ("cw", 128), ("ce", 512), ("nq", 128), ("nl", 136), ("qwx", 144),
-               ("qe", 128), ("qtk", 130), ("qlt", 256), ("w0", 512), ("w1", 512), ("w2", 512), ("w3", 128), ("ap0", 128), ("ap1", 128), ("ap2", 128)):
+_buf("lz", 32, "uint16")
+for _n, _c in (("cu", 128), ("qg", 512), ("qw", 128), ("cw", 130), ("ce", 512), ("nx", 128), ("nl", 136), ("qwz", 192), ("wn1", 512), ("wn2", 512),
+               ("qwy", 144), ("qwx", 160), ("qe", 128), ("ql", 128), ("qtk", 130), ("qlt", 256), ("w0", W1), ("w1", W1), ("w2", W1), ("w3", 128),
+               ("ap0", 128), ("ap1", 128), ("ap2", 128)):
     _codes(_n, _c)
 SMALL = {}
-for _i, _n in enumerate(("p", "ph", "pl", "pb", "a0", "a1", "a2", "a3", "s0", "s1", "s2", "s3", "aac", "ada", "sbt", "thr", "nac", "nbc",
-                         "ini", "umc", "h0", "h1")):
+for _i, _n in enumerate(("p", "ph", "pl", "pb", "pc", "a0", "a1", "a2", "a3", "s1", "s2", "s3", "sbt", "thr", "nac", "nbc",
+                         "umc", "ha", "hb", "la", "nah", "nbh")):
     SMALL[_n] = 2 * _i
 for _i in range(8):
     _buf("p%d" % _i, 512, "float32", "psum")
@@ -86,31 +92,82 @@ def rank_program(g, core, T, topo):
             for r in regs:
                 recs.setdefault(r[0], []).append((r, w, s, c, e))
 
-    def op(e, call, outs, ins):
-        waits(e, outs, ins)
-        s = ESEM[e]
-        total[s] = total.get(s, 0) + 1
-        call(Q[e]).then_inc(T.sem[s], 1)
-        hist[(s, total[s])] = dict(known[e])
-        hist[(s, total[s])][s] = total[s]
-        note(s, total[s], e, outs, ins)
+    nodes = []
 
-    nd = [0]
+    def node(e, run, outs, ins, cost, lat=None, after=()):
+        nodes.append((e, run, outs, ins, cost, CFG["hop"] if lat is None else lat, after))
+        return len(nodes) - 1
 
-    def dma(e, out, in_, outs, ins):
-        waits(e, outs, ins)
-        s = "d%d" % nd[0]
-        nd[0] += 1
-        total[s] = 16
-        Q[e].dma_start(out, in_).then_inc(T.sem[s], 16)
-        hist[(s, 16)] = dict(known[e])
-        note(s, 16, "dma", outs, ins)
+    def op(e, call, outs, ins, cost):
+        def run():
+            waits(e, outs, ins)
+            s = ESEM[e]
+            total[s] = total.get(s, 0) + 1
+            call(Q[e]).then_inc(T.sem[s], 1)
+            hist[(s, total[s])] = dict(known[e])
+            hist[(s, total[s])][s] = total[s]
+            note(s, total[s], e, outs, ins)
+        node(e, run, outs, ins, max(cost, CFG["amin"] if e == "a" else 0) * CFG["f"])
+
+    nd, dmas = [0], set()
+
+    def dma(e, out, in_, outs, ins, lat=1500):
+        def run():
+            waits(e, outs, ins)
+            s = "d%d" % nd[0]
+            nd[0] += 1
+            total[s] = 16
+            Q[e].dma_start(out, in_).then_inc(T.sem[s], 16)
+            hist[(s, 16)] = dict(known[e])
+            note(s, 16, "dma", outs, ins)
+        dmas.add(node(e, run, outs, ins, 60, lat))
+
+    def order():
+        seen, preds, tail = {}, [], {}
+        for k, (e, _run, outs, ins, _cost, _lat, after) in enumerate(nodes):
+            need = {j: nodes[j][5] for j in after}
+            for regs, isw in ((ins, False), (outs, True)):
+                for r in regs:
+                    ps = SCRATCH[r[0]][0] == "psum"
+                    for q, w, j in seen.get(r[0], []):
+                        if ps and nodes[j][0] == e == "t":
+                            need.setdefault(j, 0)
+                        elif (ps and nodes[j][0] != e) or ((w or isw) and (ps or meet(r, q))):
+                            need[j] = nodes[j][5]
+            if e in "ps" or k in dmas:
+                if e in tail:
+                    need.setdefault(tail[e], 0)
+                tail[e] = k
+            for regs, w in ((ins, False), (outs, True)):
+                for r in regs:
+                    seen.setdefault(r[0], []).append((r, w, k))
+            preds.append(need)
+        way = [n[4] + (n[5] if not n[2] else 0) for n in nodes]
+        for k in reversed(range(len(nodes))):
+            for j, lat in preds[k].items():
+                way[j] = max(way[j], nodes[j][4] + lat + way[k])
+        start, busy = {}, {}
+        for k in sorted(range(len(nodes)), key=lambda k: (-way[k], k)):
+            e, cost = nodes[k][0], nodes[k][4]
+            t = max([start[j] + nodes[j][4] + lat for j, lat in preds[k].items()] + [0])
+            if e != "x":
+                for a, b in busy.setdefault(e, []):
+                    if t + cost <= a:
+                        break
+                    t = max(t, b)
+                busy[e].append((t, t + cost))
+                busy[e].sort()
+            start[k] = t
+        return sorted(range(len(nodes)), key=lambda k: (start[k], k))
 
     def R(n, a=0, b=None, st=1):
         return (n, a, SCRATCH[n][1][1] if b is None else b, st)
 
     def C(n):
         return ("small", SMALL[n], SMALL[n] + 1, 1)
+
+    def one(r):
+        return (r[0], r[1], r[1] + 1, 1)
 
     def ap(r):
         if r[3] == 1:
@@ -129,58 +186,76 @@ def rank_program(g, core, T, topo):
     def by(win, off):
         return ap(win) if off is None else ap(win).indirect(ap(off))
 
-    def fill(r, c):
-        op("v", lambda q: q.memset(ap(r), c), [r], [])
+    def span(r, two=False, *more):
+        n = len(range(*r[1:]))
+        if two is None:
+            return max(53, 0.83 * n)
+        if two:
+            return max(53, 0.83 * n * (1 if any(SCRATCH[x[0]][0] == "psum" for x in more) else 2))
+        return max(53, 0.83 * n * (0.5 if all(SCRATCH[x[0]][2] in ("bfloat16", "uint16") for x in (r,) + more) else 1))
+
+    def listed(r):
+        return 60 + 1.25 * len(range(*r[1:]))
+
+    def fill(r, c, e="v"):
+        if e == "v":
+            op("v", lambda q: q.memset(ap(r), c), [r], [], span(r))
+        else:
+            act(r, R("ones", 0, len(range(*r[1:]))), Act.Copy, 0.0, c)
 
     def copy(o, i, e="v"):
         if e == "v":
-            op("v", lambda q: q.tensor_copy(ap(o), ap(i)), [o], [i])
+            op("v", lambda q: q.tensor_copy(ap(o), ap(i)), [o], [i], span(o, False, i))
         else:
-            op("a", lambda q: q.activation(ap(o), ap(i), Act.Copy), [o], [i])
+            op("a", lambda q: q.activation(ap(o), ap(i), Act.Copy), [o], [i], span(o, None))
 
     def act(o, i, f, bias=0.0, scale=1.0, acc=None, off=None):
         ins = [i] + [x for x in (bias, scale, off) if isr(x)]
         if acc is None:
-            op("a", lambda q: q.activation(ap(o), by(i, off), f, bias=sap(bias), scale=sap(scale)), [o], ins)
+            op("a", lambda q: q.activation(ap(o), by(i, off), f, bias=sap(bias), scale=sap(scale)), [o], ins, listed(o) if off else span(o, None))
         else:
-            op("a", lambda q: q.activation(ap(o), ap(i), f, bias=sap(bias), scale=sap(scale), accum_out=ap(acc)), [o, acc], ins)
+            op("a", lambda q: q.activation(ap(o), ap(i), f, bias=sap(bias), scale=sap(scale), accum_out=ap(acc)), [o, acc], ins, span(o, None) + 20)
 
     def tt(o, a, b, f, off=None):
-        op("v", lambda q: q.tensor_tensor(ap(o), by(a, off), ap(b), f), [o], [a, b] + ([off] if off else []))
+        op("v", lambda q: q.tensor_tensor(ap(o), by(a, off), ap(b), f), [o], [a, b] + ([off] if off else []), listed(o) if off else span(o, True, a, b))
 
     def ts(o, i, s1, f1, s2=None, f2=None, off=None):
         ins = [i] + [x for x in (s1, s2, off) if isr(x)]
         if f2 is None:
-            op("v", lambda q: q.tensor_scalar(ap(o), by(i, off), sap(s1), None, f1), [o], ins)
+            op("v", lambda q: q.tensor_scalar(ap(o), by(i, off), sap(s1), None, f1), [o], ins, listed(o) if off else span(o, False, i))
         else:
-            op("v", lambda q: q.tensor_scalar(ap(o), by(i, off), sap(s1), sap(s2), f1, f2), [o], ins)
+            op("v", lambda q: q.tensor_scalar(ap(o), by(i, off), sap(s1), sap(s2), f1, f2), [o], ins, listed(o) if off else span(o, False, i))
 
     def scan(o, a, b, f0, f1, first=0.0):
-        op("v", lambda q: q.tensor_tensor_scan(ap(o), ap(a), ap(b), sap(first), f0, f1), [o], [a, b] + ([first] if isr(first) else []))
+        op("v", lambda q: q.tensor_tensor_scan(ap(o), ap(a), ap(b), sap(first), f0, f1), [o], [a, b] + ([first] if isr(first) else []), span(o, False, a, b))
 
     def rsum(o, i):
-        op("v", lambda q: q.tensor_reduce(ap(o), ap(i), AxisListType.X, Op.add), [o], [i])
+        op("v", lambda q: q.tensor_reduce(ap(o), ap(i), AxisListType.X, Op.add), [o], [i], span(i, None))
 
     def iota(o, pat, base, cm):
-        op("p", lambda q: q.iota(ap(o), pat, base, cm, allow_small_or_imprecise_dtypes=True), [o], [])
+        op("p", lambda q: q.iota(ap(o), pat, base, cm, allow_small_or_imprecise_dtypes=True), [o], [], 130 + 1.66 * len(range(*o[1:])))
 
     def gather(o, win, off, e="v"):
         if e == "v":
-            op("v", lambda q: q.tensor_copy(ap(o), ap(win).indirect(ap(off))), [o], [win, off])
+            op("v", lambda q: q.tensor_copy(ap(o), ap(win).indirect(ap(off))), [o], [win, off], listed(o))
         else:
-            op("a", lambda q: q.activation(ap(o), ap(win).indirect(ap(off)), Act.Copy), [o], [win, off])
+            op("a", lambda q: q.activation(ap(o), ap(win).indirect(ap(off)), Act.Copy), [o], [win, off], listed(o))
 
-    def pickc(o, win, off):
-        op("v", lambda q: q.tensor_copy(ap(o).bitcast(dt.uint32), ap(win).bitcast(dt.uint32).indirect(ap(off))), [o], [win, off])
+    def scatter(win, off, i):
+        op("v", lambda q: q.tensor_copy(ap(win).indirect(ap(off)), ap(i)), [win], [off, i], 2 * listed(i))
 
-    def picks(o, win, off, e="a"):
-        gather(S(o), S(win), off, e)
+    def pick(o, win, off):
+        op("v", lambda q: q.tensor_copy(ap(o).bitcast(dt.uint32), ap(win).bitcast(dt.uint32).indirect(ap(off))), [o], [win, off], listed(o))
+        gather(S(o), S(win), off, "a")
 
     def quant(o, i):
-        op("v", lambda q: q.quantize_mx(ap(o), ap(S(o)), ap(i)), [o, S(o)], [i])
+        op("v", lambda q: q.quantize_mx(ap(o), ap(S(o)), ap(i)), [o, S(o)], [i], 12 + 0.22 * (i[2] - i[1]))
 
     def mm(o, a, b, start=True, stop=True):
-        op("t", lambda q: q.matmul_mx(ap(o), ap(a), ap(S(a)), ap(b), ap(S(b)), start, stop), [o], [a, S(a), b, S(b)])
+        op("t", lambda q: q.matmul_mx(ap(o), ap(a), ap(S(a)), ap(b), ap(S(b)), start, stop), [o], [a, S(a), b, S(b)], 0.6 * (16 + o[2] - o[1]))
+
+    def snap(o, i):
+        ts(o, i, SNAP, Op.add, SNAP, Op.subtract)
 
     partner = [T.cores[rank ^ (1 << b)] for b in range(L)]
 
@@ -193,34 +268,25 @@ def rank_program(g, core, T, topo):
         total["sent"] = total.get("sent", 0) + n
         total[sem] = total.get(sem, 0) + n
 
-    def send(b, o, i, sem, raw=False):
-        waits("p", [], [i])
-        pid, rid, mask, n = route(b)
-        x, y = (ap(o), ap(i)) if raw else (ap(o).bitcast(dt.uint8), ap(i).bitcast(dt.uint8))
-        g.remote_dma(x, y, T.sem[sem], T.sem["sent"], pid, rid, mask)
-        sent(sem, n)
-
-    def arrive(sem, outs):
-        note(sem, total[sem], "far", outs, [])
-
-    def fused(b, sem, pieces):
-        waits("p", [], [i for _o, i, _raw, _n in pieces])
-        rid, pid, _se = topo.addr(partner[b])
-        e, at, xs = topo.engines(core, partner[b]), 0, []
-        for o, i, raw, n in pieces:
+    def send(b, o, i, sem, lat, raw=False):
+        def run():
+            waits("p", [], [i])
+            pid, rid, mask, n = route(b)
             x, y = (ap(o), ap(i)) if raw else (ap(o).bitcast(dt.uint8), ap(i).bitcast(dt.uint8))
-            xs.append(RemoteDMATransfer(dst_ids=[DstId(rid=rid, pnc=pid)], dma_engine_mask=sum(1 << z for z in e[at:at + n]), remote_sem=T.sem[sem], src=y, dst=x))
-            at += n
-        g.remote_dma_fused(xs, local_sem=T.sem["sent"])
-        sent(sem, at)
-        arrive(sem, [o for o, _i, _raw, _n in pieces])
+            g.remote_dma(x, y, T.sem[sem], T.sem["sent"], pid, rid, mask)
+            sent(sem, n)
+        return node("p", run, [], [i], CFG["issue"], lat)
+
+    def arrive(sem, outs, after):
+        node("x", lambda: note(sem, total[sem], "far", outs, []), outs, [], 1, 0, after)
+
+    def send_codes(b, o, i, sem, lat):
+        arrive(sem, [o, S(o)], [send(b, o, i, sem, lat), send(b, S(o), S(i), sem, lat, True)])
 
     def send_set(b):
-        send(b, R("w%d" % b, B0, 512), R("w%d" % b, A0, B0), "ac%d" % b)
-        send(b, R("w%ds" % b, B0, 512), R("w%ds" % b, A0, B0), "ac%d" % b, True)
-        arrive("ac%d" % b, [R("w%d" % b, B0, 512), R("w%ds" % b, B0, 512)])
+        send_codes(b, R("w%d" % b, B0, W1), R("w%d" % b, A0, B0), "ac%d" % b, CFG["set"][b])
 
-    UB, WU, WX = R("cu"), R("cw"), R("qwx", 16, 144)
+    UB, WU, WR, WY, WX = R("cu"), R("cw", 0, 128), R("cw", 2, 130), R("qwy", 16, 144), R("qwx", 32, 160)
 
     def E(t):
         return R("ce", 128 * t, 128 * t + 128)
@@ -228,270 +294,324 @@ def rank_program(g, core, T, topo):
     def pb(i, n=128, a=0, st=1):
         return R("p%d" % i, a, n, st)
 
-    def D(t, c):
-        return R("dv", 32 * c + t, 32 * c + 32, 4)
+    def D(side, k):
+        return R("dv", 32 * side + 8 * k, 32 * side + 8 * k + 8)
 
-    dma("s", ap(R("u4")), T.u[:, 0:4], [R("u4")], [])
+    def Y(t):
+        return R("ye", t, 512, 4)
+
+    dma("a", ap(R("u4")), T.u[:, 0:4], [R("u4")], [], CFG["load"][0] - 300)
     for q in range(4):
         r = R("grt", 512 * q, 512 * q + 512)
-        dma("s" if q % 2 else "a", ap(r), T.gr[:, 512 * q:512 * q + 512], [r], [])
-    dma("s", ap(R("wt")), T.w[:, 0:512], [R("wt")], [])
+        dma("a" if q % 2 else "s", ap(r), T.gr[:, 512 * q:512 * q + 512], [r], [], CFG["load"][q])
 
     o128, o8 = R("ones", 0, 128), R("ones", 0, 8)
     iota(C("p"), [[1, 1]], 0, 1)
     iota(R("i128"), [[1, 128]], 0, 0)
-    iota(R("jm2"), [[0, 8], [1, 16], [0, 2]], 0, 0)
-    fill(R("dg"), 0.0)
-    ts(C("pb"), C("p"), HALF, Op.subtract)
+    iota(R("jm"), [[0, 8], [1, 16]], 0, 0)
+    iota(R("c32"), [[0, 4], [16, 8]], 0, 0)
     fill(R("ones"), 1.0)
-    quant(R("nl"), R("dg"))
-    waits("p", [R("nl"), R("nls")], [])
+    quant(R("nl"), R("ones"))
     pid, rid, mask, nready = route(0)
-    g.remote_sem_update(T.sem["ready"], T.sem["sent"], pid, rid, mask)
-    sent("ready", nready)
-    iota(R("c32"), [[0, 2], [16, 8], [0, 2]], 0, 0)
-    iota(R("d0", 32, 64), [[0, 8], [128, 4]], -256, 0)
-    ts(C("ph"), C("pb"), SNAP, Op.add, SNAP, Op.subtract)
+
+    def ready():
+        waits("p", [R("nl"), R("nls")], [])
+        g.remote_sem_update(T.sem["ready"], T.sem["sent"], pid, rid, mask)
+        sent("ready", nready)
+
+    node("p", ready, [R("nl"), R("nls")], [], 3000, 0)
     fill(R("et"), 0.0)
+    ts(C("pb"), C("p"), HALF, Op.subtract)
     ts(R("tri"), R("i128"), C("p"), Op.is_lt)
-    tt(C("pl"), C("p"), C("ph"), Op.subtract)
     ts(R("et", 3, 515, 4), R("i128"), C("p"), Op.is_equal)
+    snap(C("ph"), C("pb"))
     ts(R("f0"), R("tri"), -ULP, Op.mult, 1.0, Op.add)
-    fill(R("cc", 7, 1600, 400), -HALF)
-    fill(R("cc", 392, 1600, 1200), 0.0)
-    fill(R("cc", 664, 1200, 400), 0.0)
+    tt(C("pl"), C("p"), C("ph"), Op.subtract)
+    fill(R("cc", 407, 1600, 400), -HALF)
+    fill(R("cc", 406, 1600, 400), TOP)
+    fill(R("cc", 792, 794), 0.0)
+    fill(R("cc", 1064, 1066), 0.0)
+    fill(R("cc", 1464, 1466), 0.0)
+    fill(R("ta0"), NONE, "a")
     for t in range(4):
         act(R("iN", 128 * t, 128 * t + 128), R("i128"), Act.Copy, 128.0 * (t - 2))
-    act(R("jm2"), R("jm2"), Act.Identity, -HALF)
+    copy(R("jq"), R("jm"), "a")
+    act(R("jf"), R("jm"), Act.Identity, -HALF - TOP)
+    act(R("jm"), R("jm"), Act.Identity, -HALF)
+    ts(R("lc"), o8, C("pl"), Op.mult, 16.0, Op.add)
     act(R("d0", 0, 32), R("ones", 0, 32), Act.Copy, 0.0, C("pl"))
+    for t in range(4):
+        act(R("d0", 32 + t, 64, 4), o8, Act.Identity, C("ph"), 128.0 * (t - 2))
+    for t in range(4):
+        quant(E(t), R("et", 3 - t, 515 - t))
     for t in range(3):
         ts(R("ut", t, 512, 4), o128, R("u4", t, t + 1), Op.mult)
     act(R("ut", 3, 512, 4), o128, Act.Identity, R("u4", 3, 4), 0.0)
     quant(R("cu"), R("ut"))
+    fill(R("cwt"), 0.0, "a")
 
     def blk(q, n=1):
         return R("ar", 128 * q, 128 * (q + n))
 
-    for q in range(4):
+    def pack(q):
         a, b = 128 * q, 128 * q + 128
         quant(R("qg", a, b), R("grt", 4 * a, 4 * b))
         mm(pb(4 + q), R("qg", a, b), UB)
         mm(pb(q), UB, R("qg", a, b))
+
+    def sizes(q):
         act(C("a%d" % q), pb(4 + q, 1), Act.Abs, TINY)
         act(blk(q), pb(q), Act.Abs, TINY)
-    for t in range(4):
-        quant(E(t), R("et", 3 - t, 515 - t))
-    plan = ((1, 2, 3, 1, 0), (0, 1, 2, 2, 128), (3, 1, 0, 2, 384), (1, 2, 0, 1, 640))
 
-    def limit(q, e):
-        o = R("t0", 128 * q, 128 * q + 128)
-        if e == "v":
-            ts(o, R("f0"), C("a%d" % q), Op.mult)
-        else:
-            act(o, R("f0"), Act.Copy, 0.0, C("a%d" % q))
+    def limit(q):
+        act(R("t0", 128 * q, 128 * q + 128), R("f0"), Act.Copy, 0.0, C("a%d" % q))
+
+    def sg(q):
+        return R("sg", 256 * (q - 1), 256 * (q - 1) + 128 * min(q, 2))
 
     def signs(q):
-        _v0, _vn, s0, sn, at = plan[q]
-        act(R("sg", at, at + 128 * sn), blk(s0, sn), Act.Sign, C("a%d" % q), -1.0)
+        act(sg(q), blk(0, min(q, 2)), Act.Sign, C("a%d" % q), -1.0)
 
     def count(q):
-        _v0, _vn, s0, sn, at = plan[q]
-        r = R("sg", at, at + 128 * sn)
-        act(r, r, Act.Sign if s0 < q else Act.Relu, 1.0 if s0 < q else 0.0, -1.0, acc=C("s%d" % q))
+        act(sg(q), sg(q), Act.Sign, 1.0, -1.0, acc=C("s%d" % q))
+
+    def cc(q, j):
+        a = 128 * j if q == 0 else 400 * q + 8 + 128 * abs(j - q)
+        return R("cc", a, a + 128) if (q, j) != (0, 3) else R("r0")
 
     def diag(q):
-        tt(R("cc", 400 * q + 8, 400 * q + 136), blk(q), R("t0", 128 * q, 128 * q + 128), Op.is_gt)
+        tt(cc(q, q), blk(q), R("t0", 128 * q, 128 * q + 128), Op.is_gt)
 
-    def side(q):
-        v0, vn = plan[q][:2]
-        ts(R("cc", 400 * q + 136, 400 * q + 136 + 128 * vn), blk(v0, vn), C("a%d" % q), Op.is_ge if v0 < q else Op.is_gt)
+    def side(q, j):
+        ts(cc(q, j), blk(j), C("a%d" % q), Op.is_gt if j > q else Op.is_ge)
 
     def place(q):
-        n, a = 64 * (plan[q][1] + 1) + 1, 400 * q + 7
+        n, a = 64 * max(4 - q, 2) + 1, 400 * q + 7
         scan(R("rs", 200 * q + 200 - n, 200 * q + 200), R("cc", a, a + n), R("cc", a + n, a + 2 * n), Op.add, Op.add, C("s%d" % q))
 
-    def high(q, n):
-        ts(R("hq", q, q + n), R("rs", 200 * q + 199, 200 * (q + n), 200), SNAP, Op.add, SNAP, Op.subtract)
+    def high(q):
+        n, a = 64 * max(4 - q, 2) + 2, 400 * q + 6
+        scan(R("rh", 200 * q + 200 - n, 200 * q + 200), R("cc", a, a + n), R("cc", a + n, a + 2 * n), Op.add, Op.add, C("s%d" % q))
 
-    def col(q):
-        ts(R("ex", q, 64, 4), R("c32", 0, 32, 2), R("hq", q, q + 1), Op.is_equal)
+    def onehot(q):
+        r = R("rs", 200 * q + 199, 200 * q + 200)
+        if CFG["dual0"] and q:
+            high(q)
+            h = R("rh", 200 * q + 199, 200 * q + 200)
+            ts(R("ey", q, 64, 4), R("c32", 0, 16), TOP, Op.add, h, Op.is_equal)
+            ts(R("wy", 64 + q, 576, 4), R("jf"), h, Op.add, r, Op.is_equal)
+        else:
+            h = R("hq", q, q + 1)
+            snap(h, r)
+            if CFG["fuse0"]:
+                for k in range(2):
+                    ts(R("wy", 32 * k + q, 32 * k + 32, 4), R("c32", 0, 8), h, Op.is_equal, R("d0", 32 * k + q, 32 * k + q + 1), Op.mult)
+            else:
+                ts(R("ey", q, 64, 4), R("c32", 0, 16), h, Op.is_equal)
+            ts(R("wy", 64 + q, 576, 4), R("jm"), h, Op.add, r, Op.is_equal)
 
-    def row(q):
-        ts(R("wx", 64 + q, 576, 4), R("jm2", 0, 256, 2), R("hq", q, q + 1), Op.add, R("rs", 200 * q + 199, 200 * q + 200), Op.is_equal)
-
-    limit(0, "v"), limit(1, "v"), diag(0), side(1), diag(1), side(0)
-    limit(2, "a"), signs(0), signs(1), limit(3, "a"), count(0), count(1), signs(2), signs(3), count(2), count(3)
-    act(R("d0", 32, 64), R("d0", 32, 64), Act.Identity, C("ph"))
-    act(R("ta0"), R("ones"), Act.Copy, 0.0, NONE)
-    diag(2), side(2), place(0), diag(3), place(1), side(3), high(0, 2), place(2), place(3), col(0), col(1), row(0), row(1)
-    high(2, 2), ts(R("m8"), R("c32", 0, 16, 2), C("ph"), Op.is_equal), col(2), col(3), row(2), row(3)
-    tt(R("wx", 0, 64), R("ex"), R("d0"), Op.mult)
-    quant(R("qwx"), R("wx"))
-    mm(pb(5), WX, R("qwx", 0, 128))
-    mm(pb(2), WX, R("qwx", 0, 128), True, False)
-    mm(pb(2), WX, R("qwx", 8, 136), False, True)
+    for q in range(4):
+        pack(q), sizes(q), limit(q), diag(q)
+    for q in range(1, 4):
+        signs(q), count(q)
+    for q, j in ((0, 1), (0, 2), (1, 2), (3, 2), (0, 3), (1, 3), (2, 3)):
+        side(q, j)
+    dma("s", ap(R("wt")), T.w[:, 0:512], [R("wt")], [R("grt", 1536, 2048)])
+    scan(R("r1"), cc(0, 0), cc(0, 1), Op.add, Op.add, -HALF)
+    scan(R("rs", 72, 200), cc(0, 2), cc(0, 3), Op.add, Op.add, R("r1", 127, 128))
+    for q in range(4):
+        if q:
+            place(q)
+        onehot(q)
+    ts(R("m8"), R("c32", 0, 8), C("ph"), Op.is_equal)
+    if not CFG["fuse0"]:
+        tt(R("wy", 0, 64), R("ey"), R("d0"), Op.mult)
+    quant(R("qwy"), R("wy"))
+    node("p", lambda: g.wait_ge(T.sem["ready"], nready), [], [], 1, 0)
+    send_codes(0, R("nl", 0, 32), R("qwy", 0, 32), "an0", CFG["num"][0])
+    mm(pb(2), WY, R("qwy", 0, 128), True, False)
+    mm(pb(2), WY, R("qwy", 8, 136), False, True)
     lw = R("lw0", 0, 8)
-    copy(R("dg", 0, 64, 4), pb(5, 16))
     ts(lw, pb(2, 8), 256.0, Op.add)
-    quant(R("nq"), R("dg", 0, 512))
-    picks(R("w0", A0, B0), R("qg"), lw)
-    pickc(R("w0", A0, B0), R("qg"), lw)
-    g.wait_ge(T.sem["ready"], nready)
-    fused(0, "an0", [(R("nl", 0, 16), R("nq", 0, 16), False, nready // 2), (R("nls", 0, 64), R("nqs", 0, 64), True, nready // 2)])
+    pick(R("w0", A0, B0), R("qg"), lw)
     send_set(0)
     mine, wrapped = lw, pb(2, 8)
 
-    nac, nbc, umc, thr = [C(x) for x in ("nac", "nbc", "umc", "thr")]
+    nac, nbc, umc, thr, ha, hb = [C(x) for x in ("nac", "nbc", "umc", "thr", "ha", "hb")]
     for b in range(L):
-        w, nw, ta, nb, off, apn = ["%s%d" % (x, b) for x in ("w", "nw", "ta", "nb", "off", "ap")]
+        w, nw, ta, nb, apn = ["%s%d" % (x, b) for x in ("w", "nw", "ta", "nb", "ap")]
         last = b == L - 1
-        own, far, mrg = R(w, A0, B0), R(w, B0, 512), R(w, M0, A0)
-        nar, nbr = R(nw, A0, B0), R(nw, B0, 512)
-        tt(R("x8"), wrapped, R("m8"), Op.mult)
-        op("v", lambda q: q.tensor_copy(ap(R(ta)).indirect(ap(mine)), ap(R("i128"))), [R(ta)], [mine, R("i128")])
-        rsum(nac, R("x8"))
+        own, far, mrg = R(w, A0, B0), R(w, B0, W1), R(w, M0, A0)
+        nar, nbr = R(nw, A0, B0), R(nw, B0, W1)
+        tt(R("x8", 0, 8), wrapped, R("m8"), Op.mult)
+        scatter(R(ta), mine, R("i128"))
+        rsum(nac, R("x8", 0, 8))
         gather(nar, R("iN"), mine, "a")
         mm(pb(4), UB, own)
-        mm(pb(5), own, UB)
-        act(C("aac"), pb(5, 1), Act.Abs, TINY)
-        act(R("absa"), pb(4), Act.Abs, TINY)
-        act(C("ada"), C("aac"), Act.Copy, 0.0, ULP)
+        act(R("absa"), pb(4), Act.Abs, TINY * ULP, ULP)
+        if not last:
+            fill(R("ta%d" % (b + 1)), NONE, "a")
         if b == 0:
             fill(R("snap"), SNAP)
-            fill(R("cwt"), 0.0)
-            fill(R("ye"), 0.0)
-            fill(R("neg", 8, 16), 256.0)
-            ts(R("cwt", 0, 512, 4), o128, -1.0, Op.mult)
-            ts(R("cwt", 1, 512, 4), o128, 2.0 ** -7, Op.mult)
-            ts(R("ye", 1, 512, 4), o128, 1.0, Op.mult)
-            ts(C("pb"), C("ph"), 128.0, Op.subtract)
-            quant(WU, R("cwt"))
+            fill(R("neg"), 256.0)
+            fill(Y(1), 1.0)
+            fill(Y(3), 0.0)
+            fill(R("wx", 1, 640, 2), 0.0)
+            fill(R("wz", 1, 768, 2), 0.0)
+            ts(C("pb"), C("ph"), 256.0, Op.subtract)
+            ts(C("pc"), C("ph"), 128.0, Op.subtract)
+            fill(R("cwt", 0, 512, 4), -1.0 / ULP)
+            fill(R("cwt", 1, 512, 4), 2.0 ** -7 / ULP)
+            fill(R("cwt", 512, 513), 256.0)
+            ts(R("cwt", 513, 514), R("tri", 0, 1), HALF, Op.mult, 1.0 - HALF, Op.add)
+            fill(R("cwt", 514, 515), 1.0)
+            fill(R("cwt", 515, 517), -1.0)
+            fill(R("cwt", 517, 518), 2.0 ** -7)
+            quant(R("cw"), R("cwt"))
             act(D(0, 0), o8, Act.Copy, 0.0, C("pl"))
             act(D(1, 0), o8, Act.Copy, 0.0, C("pl"))
-            act(D(2, 0), o8, Act.Copy, 0.0, C("ph"))
-        ts(D(2, 1), R("snap"), nac, Op.add, SNAP, Op.subtract)
-        act(D(0, 1), D(2, 1), Act.Identity, nac, -1.0)
+            act(D(0, 2), o8, Act.Copy, 0.0, C("pc"))
+        act(C("nah"), nac, Act.Identity, -HALF)
+        ts(D(0, 3), R("snap"), C("nah"), Op.add, SNAP, Op.subtract)
+        act(D(0, 1), D(0, 3), Act.Identity, nac, -1.0)
         if b == 1:
             ts(R("idn"), R("i128"), C("p"), Op.is_equal)
-            ts(R("m16"), R("jm2", 0, 256, 2), HALF, Op.add, C("pl"), Op.is_equal)
-            ts(R("rs16"), R("jm2", 0, 256, 2), -7.0, Op.is_gt)
-            fill(R("tk"), 0.0)
-            fill(R("nlt"), 0.0)
-        if last:
             quant(R("qw"), R("wt"))
-            fill(R(nw, 0, 128), 0.0)
-            fill(R("yw", 0, 128), 0.0)
+            fill(R("tk"), 0.0)
+            fill(R("nlt", 1, 512, 4), 0.0)
+            fill(R("nlt", 512, 1024, 4), 0.0)
+        if last:
             act(R("nlt", 0, 512, 4), R("idn"), Act.Copy, 0.0, -240.0)
             act(R("nlt", 513, 1024, 4), R("idn"), Act.Copy, 0.0, -240.0)
-        else:
-            act(R("ta%d" % (b + 1)), R("ones"), Act.Copy, 0.0, NONE)
+            ts(R("nlt", 2, 512, 4), nar, nac, Op.is_gt)
         if b == 0:
-            mm(pb(6), E(0), R("nl", 0, 128), True, False)
-            mm(pb(6), E(0), R("nl", 8, 136), False, True)
+            pick(R("nx"), R("nl"), R("lc"))
+            mm(pb(6), R("nx"), R("nl", 0, 128), True, False)
+            mm(pb(6), R("nx"), R("nl", 8, 136), False, True)
             ts(R(nb), pb(6, 8), 256.0, Op.add)
-            tt(R("x8"), pb(6, 8), R("m8"), Op.mult)
-            pickc(R(apn), R("qg"), R(nb))
-            picks(R(apn), R("qg"), R(nb))
-            rsum(nbc, R("x8"))
-            act(R("mk"), R(ta), Act.Sign, NONE, -1.0, off=R(nb))
-            gather(nbr, R("iN"), R(nb))
+            tt(R("x8", 8, 16), pb(6, 8), R("m8"), Op.mult)
+            rsum(nbc, R("x8", 8, 16))
         else:
-            tt(R("xm"), R(ta), R("m16"), Op.mult, R(nb))
             tt(R("xp"), R("iN"), R("idn"), Op.mult, R(nb))
-            scan(R("sc"), R("rs16"), R("xm"), Op.mult, Op.add)
-            act(R("mk"), R(ta), Act.Sign, NONE, -1.0, off=R(nb))
             act(R("xj"), R("xp"), Act.Copy, acc=nbc)
-            ts(R(off), R("sc", 15, 128, 16), 127.0, Op.min)
-            gather(nbr, R("iN"), R(nb), "a")
-            ts(R("ye", 0, 512, 4), nar, nbc, Op.is_equal)
-            pickc(R(apn), own, R(off))
-            picks(R(apn), own, R(off))
-        for t in range(4):
-            mm(pb(t), E(t), far, True, False)
-        for t in range(4):
-            mm(pb(t), E(t), R(apn), False, True)
-        if b == 0:
-            ts(R("ye", 0, 512, 4), nar, nbc, Op.is_equal)
-        ts(R("fb", 0, 128), nar, nbc, Op.is_lt, 1.0 - ULP, Op.max)
+        pick(R(apn), R("wn%d" % b if b else "qg"), R(nb))
+        act(R("mk"), R(ta), Act.Sign, NONE, -1.0, off=R(nb))
+        gather(nbr, R("iN"), R(nb), "a")
+        for first in (True, False):
+            for t in range(4):
+                mm(pb(t), E(t), R(apn) if first == bool(CFG["own_first"][b]) else far, first, not first)
+        ts(Y(0), nar, nbc, Op.is_equal)
+        ts(Y(2), nar, nbc, Op.is_gt, -1.0, Op.mult)
+        act(C("nbh"), nbc, Act.Identity, -HALF)
+        ts(D(1, 3), R("snap"), C("nbh"), Op.add, SNAP, Op.subtract)
         quant(R("qe"), R("ye"))
-        ts(R("lta"), nbr, nac, Op.is_lt, -1.0, Op.mult)
-        mm(pb(4), WU, R("qe"))
+        if last:
+            ts(R("nlt", 514, 1024, 4), nbr, nac, Op.is_gt)
+            ts(R("nlt", 3, 1024, 4), R(nw, A0, W1), nbc, Op.is_gt)
         mm(pb(6), UB, far)
         mm(pb(7), far, UB)
-        mm(pb(5), R("qe"), WU)
+        mm(pb(4), WU, R("qe"), True, False)
+        mm(pb(4), E(2), R("qe"), False, True)
+        mm(pb(5), R("qe"), WR)
         act(R("um"), R("mk"), Act.Identity, 1.0, -1.0)
-        act(R("yj"), R("ye", 0, 512, 4), Act.Identity, 2.0 ** -7, -1.0, acc=umc)
-        act(R("ta"), R("lta"), Act.Identity, C("aac"), C("ada"))
+        act(R("yj"), Y(0), Act.Identity, 2.0 ** -7, -1.0, acc=umc)
+        act(D(1, 1), D(1, 3), Act.Identity, nbc, -1.0)
         act(C("sbt"), pb(7, 1), Act.Identity, TINY, umc)
-        act(C("ini"), pb(5, 1), Act.Identity, 128.0 - HALF, -128.0)
-        act(D(3, 0), R("neg", 8, 16), Act.Identity, C("pb"), umc)
-        for t in range(4):
-            tt(R("hm", t, 512, 4), pb(t), R("mk"), Op.mult)
-        tt(R("arow"), R("absa"), pb(4), Op.mult)
-        quant(mrg, R("hm"))
-        tt(R("sbs"), pb(6), R("um"), Op.mult)
-        ts(R("fb", 128, 256), nbr, nbc, Op.is_ge, 1.0 - ULP, Op.max)
-        tt(R("za"), R("arow"), R("fb", 0, 128), Op.mult)
-        mm(pb(0), UB, mrg)
-        mm(pb(1), mrg, UB)
-        if last:
-            mm(pb(3, 384), R("qw"), R(w, M0, 512))
-        tt(R("xb"), pb(0), R("sbs"), Op.add)
-        act(thr, pb(1, 1), Act.Abs, C("sbt"))
-        act(R("rowb"), R("xb"), Act.Abs, TINY)
-        act(R("tb"), R("fb", 128, 256), Act.Copy, 0.0, thr)
-        tt(R("ca", 0, 128), R("tri"), pb(4), Op.mult)
-        ts(D(3, 1), R("snap"), nbc, Op.add, SNAP, Op.subtract)
-        ts(R("cb", 0, 128), R("za"), thr, Op.is_ge)
-        act(D(1, 1), D(3, 1), Act.Identity, nbc, -1.0)
-        tt(R("ca", 128, 256), R("rowb"), R("ta"), Op.is_gt)
-        tt(R("cb", 128, 256), R("rowb"), R("tb"), Op.is_gt)
+        act(D(1, 2), R("neg"), Act.Identity, C("pb"), umc)
         if last:
             copy(R(nw, M0, A0), nbr, "a")
-            copy(R("yw", M0, 512), pb(3, 384), "a")
-        scan(R("rk", 0, 128), R("ca", 0, 128), R("ca", 128, 256), Op.add, Op.add, C("ini"))
+        for t in range(4):
+            tt(R("hm", t, 512, 4), pb(t), R("mk"), Op.mult)
+        tt(R("sbs"), pb(6), R("um"), Op.mult)
+        quant(mrg, R("hm"))
+        tt(R("za"), pb(4), R("absa"), Op.mult)
+        ts(R("fb"), nbr, nbc, Op.is_ge, 1.0 - ULP, Op.max)
+        ts(Y(2), R("i128"), C("p"), Op.is_gt, pb(5, 128, 127), Op.mult)
+        if not last:
+            act(C("la"), one(D(0, 3)), Act.Identity, nac, -1.0)
+            ts(R("wz", 256, 768, 4), R("jq"), C("la"), Op.is_equal, pb(5, 128, 127), Op.mult)
+            ts(R("wz", 258, 768, 4), R("jq"), one(D(1, 1)), Op.is_equal)
+            for sd in range(2):
+                for k in range(2):
+                    ts(R("wz", 128 * k + 2 * sd, 128 * k + 128, 4), R("iN", 0, 512, 16), one(D(sd, 3)), Op.is_equal, one(D(sd, 2 * k)), Op.mult)
+            quant(R("qwz"), R("wz"))
+            mm(pb(3), R("qwz", 64, 192), R("qwz", 0, 128), True, False)
+            mm(pb(3), R("qwz", 64, 192), R("qwz", 32, 160), False, True)
+            ts(R("lz"), pb(3, 32), 256.0, Op.add)
+            for k in range(4):
+                pick(R("wn%d" % (b + 1), 128 * k, 128 * k + 128), R(w), R("lz", 8 * k, 8 * k + 8))
+        mm(pb(1), mrg, UB)
+        mm(pb(0), UB, mrg)
         if last:
-            ts(R("nlt", 2, 1024, 4), R(nw, A0, 512), nac, Op.is_gt)
-        scan(R("rk", 128, 256), R("cb", 0, 128), R("cb", 128, 256), Op.add, Op.add, -HALF)
+            mm(pb(3, W1), R("qw"), R(w))
+        act(thr, pb(1, 1), Act.Abs, C("sbt"))
+        tt(R("xb"), pb(0), R("sbs"), Op.add)
+        act(R("tb"), R("fb"), Act.Copy, 0.0, thr)
+        ts(Y(3), R("za"), thr, Op.is_ge)
+        act(R("rowb"), R("xb"), Act.Abs, TINY)
         if last:
-            ts(R("nlt", 3, 1024, 4), R(nw, A0, 512), nbc, Op.is_gt)
-        both, ra, rb = R("rk", 127, 256, 128), R("rk", 127, 128), R("rk", 255, 256)
+            quant(R("qlt", 0, 128), R("nlt", 0, 512))
+            quant(R("qlt", 128, 256), R("nlt", 512, 1024))
+        quant(R("ql"), R("ye"))
+        mm(pb(5), R("ql"), WR)
+        tt(R("cb"), R("rowb"), R("tb"), Op.is_gt)
+        ra, rb, rh = pb(5, 127, 126), R("rk", 127, 128), R("rk", 255, 256)
+        ea, eb = R("ex", 0, 32), R("ex", 32, 64)
+
+        def cols(e, h):
+            ts(e, R("c32"), h, Op.is_equal)
+
+        def rows(t, h, r):
+            ts(R("wx", 128 + t, 640, 4), R("jm"), h, Op.add, r, Op.is_equal)
+
+        def digits(sd, e):
+            tt(R("wx", 2 * sd, 128, 4), e, R("dv", 32 * sd, 32 * sd + 32), Op.mult)
+
+        scan(R("rk", 0, 128), Y(3), R("cb"), Op.add, Op.add, -HALF)
         if last:
-            ts(R("tk", 8, 10), both, 128.0 - 8, Op.is_lt, 31.0 / 32, Op.subtract)
-            ts(R("tk", 10, 12), both, 128.0 - 8, Op.is_lt)
-            quant(R("qlt"), R("nlt"))
+            copy(R("yw"), pb(3, W1), "a")
+            ts(R("tk", 8, 9), ra, 128.0 - 8, Op.is_lt, 31.0 / 32, Op.subtract)
+            ts(R("tk", 10, 11), ra, 128.0 - 8, Op.is_lt)
+            ts(R("tk", 9, 10), rb, 128.0 - 8, Op.is_lt, 31.0 / 32, Op.subtract)
+            ts(R("tk", 11, 12), rb, 128.0 - 8, Op.is_lt)
             quant(R("qtk"), R("tk"))
-            mm(pb(6), R("qlt", 0, 128), R("qtk", 2, 130), True, False)
-            mm(pb(6), R("qlt", 128, 256), R("qtk", 0, 128), False, True)
-            both, ra, rb = pb(6, 3, 0, 2), pb(6, 1), pb(6, 3, 2)
-        ha, hb = (C("h0"), C("h1")) if last else (R("rk", 0, 1), R("rk", 2, 3))
-        ts(ha[:2] + (ha[1] + 3, 2), both, SNAP, Op.add, SNAP, Op.subtract)
-        ts(R("ex", 0, 64, 2), R("c32"), ha, Op.is_equal)
-        ts(R("ex", 1, 64, 2), R("c32"), hb, Op.is_equal)
-        ts(R("wx", 64, 576, 2), R("jm2"), ha, Op.add, ra, Op.is_equal)
-        ts(R("wx", 65, 576, 2), R("jm2"), hb, Op.add, rb, Op.is_equal)
-        tt(R("wx", 0, 64), R("ex"), R("dv"), Op.mult)
+            mm(pb(6), R("qlt", 0, 128), R("qtk", 2, 130))
+            mm(pb(7), R("qlt", 128, 256), R("qtk", 2, 130))
+            ra, rb = pb(6, 1), pb(7, 1)
+            snap(ha, ra), cols(ea, ha), snap(hb, rb), rows(0, ha, ra), digits(0, ea), cols(eb, hb), rows(2, hb, rb), digits(1, eb)
+        else:
+            snap(ha, ra)
+            scan(R("rk", 128, 256), Y(3), R("cb"), Op.add, Op.add, TOP - HALF)
+            cols(ea, ha), rows(0, ha, ra), digits(0, ea)
+            ts(eb, R("c32"), TOP, Op.add, rh, Op.is_equal)
+            ts(R("wx", 130, 640, 4), R("jf"), rh, Op.add, rb, Op.is_equal)
+            digits(1, eb)
         quant(R("qwx"), R("wx"))
-        mm(pb(2), WX, R("qwx", 0, 128))
+        mm(pb(2), WX, R("qwx", 0, 128), True, False)
+        mm(pb(2), WX, R("qwx", 16, 144), False, True)
         ln = "lw%d" % (b + 1)
         ts(R(ln), pb(2, 16), 256.0, Op.add)
         lw, mine, wrapped = R(ln, 0, 8), R(ln, 8, 16), pb(2, 16, 8)
         if not last:
-            nxt = R("w%d" % (b + 1), A0, B0)
-            pickc(nxt, R(w), lw)
-            picks(nxt, R(w), lw)
-            send(b + 1, R("nb%d" % (b + 1)), mine, "an%d" % (b + 1), True)
-            arrive("an%d" % (b + 1), [R("nb%d" % (b + 1))])
+            pick(R("w%d" % (b + 1), A0, B0), R(w), lw)
+            arrive("an%d" % (b + 1), [R("nb%d" % (b + 1))], [send(b + 1, R("nb%d" % (b + 1)), mine, "an%d" % (b + 1), CFG["num"][b + 1], True)])
             send_set(b + 1)
         else:
-            pickc(R("w3"), R(w), lw)
-            gather(R("yo"), R("yw"), lw, "a")
+            pick(R("w3"), R(w), lw)
             dma("s", T.oc[:, 0:512], ap(R("w3")).bitcast(dt.uint8), [], [R("w3")])
-            ts(R("nbo"), R(nw), 256.0, Op.add, off=lw)
-            picks(R("w3"), R(w), lw)
+            gather(R("yo"), R("yw"), lw)
+            act(R("nbo"), R(nw), Act.Identity, 256.0, off=lw)
+
+            def scales(e, k):
+                dma(e, T.osc[4 * k:4 * k + 4, 0:128], T["w3s"][32 * k:32 * k + 4, 0:128], [], [R("w3s")])
+
+            scales("s", 0), scales("s", 1)
             dma("s", T.y[:, 0:128], ap(R("yo")), [], [R("yo")])
-            dma("s", T.nb[0:1, 0:128], T.nbo[0:1, 0:128], [], [R("nbo")])
-            for k in range(4):
-                dma("s" if k == 3 else "a", T.osc[4 * k:4 * k + 4, 0:128], T["w3s"][32 * k:32 * k + 4, 0:128], [], [R("w3s")])
+            scales("a", 2), scales("a", 3)
+            dma("a", T.nb[0:1, 0:128], T.nbo[0:1, 0:128], [], [R("nbo")])
+    if str(CFG) not in ORDER:
+        ORDER[str(CFG)] = order()
+    for k in ORDER[str(CFG)]:
+        nodes[k][1]()
     for s in sorted(total):
         g.wait_ge(T.sem[s], total[s])

@@ -10,9 +10,8 @@ SNAP = 1.5 * 2.0 ** 27
 HALF = 7.5
 TOP = 3072.0
 
-CFG = dict(hop=220, f=1.0, load=(1500, 1900, 2300, 2700), num=(1100, 1100, 1100), set=(1100, 1400, 1400), issue=150, amin=120,
-           dual0=False, fuse0=False, fuse=False, own_first=(0, 1, 1))
-ORDER = {}
+PLAN = dict(ORDER=r"000102030409061K078=8<0@0>0G0:0B0P0U8E080V0X0C8W0H0Z0;0Y0[0\960`8F0a8A9U0b8J1h0f9A8O0N0]0?0^050h0_0c0l0g0e0m0d0j120i131<1>0o0n101\0k1?1=1S1G1@1J14151Q1B1I17911C1T181H1L1E1D1F1R:6:31V1M:81:19:41W9m1O1N1P1;1Z1X1Y9n2<221[0Q0S:1:70M1`0R1]1a1^:5:@8D1b292C1c9l2E1_1e2L9d8K2G:M2N2D:I2O:F2H:01f1g2W2X9k2P2Q2J0T2R2S2Z2_:T2`392Y:U0L2]2d2\2^2[9o302i2o:V2k312n:a:j8I2f35332e2b:l2g:m2h3E:c323F3G36343::K3H3J3I3<3L3K3M9j::3N9i38373Q3O3P3W3S3V3T3R3U3[3Y3X3Z3\3;:A3`3]3^2=3a3=3b3_3c3>3k3?;e3d3o3@;n3l;D3f3C3A3g3h4446;B3i3m<74=4;4<<5<83j4:2;404B4?4C4>4A4@41<94N4G4R<M4J4Q4T4S4X4I4L424H4V4U4K<D<O4h4]<34E4j4W4i4Y4k4m4l4^<F4o4Z4n51504\<P534[52545758555:59:>565=5;5<5>5?4_5C5@4`5A5D5E5B5F4a=H4b5G4c5O=Q5R4d5I5J<g<e4f=X5K5L5U=V5M5W5^5N5[5\5Z5d5]5`=Y5c5e5S5a>05b5_5m5l655n665k6764:?615P6;>25o69685T6=5j6A6>6:6<6B6D6C5f6?6F6E6H5g6I:B6G6J6K6L6M5h6N6O5i6P6Q>3>@6R6V6S6U6T6X6W6Y6Z6[6\>^6]6_>a6b6`6c>d>e>f>g",
+            signs=(0, 1, 2, 2), chunks=2, own_first=(0, 1, 1), loads=((0, 512), (512, 1024), (1024, 1536), (1536, 2048)))
 SCRATCH = {}
 
 
@@ -25,32 +24,28 @@ def _codes(name, cols):
     _buf(name + "s", cols, "uint8")
 
 
-for _n, _c in (("ones", 544), ("tri", 128), ("jq", 128), ("wz", 768), ("rh", 800), ("i128", 128), ("hq", 4), ("d0", 64), ("jm", 128), ("c32", 32),
-               ("iN", 512), ("m8", 8), ("neg", 8), ("u4", 4), ("ut", 512), ("grt", 2048), ("wt", 512), ("cwt", 520), ("et", 520),
-               ("wy", 576), ("wx", 640), ("ey", 64), ("ex", 64), ("dv", 64), ("tk", 520), ("nlt", 1024), ("sg", 768), ("cc", 1600),
-               ("rs", 800), ("r0", 128), ("ye", 512), ("yj", 128), ("r1", 128), ("xp", 128), ("xj", 128), ("x8", 16), ("mk", 128),
-               ("um", 128), ("hm", 512), ("cb", 128), ("idn", 128), ("rk", 256), ("nw0", W1), ("nw1", W1), ("nw2", W1),
-               ("ta0", 512), ("ta1", 512), ("ta2", 512)):
+for _n, _c in (("ones", 544), ("tri", 128), ("jq", 128), ("jm", 128), ("i128", 128), ("ct", 8), ("hq", 4), ("d0", 8), ("iN", 512), ("m8", 8),
+               ("u4", 4), ("ut", 512), ("grt", 2048), ("wt", 512), ("cwt", 520), ("et", 520), ("wy", 576), ("wx", 576), ("wv", 512), ("wz", 768),
+               ("dv", 4), ("tk", 520), ("nlt", 1024), ("sg", 1536), ("cc", 2080), ("rs", 1040), ("ye", 512), ("yj", 128), ("xp", 128),
+               ("xj", 128), ("x8", 16), ("mk", 128), ("um", 128), ("hm", 512), ("cb", 128), ("idn", 128), ("rk", 256),
+               ("nw0", W1), ("nw1", W1), ("nw2", W1), ("ta0", 512), ("ta1", 512), ("ta2", 512)):
     _buf(_n, _c, "bfloat16")
 for _n, _c in (("f0", 128), ("t0", 512), ("ar", 512), ("small", 64), ("absa", 128), ("za", 128), ("sbs", 128), ("xb", 128),
-               ("rowb", 128), ("fb", 128), ("tb", 128), ("nbo", 128), ("snap", 8), ("yw", W1), ("yo", 128), ("jf", 128)):
+               ("rowb", 128), ("fb", 128), ("tb", 128), ("nbo", 128), ("yw", W1), ("yo", 128), ("jf", 128)):
     _buf(_n, _c, "float32")
-for _n in ("lw0", "lw1", "lw2", "lw3"):
-    _buf(_n, 16, "uint16")
-for _n in ("nb0", "nb1", "nb2", "lc"):
-    _buf(_n, 8, "uint16")
-_buf("lz", 32, "uint16")
+for _n, _c in (("lw0", 16), ("lw1", 16), ("lw2", 16), ("lw3", 16), ("nb0", 8), ("nb1", 8), ("nb2", 8), ("lc", 8), ("lz", 32)):
+    _buf(_n, _c, "uint16")
 for _n, _c in (("cu", 128), ("qg", 512), ("qw", 128), ("cw", 130), ("ce", 512), ("nx", 128), ("nl", 136), ("qwz", 192), ("wn1", 512), ("wn2", 512),
-               ("qwy", 144), ("qwx", 160), ("qe", 128), ("ql", 128), ("qtk", 130), ("qlt", 256), ("w0", W1), ("w1", W1), ("w2", W1), ("w3", 128),
-               ("ap0", 128), ("ap1", 128), ("ap2", 128)):
+               ("qwy", 144), ("qwx", 144), ("qwv", 136), ("qe", 128), ("ql", 128), ("qtk", 130), ("qlt", 256),
+               ("w0", W1), ("w1", W1), ("w2", W1), ("w3", 128), ("ap0", 128), ("ap1", 128), ("ap2", 128)):
     _codes(_n, _c)
 SMALL = {}
-for _i, _n in enumerate(("p", "ph", "pl", "pb", "pc", "a0", "a1", "a2", "a3", "s1", "s2", "s3", "sbt", "thr", "nac", "nbc",
-                         "umc", "ha", "hb", "la", "nah", "nbh")):
+for _i, _n in enumerate(("p", "ph", "pl", "pb", "pc", "pd", "a0", "a1", "a2", "a3", "s1", "s2", "s3", "sbt", "thr", "nac", "nbc",
+                         "umc", "ha", "hb", "la", "nah", "nbh", "nahi", "sbh")):
     SMALL[_n] = 2 * _i
 for _i in range(8):
     _buf("p%d" % _i, 512, "float32", "psum")
-SEMAPHORES = ["sv", "sa", "st", "sp", "sent", "ac0", "ac1", "ac2", "an0", "an1", "an2", "ready"] + ["d%d" % i for i in range(16)]
+SEMAPHORES = ["sv", "sa", "st", "sp", "sent", "ac0", "ac1", "ac2", "an0", "an1", "an2", "ready", "out"] + ["d%d" % i for i in range(6)]
 
 
 def rank_program(g, core, T, topo):
@@ -92,13 +87,15 @@ def rank_program(g, core, T, topo):
             for r in regs:
                 recs.setdefault(r[0], []).append((r, w, s, c, e))
 
-    nodes = []
+    nodes, either = [], []
+    code = [64 * (ord(x) - 48) + ord(y) - 48 for x, y in zip((PLAN["ORDER"] or "")[::2], (PLAN["ORDER"] or "")[1::2])]
+    order, marked = [k % 512 for k in code], {k % 512 for k in code if k >= 512}
 
-    def node(e, run, outs, ins, cost, lat=None, after=()):
-        nodes.append((e, run, outs, ins, cost, CFG["hop"] if lat is None else lat, after))
+    def node(e, run, outs, ins, after=()):
+        nodes.append((e, run, outs, ins, list(after)))
         return len(nodes) - 1
 
-    def op(e, call, outs, ins, cost):
+    def op(e, call, outs, ins):
         def run():
             waits(e, outs, ins)
             s = ESEM[e]
@@ -107,67 +104,33 @@ def rank_program(g, core, T, topo):
             hist[(s, total[s])] = dict(known[e])
             hist[(s, total[s])][s] = total[s]
             note(s, total[s], e, outs, ins)
-        node(e, run, outs, ins, max(cost, CFG["amin"] if e == "a" else 0) * CFG["f"])
+        node(e, run, outs, ins)
 
-    nd, dmas = [0], set()
+    nd = [0]
 
-    def dma(e, out, in_, outs, ins, lat=1500):
+    def dma(e, out, in_, outs, ins, after=()):
         def run():
             waits(e, outs, ins)
-            s = "d%d" % nd[0]
+            s = "d%d" % nd[0] if outs else "out"
             nd[0] += 1
-            total[s] = 16
+            total[s] = total.get(s, 0) + 16
             Q[e].dma_start(out, in_).then_inc(T.sem[s], 16)
-            hist[(s, 16)] = dict(known[e])
-            note(s, 16, "dma", outs, ins)
-        dmas.add(node(e, run, outs, ins, 60, lat))
+            if outs:
+                hist[(s, 16)] = dict(known[e])
+                note(s, 16, "dma", outs, ins)
+        return node(e, run, outs, ins, after)
 
-    def order():
-        seen, preds, tail = {}, [], {}
-        for k, (e, _run, outs, ins, _cost, _lat, after) in enumerate(nodes):
-            need = {j: nodes[j][5] for j in after}
-            for regs, isw in ((ins, False), (outs, True)):
-                for r in regs:
-                    ps = SCRATCH[r[0]][0] == "psum"
-                    for q, w, j in seen.get(r[0], []):
-                        if ps and nodes[j][0] == e == "t":
-                            need.setdefault(j, 0)
-                        elif (ps and nodes[j][0] != e) or ((w or isw) and (ps or meet(r, q))):
-                            need[j] = nodes[j][5]
-            if e in "ps" or k in dmas:
-                if e in tail:
-                    need.setdefault(tail[e], 0)
-                tail[e] = k
-            for regs, w in ((ins, False), (outs, True)):
-                for r in regs:
-                    seen.setdefault(r[0], []).append((r, w, k))
-            preds.append(need)
-        way = [n[4] + (n[5] if not n[2] else 0) for n in nodes]
-        for k in reversed(range(len(nodes))):
-            for j, lat in preds[k].items():
-                way[j] = max(way[j], nodes[j][4] + lat + way[k])
-        start, busy = {}, {}
-        for k in sorted(range(len(nodes)), key=lambda k: (-way[k], k)):
-            e, cost = nodes[k][0], nodes[k][4]
-            t = max([start[j] + nodes[j][4] + lat for j, lat in preds[k].items()] + [0])
-            if e != "x":
-                for a, b in busy.setdefault(e, []):
-                    if t + cost <= a:
-                        break
-                    t = max(t, b)
-                busy[e].append((t, t + cost))
-                busy[e].sort()
-            start[k] = t
-        return sorted(range(len(nodes)), key=lambda k: (start[k], k))
+    def scalar(e):
+        either.append(len(nodes))
+        if PLAN.get("SIDE"):
+            return PLAN["SIDE"][len(either) - 1] == "a"
+        return len(nodes) in marked if code else e == "a"
 
     def R(n, a=0, b=None, st=1):
         return (n, a, SCRATCH[n][1][1] if b is None else b, st)
 
     def C(n):
         return ("small", SMALL[n], SMALL[n] + 1, 1)
-
-    def one(r):
-        return (r[0], r[1], r[1] + 1, 1)
 
     def ap(r):
         if r[3] == 1:
@@ -186,73 +149,65 @@ def rank_program(g, core, T, topo):
     def by(win, off):
         return ap(win) if off is None else ap(win).indirect(ap(off))
 
-    def span(r, two=False, *more):
-        n = len(range(*r[1:]))
-        if two is None:
-            return max(53, 0.83 * n)
-        if two:
-            return max(53, 0.83 * n * (1 if any(SCRATCH[x[0]][0] == "psum" for x in more) else 2))
-        return max(53, 0.83 * n * (0.5 if all(SCRATCH[x[0]][2] in ("bfloat16", "uint16") for x in (r,) + more) else 1))
-
-    def listed(r):
-        return 60 + 1.25 * len(range(*r[1:]))
-
-    def fill(r, c, e="v"):
-        if e == "v":
-            op("v", lambda q: q.memset(ap(r), c), [r], [], span(r))
-        else:
-            act(r, R("ones", 0, len(range(*r[1:]))), Act.Copy, 0.0, c)
-
-    def copy(o, i, e="v"):
-        if e == "v":
-            op("v", lambda q: q.tensor_copy(ap(o), ap(i)), [o], [i], span(o, False, i))
-        else:
-            op("a", lambda q: q.activation(ap(o), ap(i), Act.Copy), [o], [i], span(o, None))
-
     def act(o, i, f, bias=0.0, scale=1.0, acc=None, off=None):
         ins = [i] + [x for x in (bias, scale, off) if isr(x)]
         if acc is None:
-            op("a", lambda q: q.activation(ap(o), by(i, off), f, bias=sap(bias), scale=sap(scale)), [o], ins, listed(o) if off else span(o, None))
+            op("a", lambda q: q.activation(ap(o), by(i, off), f, bias=sap(bias), scale=sap(scale)), [o], ins)
         else:
-            op("a", lambda q: q.activation(ap(o), ap(i), f, bias=sap(bias), scale=sap(scale), accum_out=ap(acc)), [o, acc], ins, span(o, None) + 20)
+            op("a", lambda q: q.activation(ap(o), ap(i), f, bias=sap(bias), scale=sap(scale), accum_out=ap(acc)), [o, acc], ins)
 
     def tt(o, a, b, f, off=None):
-        op("v", lambda q: q.tensor_tensor(ap(o), by(a, off), ap(b), f), [o], [a, b] + ([off] if off else []), listed(o) if off else span(o, True, a, b))
+        op("v", lambda q: q.tensor_tensor(ap(o), by(a, off), ap(b), f), [o], [a, b] + ([off] if off else []))
 
     def ts(o, i, s1, f1, s2=None, f2=None, off=None):
         ins = [i] + [x for x in (s1, s2, off) if isr(x)]
         if f2 is None:
-            op("v", lambda q: q.tensor_scalar(ap(o), by(i, off), sap(s1), None, f1), [o], ins, listed(o) if off else span(o, False, i))
+            op("v", lambda q: q.tensor_scalar(ap(o), by(i, off), sap(s1), None, f1), [o], ins)
         else:
-            op("v", lambda q: q.tensor_scalar(ap(o), by(i, off), sap(s1), sap(s2), f1, f2), [o], ins, listed(o) if off else span(o, False, i))
+            op("v", lambda q: q.tensor_scalar(ap(o), by(i, off), sap(s1), sap(s2), f1, f2), [o], ins)
 
-    def scan(o, a, b, f0, f1, first=0.0):
-        op("v", lambda q: q.tensor_tensor_scan(ap(o), ap(a), ap(b), sap(first), f0, f1), [o], [a, b] + ([first] if isr(first) else []), span(o, False, a, b))
+    def scan(o, a, b, first):
+        op("v", lambda q: q.tensor_tensor_scan(ap(o), ap(a), ap(b), sap(first), Op.add, Op.add), [o], [a, b] + ([first] if isr(first) else []))
 
     def rsum(o, i):
-        op("v", lambda q: q.tensor_reduce(ap(o), ap(i), AxisListType.X, Op.add), [o], [i], span(i, None))
+        op("v", lambda q: q.tensor_reduce(ap(o), ap(i), AxisListType.X, Op.add), [o], [i])
 
-    def iota(o, pat, base, cm):
-        op("p", lambda q: q.iota(ap(o), pat, base, cm, allow_small_or_imprecise_dtypes=True), [o], [], 130 + 1.66 * len(range(*o[1:])))
+    def iota(o, pat, cm):
+        op("p", lambda q: q.iota(ap(o), pat, 0, cm, allow_small_or_imprecise_dtypes=True), [o], [])
 
-    def gather(o, win, off, e="v"):
-        if e == "v":
-            op("v", lambda q: q.tensor_copy(ap(o), ap(win).indirect(ap(off))), [o], [win, off], listed(o))
+    def memset(r, c):
+        op("v", lambda q: q.memset(ap(r), c), [r], [])
+
+    def fill(r, c, e="v"):
+        if scalar(e):
+            act(r, R("ones", 0, len(range(*r[1:]))), Act.Copy, 0.0, c)
         else:
-            op("a", lambda q: q.activation(ap(o), ap(win).indirect(ap(off)), Act.Copy), [o], [win, off], listed(o))
+            memset(r, c)
+
+    def line(o, i, mul, add, e="a"):
+        if scalar(e):
+            act(o, i, Act.Identity, add, mul)
+        else:
+            ts(o, i, mul, Op.mult, add, Op.add)
+
+    def copy(o, i, e="a", off=None):
+        if scalar(e):
+            op("a", lambda q: q.activation(ap(o), by(i, off), Act.Copy), [o], [i] + ([off] if off else []))
+        else:
+            op("v", lambda q: q.tensor_copy(ap(o), by(i, off)), [o], [i] + ([off] if off else []))
 
     def scatter(win, off, i):
-        op("v", lambda q: q.tensor_copy(ap(win).indirect(ap(off)), ap(i)), [win], [off, i], 2 * listed(i))
+        op("v", lambda q: q.tensor_copy(ap(win).indirect(ap(off)), ap(i)), [win], [off, i])
 
     def pick(o, win, off):
-        op("v", lambda q: q.tensor_copy(ap(o).bitcast(dt.uint32), ap(win).bitcast(dt.uint32).indirect(ap(off))), [o], [win, off], listed(o))
-        gather(S(o), S(win), off, "a")
+        op("v", lambda q: q.tensor_copy(ap(o).bitcast(dt.uint32), ap(win).bitcast(dt.uint32).indirect(ap(off))), [o], [win, off])
+        copy(S(o), S(win), "a", off)
 
     def quant(o, i):
-        op("v", lambda q: q.quantize_mx(ap(o), ap(S(o)), ap(i)), [o, S(o)], [i], 12 + 0.22 * (i[2] - i[1]))
+        op("v", lambda q: q.quantize_mx(ap(o), ap(S(o)), ap(i)), [o, S(o)], [i])
 
     def mm(o, a, b, start=True, stop=True):
-        op("t", lambda q: q.matmul_mx(ap(o), ap(a), ap(S(a)), ap(b), ap(S(b)), start, stop), [o], [a, S(a), b, S(b)], 0.6 * (16 + o[2] - o[1]))
+        op("t", lambda q: q.matmul_mx(ap(o), ap(a), ap(S(a)), ap(b), ap(S(b)), start, stop), [o], [a, S(a), b, S(b)])
 
     def snap(o, i):
         ts(o, i, SNAP, Op.add, SNAP, Op.subtract)
@@ -268,49 +223,47 @@ def rank_program(g, core, T, topo):
         total["sent"] = total.get("sent", 0) + n
         total[sem] = total.get(sem, 0) + n
 
-    def send(b, o, i, sem, lat, raw=False):
+    gate = []
+
+    def send(b, o, i, sem, raw=False):
         def run():
             waits("p", [], [i])
             pid, rid, mask, n = route(b)
             x, y = (ap(o), ap(i)) if raw else (ap(o).bitcast(dt.uint8), ap(i).bitcast(dt.uint8))
             g.remote_dma(x, y, T.sem[sem], T.sem["sent"], pid, rid, mask)
             sent(sem, n)
-        return node("p", run, [], [i], CFG["issue"], lat)
+        return node("p", run, [], [i], gate)
 
     def arrive(sem, outs, after):
-        node("x", lambda: note(sem, total[sem], "far", outs, []), outs, [], 1, 0, after)
+        node("x", lambda: note(sem, total[sem], "far", outs, []), outs, [], after)
 
-    def send_codes(b, o, i, sem, lat):
-        arrive(sem, [o, S(o)], [send(b, o, i, sem, lat), send(b, S(o), S(i), sem, lat, True)])
+    def send_codes(b, o, i, sem):
+        arrive(sem, [o, S(o)], [send(b, o, i, sem), send(b, S(o), S(i), sem, True)])
 
     def send_set(b):
-        send_codes(b, R("w%d" % b, B0, W1), R("w%d" % b, A0, B0), "ac%d" % b, CFG["set"][b])
+        send_codes(b, R("w%d" % b, B0, W1), R("w%d" % b, A0, B0), "ac%d" % b)
 
-    UB, WU, WR, WY, WX = R("cu"), R("cw", 0, 128), R("cw", 2, 130), R("qwy", 16, 144), R("qwx", 32, 160)
+    UB, WU, WR, WY, WX = R("cu"), R("cw", 0, 128), R("cw", 2, 130), R("qwy", 16, 144), R("qwx", 16, 144)
 
     def E(t):
         return R("ce", 128 * t, 128 * t + 128)
 
-    def pb(i, n=128, a=0, st=1):
-        return R("p%d" % i, a, n, st)
-
-    def D(side, k):
-        return R("dv", 32 * side + 8 * k, 32 * side + 8 * k + 8)
+    def pb(i, n=128, a=0):
+        return R("p%d" % i, a, n)
 
     def Y(t):
         return R("ye", t, 512, 4)
 
-    dma("a", ap(R("u4")), T.u[:, 0:4], [R("u4")], [], CFG["load"][0] - 300)
-    for q in range(4):
-        r = R("grt", 512 * q, 512 * q + 512)
-        dma("a" if q % 2 else "s", ap(r), T.gr[:, 512 * q:512 * q + 512], [r], [], CFG["load"][q])
+    k = dma("a", ap(R("u4")), T.u[:, 0:4], [R("u4")], [])
+    for q, (a, b) in enumerate(PLAN["loads"]):
+        k = dma("a" if q % 2 else "s", ap(R("grt", a, b)), T.gr[:, a:b], [R("grt", a, b)], [], [k])
+    dma("s", ap(R("wt")), T.w[:, 0:512], [R("wt")], [R("grt", 1536, 2048)])
 
-    o128, o8 = R("ones", 0, 128), R("ones", 0, 8)
-    iota(C("p"), [[1, 1]], 0, 1)
-    iota(R("i128"), [[1, 128]], 0, 0)
-    iota(R("jm"), [[0, 8], [1, 16]], 0, 0)
-    iota(R("c32"), [[0, 4], [16, 8]], 0, 0)
-    fill(R("ones"), 1.0)
+    o128, o8, c8 = R("ones", 0, 128), R("ones", 0, 8), R("i128", 0, 128, 16)
+    iota(C("p"), [[1, 1]], 1)
+    iota(R("i128"), [[1, 128]], 0)
+    iota(R("jq"), [[0, 8], [1, 16]], 0)
+    memset(R("ones"), 1.0)
     quant(R("nl"), R("ones"))
     pid, rid, mask, nready = route(0)
 
@@ -319,116 +272,66 @@ def rank_program(g, core, T, topo):
         g.remote_sem_update(T.sem["ready"], T.sem["sent"], pid, rid, mask)
         sent("ready", nready)
 
-    node("p", ready, [R("nl"), R("nls")], [], 3000, 0)
+    told = node("p", ready, [R("nl"), R("nls")], [])
     fill(R("et"), 0.0)
-    ts(C("pb"), C("p"), HALF, Op.subtract)
+    line(C("pb"), C("p"), 1.0, -HALF, "v")
     ts(R("tri"), R("i128"), C("p"), Op.is_lt)
     ts(R("et", 3, 515, 4), R("i128"), C("p"), Op.is_equal)
     snap(C("ph"), C("pb"))
-    ts(R("f0"), R("tri"), -ULP, Op.mult, 1.0, Op.add)
-    tt(C("pl"), C("p"), C("ph"), Op.subtract)
-    fill(R("cc", 407, 1600, 400), -HALF)
-    fill(R("cc", 406, 1600, 400), TOP)
-    fill(R("cc", 792, 794), 0.0)
-    fill(R("cc", 1064, 1066), 0.0)
-    fill(R("cc", 1464, 1466), 0.0)
-    fill(R("ta0"), NONE, "a")
+    line(R("f0"), R("tri"), -ULP, 1.0, "v")
+    line(C("pl"), C("ph"), -1.0, C("p"), "v")
+    fill(R("cc", 0, 2080, 520), -HALF)
+    fill(R("ta0"), NONE)
     for t in range(4):
-        act(R("iN", 128 * t, 128 * t + 128), R("i128"), Act.Copy, 128.0 * (t - 2))
-    copy(R("jq"), R("jm"), "a")
-    act(R("jf"), R("jm"), Act.Identity, -HALF - TOP)
-    act(R("jm"), R("jm"), Act.Identity, -HALF)
+        line(R("iN", 128 * t, 128 * t + 128), R("i128"), 1.0, 128.0 * (t - 2))
+    line(R("jf"), R("jq"), 1.0, -HALF - TOP)
+    line(R("jm"), R("jq"), 1.0, -HALF)
+    line(R("ct"), c8, 1.0, TOP)
+    quant(R("qwv", 8, 136), R("ones", 0, 512))
     ts(R("lc"), o8, C("pl"), Op.mult, 16.0, Op.add)
-    act(R("d0", 0, 32), R("ones", 0, 32), Act.Copy, 0.0, C("pl"))
-    for t in range(4):
-        act(R("d0", 32 + t, 64, 4), o8, Act.Identity, C("ph"), 128.0 * (t - 2))
+    line(R("d0", 0, 4), R("ones", 0, 4), C("pl"), 0.0)
+    line(R("d0", 4, 8), R("iN", 0, 512, 128), 1.0, C("ph"))
+    ts(R("m8"), c8, C("ph"), Op.is_equal)
     for t in range(4):
         quant(E(t), R("et", 3 - t, 515 - t))
-    for t in range(3):
-        ts(R("ut", t, 512, 4), o128, R("u4", t, t + 1), Op.mult)
-    act(R("ut", 3, 512, 4), o128, Act.Identity, R("u4", 3, 4), 0.0)
+    for t in range(4):
+        line(R("ut", t, 512, 4), o128, 0.0, R("u4", t, t + 1), "va"[t // 3])
     quant(R("cu"), R("ut"))
-    fill(R("cwt"), 0.0, "a")
 
     def blk(q, n=1):
         return R("ar", 128 * q, 128 * (q + n))
 
-    def pack(q):
+    for q in range(4):
         a, b = 128 * q, 128 * q + 128
         quant(R("qg", a, b), R("grt", 4 * a, 4 * b))
         mm(pb(4 + q), R("qg", a, b), UB)
         mm(pb(q), UB, R("qg", a, b))
-
-    def sizes(q):
         act(C("a%d" % q), pb(4 + q, 1), Act.Abs, TINY)
         act(blk(q), pb(q), Act.Abs, TINY)
-
-    def limit(q):
-        act(R("t0", 128 * q, 128 * q + 128), R("f0"), Act.Copy, 0.0, C("a%d" % q))
-
-    def sg(q):
-        return R("sg", 256 * (q - 1), 256 * (q - 1) + 128 * min(q, 2))
-
-    def signs(q):
-        act(sg(q), blk(0, min(q, 2)), Act.Sign, C("a%d" % q), -1.0)
-
-    def count(q):
-        act(sg(q), sg(q), Act.Sign, 1.0, -1.0, acc=C("s%d" % q))
-
-    def cc(q, j):
-        a = 128 * j if q == 0 else 400 * q + 8 + 128 * abs(j - q)
-        return R("cc", a, a + 128) if (q, j) != (0, 3) else R("r0")
-
-    def diag(q):
-        tt(cc(q, q), blk(q), R("t0", 128 * q, 128 * q + 128), Op.is_gt)
-
-    def side(q, j):
-        ts(cc(q, j), blk(j), C("a%d" % q), Op.is_gt if j > q else Op.is_ge)
-
-    def place(q):
-        n, a = 64 * max(4 - q, 2) + 1, 400 * q + 7
-        scan(R("rs", 200 * q + 200 - n, 200 * q + 200), R("cc", a, a + n), R("cc", a + n, a + 2 * n), Op.add, Op.add, C("s%d" % q))
-
-    def high(q):
-        n, a = 64 * max(4 - q, 2) + 2, 400 * q + 6
-        scan(R("rh", 200 * q + 200 - n, 200 * q + 200), R("cc", a, a + n), R("cc", a + n, a + 2 * n), Op.add, Op.add, C("s%d" % q))
-
-    def onehot(q):
-        r = R("rs", 200 * q + 199, 200 * q + 200)
-        if CFG["dual0"] and q:
-            high(q)
-            h = R("rh", 200 * q + 199, 200 * q + 200)
-            ts(R("ey", q, 64, 4), R("c32", 0, 16), TOP, Op.add, h, Op.is_equal)
-            ts(R("wy", 64 + q, 576, 4), R("jf"), h, Op.add, r, Op.is_equal)
-        else:
-            h = R("hq", q, q + 1)
-            snap(h, r)
-            if CFG["fuse0"]:
-                for k in range(2):
-                    ts(R("wy", 32 * k + q, 32 * k + 32, 4), R("c32", 0, 8), h, Op.is_equal, R("d0", 32 * k + q, 32 * k + q + 1), Op.mult)
+        line(R("t0", a, b), R("f0"), C("a%d" % q), 0.0)
+    for q in range(4):
+        n, size = PLAN["signs"][q], C("a%d" % q)
+        if n:
+            sg = R("sg", 384 * q, 384 * q + 128 * n)
+            act(sg, blk(0, n), Act.Sign, size, -1.0)
+            act(sg, sg, Act.Sign, 1.0, -1.0, acc=C("s%d" % q))
+        for j in range(n, 4):
+            a = 520 * q + 1 + 128 * (j - n)
+            if j == q:
+                tt(R("cc", a, a + 128), blk(q), R("t0", 128 * q, 128 * q + 128), Op.is_gt)
             else:
-                ts(R("ey", q, 64, 4), R("c32", 0, 16), h, Op.is_equal)
-            ts(R("wy", 64 + q, 576, 4), R("jm"), h, Op.add, r, Op.is_equal)
-
-    for q in range(4):
-        pack(q), sizes(q), limit(q), diag(q)
-    for q in range(1, 4):
-        signs(q), count(q)
-    for q, j in ((0, 1), (0, 2), (1, 2), (3, 2), (0, 3), (1, 3), (2, 3)):
-        side(q, j)
-    dma("s", ap(R("wt")), T.w[:, 0:512], [R("wt")], [R("grt", 1536, 2048)])
-    scan(R("r1"), cc(0, 0), cc(0, 1), Op.add, Op.add, -HALF)
-    scan(R("rs", 72, 200), cc(0, 2), cc(0, 3), Op.add, Op.add, R("r1", 127, 128))
-    for q in range(4):
-        if q:
-            place(q)
-        onehot(q)
-    ts(R("m8"), R("c32", 0, 8), C("ph"), Op.is_equal)
-    if not CFG["fuse0"]:
-        tt(R("wy", 0, 64), R("ey"), R("d0"), Op.mult)
+                ts(R("cc", a, a + 128), blk(j), size, Op.is_gt if j > q else Op.is_ge)
+        m, a = 64 * (4 - n) + 1, 520 * q
+        fill(R("cc", a + 2 * m - 1, a + 2 * m), 0.0)
+        scan(R("rs", 260 * q + 260 - m, 260 * q + 260), R("cc", a, a + m), R("cc", a + m, a + 2 * m), C("s%d" % q) if n else 0.0)
+        r, h = R("rs", 260 * q + 259, 260 * q + 260), R("hq", q, q + 1)
+        snap(h, r)
+        for k in range(2):
+            ts(R("wy", 32 * k + q, 32 * k + 32, 4), c8, h, Op.is_equal, R("d0", 4 * k + q, 4 * k + q + 1), Op.mult)
+        ts(R("wy", 64 + q, 576, 4), R("jm"), h, Op.add, r, Op.is_equal)
     quant(R("qwy"), R("wy"))
-    node("p", lambda: g.wait_ge(T.sem["ready"], nready), [], [], 1, 0)
-    send_codes(0, R("nl", 0, 32), R("qwy", 0, 32), "an0", CFG["num"][0])
+    gate.append(node("p", lambda: g.wait_ge(T.sem["ready"], nready), [], [], [told]))
+    send_codes(0, R("nl", 0, 32), R("qwy", 0, 32), "an0")
     mm(pb(2), WY, R("qwy", 0, 128), True, False)
     mm(pb(2), WY, R("qwy", 8, 136), False, True)
     lw = R("lw0", 0, 8)
@@ -437,52 +340,53 @@ def rank_program(g, core, T, topo):
     send_set(0)
     mine, wrapped = lw, pb(2, 8)
 
+    fill(R("cwt"), 0.0)
+    fill(R("wv", 1, 512, 2), 0.0)
+    fill(R("wv", 64, 512, 2), 0.0)
+    fill(Y(1), 1.0)
+    fill(Y(3), 0.0)
+    fill(R("wx", 1, 576, 2), 0.0)
+    fill(R("wz", 1, 768, 2), 0.0)
+    line(C("pd"), C("ph"), 1.0, -256.0, "v")
+    line(C("pc"), C("ph"), 1.0, -128.0, "v")
+    copy(R("dv", 0, 1), C("pl"))
+    fill(R("cwt", 0, 512, 4), -1.0 / ULP)
+    fill(R("cwt", 1, 512, 4), 2.0 ** -7 / ULP)
+    fill(R("cwt", 512, 513), 256.0)
+    line(R("cwt", 513, 514), R("tri", 0, 1), HALF, 1.0 - HALF)
+    fill(R("cwt", 514, 515), 1.0)
+    fill(R("cwt", 515, 517), -1.0)
+    fill(R("cwt", 517, 518), 2.0 ** -7)
+    quant(R("cw"), R("cwt"))
+    fill(R("ta1"), NONE)
+    fill(R("ta2"), NONE)
+    ts(R("idn"), R("i128"), C("p"), Op.is_equal)
+    quant(R("qw"), R("wt"))
+    fill(R("tk"), 0.0)
+    fill(R("nlt", 1, 512, 4), 0.0)
+    fill(R("nlt", 512, 1024, 4), 0.0)
+    line(R("nlt", 0, 512, 4), R("idn"), -240.0, 0.0)
+    line(R("nlt", 513, 1024, 4), R("idn"), -240.0, 0.0)
+
     nac, nbc, umc, thr, ha, hb = [C(x) for x in ("nac", "nbc", "umc", "thr", "ha", "hb")]
     for b in range(L):
         w, nw, ta, nb, apn = ["%s%d" % (x, b) for x in ("w", "nw", "ta", "nb", "ap")]
         last = b == L - 1
         own, far, mrg = R(w, A0, B0), R(w, B0, W1), R(w, M0, A0)
         nar, nbr = R(nw, A0, B0), R(nw, B0, W1)
+        slot = ((C("pl"), C("pc")), (C("pl"), C("sbh")) if last else (R("dv", 0, 1), R("dv", 1, 2)))
+        number = ((C("la"), C("nahi")), (R("dv", 2, 3), R("dv", 3, 4)))
         tt(R("x8", 0, 8), wrapped, R("m8"), Op.mult)
         scatter(R(ta), mine, R("i128"))
         rsum(nac, R("x8", 0, 8))
-        gather(nar, R("iN"), mine, "a")
+        copy(nar, R("iN"), "a", mine)
         mm(pb(4), UB, own)
         act(R("absa"), pb(4), Act.Abs, TINY * ULP, ULP)
         if not last:
-            fill(R("ta%d" % (b + 1)), NONE, "a")
-        if b == 0:
-            fill(R("snap"), SNAP)
-            fill(R("neg"), 256.0)
-            fill(Y(1), 1.0)
-            fill(Y(3), 0.0)
-            fill(R("wx", 1, 640, 2), 0.0)
-            fill(R("wz", 1, 768, 2), 0.0)
-            ts(C("pb"), C("ph"), 256.0, Op.subtract)
-            ts(C("pc"), C("ph"), 128.0, Op.subtract)
-            fill(R("cwt", 0, 512, 4), -1.0 / ULP)
-            fill(R("cwt", 1, 512, 4), 2.0 ** -7 / ULP)
-            fill(R("cwt", 512, 513), 256.0)
-            ts(R("cwt", 513, 514), R("tri", 0, 1), HALF, Op.mult, 1.0 - HALF, Op.add)
-            fill(R("cwt", 514, 515), 1.0)
-            fill(R("cwt", 515, 517), -1.0)
-            fill(R("cwt", 517, 518), 2.0 ** -7)
-            quant(R("cw"), R("cwt"))
-            act(D(0, 0), o8, Act.Copy, 0.0, C("pl"))
-            act(D(1, 0), o8, Act.Copy, 0.0, C("pl"))
-            act(D(0, 2), o8, Act.Copy, 0.0, C("pc"))
-        act(C("nah"), nac, Act.Identity, -HALF)
-        ts(D(0, 3), R("snap"), C("nah"), Op.add, SNAP, Op.subtract)
-        act(D(0, 1), D(0, 3), Act.Identity, nac, -1.0)
-        if b == 1:
-            ts(R("idn"), R("i128"), C("p"), Op.is_equal)
-            quant(R("qw"), R("wt"))
-            fill(R("tk"), 0.0)
-            fill(R("nlt", 1, 512, 4), 0.0)
-            fill(R("nlt", 512, 1024, 4), 0.0)
-        if last:
-            act(R("nlt", 0, 512, 4), R("idn"), Act.Copy, 0.0, -240.0)
-            act(R("nlt", 513, 1024, 4), R("idn"), Act.Copy, 0.0, -240.0)
+            line(C("nah"), nac, 1.0, -HALF)
+            snap(number[0][1], C("nah"))
+            line(number[0][0], number[0][1], -1.0, nac)
+        else:
             ts(R("nlt", 2, 512, 4), nar, nac, Op.is_gt)
         if b == 0:
             pick(R("nx"), R("nl"), R("lc"))
@@ -493,33 +397,41 @@ def rank_program(g, core, T, topo):
             rsum(nbc, R("x8", 8, 16))
         else:
             tt(R("xp"), R("iN"), R("idn"), Op.mult, R(nb))
-            act(R("xj"), R("xp"), Act.Copy, acc=nbc)
+            if scalar("a"):
+                act(R("xj"), R("xp"), Act.Copy, acc=nbc)
+            else:
+                rsum(nbc, R("xp"))
         pick(R(apn), R("wn%d" % b if b else "qg"), R(nb))
-        act(R("mk"), R(ta), Act.Sign, NONE, -1.0, off=R(nb))
-        gather(nbr, R("iN"), R(nb), "a")
+        if scalar("a"):
+            act(R("mk"), R(ta), Act.Sign, NONE, -1.0, off=R(nb))
+        else:
+            ts(R("mk"), R(ta), NONE, Op.is_lt, off=R(nb))
+        copy(nbr, R("iN"), "a", R(nb))
         for first in (True, False):
             for t in range(4):
-                mm(pb(t), E(t), R(apn) if first == bool(CFG["own_first"][b]) else far, first, not first)
+                mm(pb(t), E(t), R(apn) if first == bool(PLAN["own_first"][b]) else far, first, not first)
         ts(Y(0), nar, nbc, Op.is_equal)
         ts(Y(2), nar, nbc, Op.is_gt, -1.0, Op.mult)
-        act(C("nbh"), nbc, Act.Identity, -HALF)
-        ts(D(1, 3), R("snap"), C("nbh"), Op.add, SNAP, Op.subtract)
+        if not last:
+            line(C("nbh"), nbc, 1.0, -HALF)
+            snap(number[1][1], C("nbh"))
+            line(number[1][0], number[1][1], -1.0, nbc)
         quant(R("qe"), R("ye"))
         if last:
             ts(R("nlt", 514, 1024, 4), nbr, nac, Op.is_gt)
             ts(R("nlt", 3, 1024, 4), R(nw, A0, W1), nbc, Op.is_gt)
+            quant(R("qlt", 0, 128), R("nlt", 0, 512))
+            quant(R("qlt", 128, 256), R("nlt", 512, 1024))
+            copy(R(nw, M0, A0), nbr)
         mm(pb(6), UB, far)
         mm(pb(7), far, UB)
         mm(pb(4), WU, R("qe"), True, False)
         mm(pb(4), E(2), R("qe"), False, True)
         mm(pb(5), R("qe"), WR)
-        act(R("um"), R("mk"), Act.Identity, 1.0, -1.0)
+        line(R("um"), R("mk"), -1.0, 1.0)
         act(R("yj"), Y(0), Act.Identity, 2.0 ** -7, -1.0, acc=umc)
-        act(D(1, 1), D(1, 3), Act.Identity, nbc, -1.0)
-        act(C("sbt"), pb(7, 1), Act.Identity, TINY, umc)
-        act(D(1, 2), R("neg"), Act.Identity, C("pb"), umc)
-        if last:
-            copy(R(nw, M0, A0), nbr, "a")
+        line(C("sbt"), pb(7, 1), umc, TINY)
+        line(slot[1][1], umc, 256.0, C("pd"))
         for t in range(4):
             tt(R("hm", t, 512, 4), pb(t), R("mk"), Op.mult)
         tt(R("sbs"), pb(6), R("um"), Op.mult)
@@ -528,48 +440,43 @@ def rank_program(g, core, T, topo):
         ts(R("fb"), nbr, nbc, Op.is_ge, 1.0 - ULP, Op.max)
         ts(Y(2), R("i128"), C("p"), Op.is_gt, pb(5, 128, 127), Op.mult)
         if not last:
-            act(C("la"), one(D(0, 3)), Act.Identity, nac, -1.0)
-            ts(R("wz", 256, 768, 4), R("jq"), C("la"), Op.is_equal, pb(5, 128, 127), Op.mult)
-            ts(R("wz", 258, 768, 4), R("jq"), one(D(1, 1)), Op.is_equal)
+            ts(R("wz", 256, 768, 4), R("jq"), number[0][0], Op.is_equal, pb(5, 128, 127), Op.mult)
+            ts(R("wz", 258, 768, 4), R("jq"), number[1][0], Op.is_equal)
             for sd in range(2):
                 for k in range(2):
-                    ts(R("wz", 128 * k + 2 * sd, 128 * k + 128, 4), R("iN", 0, 512, 16), one(D(sd, 3)), Op.is_equal, one(D(sd, 2 * k)), Op.mult)
+                    ts(R("wz", 128 * k + 2 * sd, 128 * k + 128, 4), R("iN", 0, 512, 16), number[sd][1], Op.is_equal, slot[sd][k], Op.mult)
             quant(R("qwz"), R("wz"))
             mm(pb(3), R("qwz", 64, 192), R("qwz", 0, 128), True, False)
             mm(pb(3), R("qwz", 64, 192), R("qwz", 32, 160), False, True)
             ts(R("lz"), pb(3, 32), 256.0, Op.add)
-            for k in range(4):
-                pick(R("wn%d" % (b + 1), 128 * k, 128 * k + 128), R(w), R("lz", 8 * k, 8 * k + 8))
+            n = 32 // PLAN["chunks"]
+            for k in range(PLAN["chunks"]):
+                pick(R("wn%d" % (b + 1), 16 * n * k, 16 * n * (k + 1)), R(w), R("lz", n * k, n * k + n))
         mm(pb(1), mrg, UB)
         mm(pb(0), UB, mrg)
         if last:
             mm(pb(3, W1), R("qw"), R(w))
+            copy(R("yw"), pb(3, W1))
         act(thr, pb(1, 1), Act.Abs, C("sbt"))
         tt(R("xb"), pb(0), R("sbs"), Op.add)
-        act(R("tb"), R("fb"), Act.Copy, 0.0, thr)
+        line(R("tb"), R("fb"), thr, 0.0)
         ts(Y(3), R("za"), thr, Op.is_ge)
         act(R("rowb"), R("xb"), Act.Abs, TINY)
-        if last:
-            quant(R("qlt", 0, 128), R("nlt", 0, 512))
-            quant(R("qlt", 128, 256), R("nlt", 512, 1024))
         quant(R("ql"), R("ye"))
-        mm(pb(5), R("ql"), WR)
+        bank = 5 if last else 7
+        mm(pb(bank), R("ql"), WR)
         tt(R("cb"), R("rowb"), R("tb"), Op.is_gt)
-        ra, rb, rh = pb(5, 127, 126), R("rk", 127, 128), R("rk", 255, 256)
-        ea, eb = R("ex", 0, 32), R("ex", 32, 64)
+        ra, rb, rh = pb(bank, 127, 126), R("rk", 127, 128), R("rk", 255, 256)
 
-        def cols(e, h):
-            ts(e, R("c32"), h, Op.is_equal)
+        def digits(tile, sd, cs, h, of):
+            for k in range(2):
+                ts(R(tile, 32 * k + 2 * sd, 32 * k + 32, 4), cs, h, Op.is_equal, of[sd][k], Op.mult)
 
-        def rows(t, h, r):
-            ts(R("wx", 128 + t, 640, 4), R("jm"), h, Op.add, r, Op.is_equal)
+        def rows(sd, jm, h, r):
+            ts(R("wx", 64 + 2 * sd, 576, 4), jm, h, Op.add, r, Op.is_equal)
 
-        def digits(sd, e):
-            tt(R("wx", 2 * sd, 128, 4), e, R("dv", 32 * sd, 32 * sd + 32), Op.mult)
-
-        scan(R("rk", 0, 128), Y(3), R("cb"), Op.add, Op.add, -HALF)
+        scan(R("rk", 0, 128), Y(3), R("cb"), -HALF)
         if last:
-            copy(R("yw"), pb(3, W1), "a")
             ts(R("tk", 8, 9), ra, 128.0 - 8, Op.is_lt, 31.0 / 32, Op.subtract)
             ts(R("tk", 10, 11), ra, 128.0 - 8, Op.is_lt)
             ts(R("tk", 9, 10), rb, 128.0 - 8, Op.is_lt, 31.0 / 32, Op.subtract)
@@ -578,40 +485,43 @@ def rank_program(g, core, T, topo):
             mm(pb(6), R("qlt", 0, 128), R("qtk", 2, 130))
             mm(pb(7), R("qlt", 128, 256), R("qtk", 2, 130))
             ra, rb = pb(6, 1), pb(7, 1)
-            snap(ha, ra), cols(ea, ha), snap(hb, rb), rows(0, ha, ra), digits(0, ea), cols(eb, hb), rows(2, hb, rb), digits(1, eb)
+            snap(ha, ra), snap(hb, rb), rows(0, R("jm"), ha, ra), rows(1, R("jm"), hb, rb)
+            digits("wx", 0, c8, ha, slot), digits("wx", 1, c8, hb, slot)
         else:
             snap(ha, ra)
-            scan(R("rk", 128, 256), Y(3), R("cb"), Op.add, Op.add, TOP - HALF)
-            cols(ea, ha), rows(0, ha, ra), digits(0, ea)
-            ts(eb, R("c32"), TOP, Op.add, rh, Op.is_equal)
-            ts(R("wx", 130, 640, 4), R("jf"), rh, Op.add, rb, Op.is_equal)
-            digits(1, eb)
+            scan(R("rk", 128, 256), Y(3), R("cb"), TOP - HALF)
+            rows(0, R("jm"), ha, ra), rows(1, R("jf"), rh, rb)
+            for tile, of in (("wx", slot), ("wv", number)):
+                digits(tile, 0, c8, ha, of), digits(tile, 1, R("ct"), rh, of)
         quant(R("qwx"), R("wx"))
         mm(pb(2), WX, R("qwx", 0, 128), True, False)
-        mm(pb(2), WX, R("qwx", 16, 144), False, True)
+        mm(pb(2), WX, R("qwx", 8, 136), False, True)
         ln = "lw%d" % (b + 1)
-        ts(R(ln), pb(2, 16), 256.0, Op.add)
-        lw, mine, wrapped = R(ln, 0, 8), R(ln, 8, 16), pb(2, 16, 8)
+        lw, mine, wrapped = R(ln, 0, 8), R(ln, 8, 16), pb(6, 8)
+        ts(lw, pb(2, 8), 256.0, Op.add)
         if not last:
+            quant(R("qwv", 0, 128), R("wv"))
+            mm(pb(6), WX, R("qwv", 0, 128), True, False)
+            mm(pb(6), WX, R("qwv", 8, 136), False, True)
+            ts(mine, wrapped, 256.0, Op.add)
             pick(R("w%d" % (b + 1), A0, B0), R(w), lw)
-            arrive("an%d" % (b + 1), [R("nb%d" % (b + 1))], [send(b + 1, R("nb%d" % (b + 1)), mine, "an%d" % (b + 1), CFG["num"][b + 1], True)])
+            arrive("an%d" % (b + 1), [R("nb%d" % (b + 1))], [send(b + 1, R("nb%d" % (b + 1)), mine, "an%d" % (b + 1), True)])
             send_set(b + 1)
         else:
             pick(R("w3"), R(w), lw)
-            dma("s", T.oc[:, 0:512], ap(R("w3")).bitcast(dt.uint8), [], [R("w3")])
-            gather(R("yo"), R("yw"), lw)
-            act(R("nbo"), R(nw), Act.Identity, 256.0, off=lw)
+            dma("a" if scalar("s") else "s", T.oc[:, 0:512], ap(R("w3")).bitcast(dt.uint8), [], [R("w3")])
+            copy(R("yo"), R("yw"), "v", lw)
+            if scalar("a"):
+                act(R("nbo"), R(nw), Act.Identity, 256.0, off=lw)
+            else:
+                ts(R("nbo"), R(nw), 256.0, Op.add, off=lw)
+            for k in range(4):
+                dma("a" if scalar("a") else "s", T.osc[4 * k:4 * k + 4, 0:128], T["w3s"][32 * k:32 * k + 4, 0:128], [], [R("w3s")])
+            dma("a" if scalar("s") else "s", T.y[:, 0:128], ap(R("yo")), [], [R("yo")])
+            dma("a" if scalar("a") else "s", T.nb[0:1, 0:128], T.nbo[0:1, 0:128], [], [R("nbo")])
 
-            def scales(e, k):
-                dma(e, T.osc[4 * k:4 * k + 4, 0:128], T["w3s"][32 * k:32 * k + 4, 0:128], [], [R("w3s")])
-
-            scales("s", 0), scales("s", 1)
-            dma("s", T.y[:, 0:128], ap(R("yo")), [], [R("yo")])
-            scales("a", 2), scales("a", 3)
-            dma("a", T.nb[0:1, 0:128], T.nbo[0:1, 0:128], [], [R("nbo")])
-    if str(CFG) not in ORDER:
-        ORDER[str(CFG)] = order()
-    for k in ORDER[str(CFG)]:
+    PLAN.get("hook", lambda *a: 0)(nodes, either, Q, meet)
+    for k in order or range(len(nodes)):
         nodes[k][1]()
-    for s in sorted(total):
+    for s in sorted(total, key=lambda s: (s == "out", s)):
         g.wait_ge(T.sem[s], total[s])

from concourse.bass import DstId, RemoteDMATransfer
from concourse.mybir import dt, AluOpType as Op, AxisListType, ActivationFunctionType as Act

K, P, L = 128, 512, 3
M0, A0, B0, W1 = 0, 128, 256, 384
TINY = 2.0 ** -100
ULP = 2.0 ** -24
NONE = 255.0
SNAP = 1.5 * 2.0 ** 27
HALF = 7.5
TOP = 3072.0

PLAN = dict(ORDER=r"000102030409061K078=8<0@0>0G0:0B0P0U8E080V0X0C8W0H0Z0;0Y0[0\960`8F0a8A9U0b8J1h0f9A8O0N0]0?0^050h0_0c0l0g0e0m0d0j120i131<1>0o0n101\0k1?1=1S1G1@1J14151Q1B1I17911C1T181H1L1E1D1F1R:6:31V1M:81:19:41W9m1O1N1P1;1Z1X1Y9n2<221[0Q0S:1:70M1`0R1]1a1^:5:@8D1b292C1c9l2E1_1e2L9d8K2G:M2N2D:I2O:F2H:01f1g2W2X9k2P2Q2J0T2R2S2Z2_:T2`392Y:U0L2]2d2\2^2[9o302i2o:V2k312n:a:j8I2f35332e2b:l2g:m2h3E:c323F3G36343::K3H3J3I3<3L3K3M9j::3N9i38373Q3O3P3W3S3V3T3R3U3[3Y3X3Z3\3;:A3`3]3^2=3a3=3b3_3c3>3k3?;e3d3o3@;n3l;D3f3C3A3g3h4446;B3i3m<74=4;4<<5<83j4:2;404B4?4C4>4A4@41<94N4G4R<M4J4Q4T4S4X4I4L424H4V4U4K<D<O4h4]<34E4j4W4i4Y4k4m4l4^<F4o4Z4n51504\<P534[52545758555:59:>565=5;5<5>5?4_5C5@4`5A5D5E5B5F4a=H4b5G4c5O=Q5R4d5I5J<g<e4f=X5K5L5U=V5M5W5^5N5[5\5Z5d5]5`=Y5c5e5S5a>05b5_5m5l655n665k6764:?615P6;>25o69685T6=5j6A6>6:6<6B6D6C5f6?6F6E6H5g6I:B6G6J6K6L6M5h6N6O5i6P6Q>3>@6R6V6S6U6T6X6W6Y6Z6[6\>^6]6_>a6b6`6c>d>e>f>g",
            signs=(0, 1, 2, 2), chunks=2, own_first=(0, 1, 1), loads=((0, 512), (512, 1024), (1024, 1536), (1536, 2048)))
SCRATCH = {}


def _buf(name, cols, dtype, where="sbuf"):
    SCRATCH[name] = (where, [128, cols], dtype)


def _codes(name, cols):
    _buf(name, cols, "float8_e4m3fn_x4")
    _buf(name + "s", cols, "uint8")


for _n, _c in (("ones", 544), ("tri", 128), ("jq", 128), ("jm", 128), ("i128", 128), ("ct", 8), ("hq", 4), ("d0", 8), ("iN", 512), ("m8", 8),
               ("u4", 4), ("ut", 512), ("grt", 2048), ("wt", 512), ("cwt", 520), ("et", 520), ("wy", 576), ("wx", 576), ("wv", 512), ("wz", 768),
               ("dv", 4), ("tk", 520), ("nlt", 1024), ("sg", 1536), ("cc", 2080), ("rs", 1040), ("ye", 512), ("yj", 128), ("xp", 128),
               ("xj", 128), ("x8", 16), ("mk", 128), ("um", 128), ("hm", 512), ("cb", 128), ("idn", 128), ("rk", 256),
               ("nw0", W1), ("nw1", W1), ("nw2", W1), ("ta0", 512), ("ta1", 512), ("ta2", 512)):
    _buf(_n, _c, "bfloat16")
for _n, _c in (("f0", 128), ("t0", 512), ("ar", 512), ("small", 64), ("absa", 128), ("za", 128), ("sbs", 128), ("xb", 128),
               ("rowb", 128), ("fb", 128), ("tb", 128), ("nbo", 128), ("yw", W1), ("yo", 128), ("jf", 128)):
    _buf(_n, _c, "float32")
for _n, _c in (("lw0", 16), ("lw1", 16), ("lw2", 16), ("lw3", 16), ("nb0", 8), ("nb1", 8), ("nb2", 8), ("lc", 8), ("lz", 32)):
    _buf(_n, _c, "uint16")
for _n, _c in (("cu", 128), ("qg", 512), ("qw", 128), ("cw", 130), ("ce", 512), ("nx", 128), ("nl", 136), ("qwz", 192), ("wn1", 512), ("wn2", 512),
               ("qwy", 144), ("qwx", 144), ("qwv", 136), ("qe", 128), ("ql", 128), ("qtk", 130), ("qlt", 256),
               ("w0", W1), ("w1", W1), ("w2", W1), ("w3", 128), ("ap0", 128), ("ap1", 128), ("ap2", 128)):
    _codes(_n, _c)
SMALL = {}
for _i, _n in enumerate(("p", "ph", "pl", "pb", "pc", "pd", "a0", "a1", "a2", "a3", "s1", "s2", "s3", "sbt", "thr", "nac", "nbc",
                         "umc", "ha", "hb", "la", "nah", "nbh", "nahi", "sbh")):
    SMALL[_n] = 2 * _i
for _i in range(8):
    _buf("p%d" % _i, 512, "float32", "psum")
SEMAPHORES = ["sv", "sa", "st", "sp", "sent", "ac0", "ac1", "ac2", "an0", "an1", "an2", "ready", "out"] + ["d%d" % i for i in range(6)]


def rank_program(g, core, T, topo):
    rank = T.rank_of(core)
    if rank is None:
        return
    Q = {"v": g.vector, "a": g.scalar, "t": g.tensor, "p": g, "s": g.sync}
    ESEM = {"v": "sv", "a": "sa", "t": "st", "p": "sp"}
    total, known, hist, recs = {}, {e: {} for e in Q}, {}, {}

    def meet(x, y):
        if x[1] >= y[2] or y[1] >= x[2]:
            return False
        return x[3] == y[3] == 1 or not set(range(*x[1:])).isdisjoint(range(*y[1:]))

    def waits(e, outs, ins):
        need = {}
        for regs, isw in ((ins, False), (outs, True)):
            for r in regs:
                ps = SCRATCH[r[0]][0] == "psum"
                for q, w, s, c, e2 in recs.get(r[0], []):
                    if ps:
                        if e2 == e and (e == "t" or not (w or isw)):
                            continue
                    elif not (w or isw) or not meet(r, q):
                        continue
                    need[s] = max(need.get(s, 0), c)
        for s in sorted(need):
            c = need[s]
            if known[e].get(s, 0) < c:
                Q[e].wait_ge(T.sem[s], c)
                known[e][s] = c
                for s2, c2 in hist.get((s, c), {}).items():
                    if known[e].get(s2, 0) < c2:
                        known[e][s2] = c2

    def note(s, c, e, outs, ins):
        for regs, w in ((ins, False), (outs, True)):
            for r in regs:
                recs.setdefault(r[0], []).append((r, w, s, c, e))

    nodes, either = [], []
    code = [64 * (ord(x) - 48) + ord(y) - 48 for x, y in zip((PLAN["ORDER"] or "")[::2], (PLAN["ORDER"] or "")[1::2])]
    order, marked = [k % 512 for k in code], {k % 512 for k in code if k >= 512}

    def node(e, run, outs, ins, after=()):
        nodes.append((e, run, outs, ins, list(after)))
        return len(nodes) - 1

    def op(e, call, outs, ins):
        def run():
            waits(e, outs, ins)
            s = ESEM[e]
            total[s] = total.get(s, 0) + 1
            call(Q[e]).then_inc(T.sem[s], 1)
            hist[(s, total[s])] = dict(known[e])
            hist[(s, total[s])][s] = total[s]
            note(s, total[s], e, outs, ins)
        node(e, run, outs, ins)

    nd = [0]

    def dma(e, out, in_, outs, ins, after=()):
        def run():
            waits(e, outs, ins)
            s = "d%d" % nd[0] if outs else "out"
            nd[0] += 1
            total[s] = total.get(s, 0) + 16
            Q[e].dma_start(out, in_).then_inc(T.sem[s], 16)
            if outs:
                hist[(s, 16)] = dict(known[e])
                note(s, 16, "dma", outs, ins)
        return node(e, run, outs, ins, after)

    def scalar(e):
        either.append(len(nodes))
        if PLAN.get("SIDE"):
            return PLAN["SIDE"][len(either) - 1] == "a"
        return len(nodes) in marked if code else e == "a"

    def R(n, a=0, b=None, st=1):
        return (n, a, SCRATCH[n][1][1] if b is None else b, st)

    def C(n):
        return ("small", SMALL[n], SMALL[n] + 1, 1)

    def ap(r):
        if r[3] == 1:
            return T[r[0]][:, r[1]:r[2]]
        return T[r[0]][:, r[1]:r[2]:r[3]]

    def S(r):
        return (r[0] + "s",) + r[1:]

    def isr(x):
        return isinstance(x, tuple)

    def sap(x):
        return ap(x) if isr(x) else x

    def by(win, off):
        return ap(win) if off is None else ap(win).indirect(ap(off))

    def act(o, i, f, bias=0.0, scale=1.0, acc=None, off=None):
        ins = [i] + [x for x in (bias, scale, off) if isr(x)]
        if acc is None:
            op("a", lambda q: q.activation(ap(o), by(i, off), f, bias=sap(bias), scale=sap(scale)), [o], ins)
        else:
            op("a", lambda q: q.activation(ap(o), ap(i), f, bias=sap(bias), scale=sap(scale), accum_out=ap(acc)), [o, acc], ins)

    def tt(o, a, b, f, off=None):
        op("v", lambda q: q.tensor_tensor(ap(o), by(a, off), ap(b), f), [o], [a, b] + ([off] if off else []))

    def ts(o, i, s1, f1, s2=None, f2=None, off=None):
        ins = [i] + [x for x in (s1, s2, off) if isr(x)]
        if f2 is None:
            op("v", lambda q: q.tensor_scalar(ap(o), by(i, off), sap(s1), None, f1), [o], ins)
        else:
            op("v", lambda q: q.tensor_scalar(ap(o), by(i, off), sap(s1), sap(s2), f1, f2), [o], ins)

    def scan(o, a, b, first):
        op("v", lambda q: q.tensor_tensor_scan(ap(o), ap(a), ap(b), sap(first), Op.add, Op.add), [o], [a, b] + ([first] if isr(first) else []))

    def rsum(o, i):
        op("v", lambda q: q.tensor_reduce(ap(o), ap(i), AxisListType.X, Op.add), [o], [i])

    def iota(o, pat, cm):
        op("p", lambda q: q.iota(ap(o), pat, 0, cm, allow_small_or_imprecise_dtypes=True), [o], [])

    def memset(r, c):
        op("v", lambda q: q.memset(ap(r), c), [r], [])

    def fill(r, c, e="v"):
        if scalar(e):
            act(r, R("ones", 0, len(range(*r[1:]))), Act.Copy, 0.0, c)
        else:
            memset(r, c)

    def line(o, i, mul, add, e="a"):
        if scalar(e):
            act(o, i, Act.Identity, add, mul)
        else:
            ts(o, i, mul, Op.mult, add, Op.add)

    def copy(o, i, e="a", off=None):
        if scalar(e):
            op("a", lambda q: q.activation(ap(o), by(i, off), Act.Copy), [o], [i] + ([off] if off else []))
        else:
            op("v", lambda q: q.tensor_copy(ap(o), by(i, off)), [o], [i] + ([off] if off else []))

    def scatter(win, off, i):
        op("v", lambda q: q.tensor_copy(ap(win).indirect(ap(off)), ap(i)), [win], [off, i])

    def pick(o, win, off):
        op("v", lambda q: q.tensor_copy(ap(o).bitcast(dt.uint32), ap(win).bitcast(dt.uint32).indirect(ap(off))), [o], [win, off])
        copy(S(o), S(win), "a", off)

    def quant(o, i):
        op("v", lambda q: q.quantize_mx(ap(o), ap(S(o)), ap(i)), [o, S(o)], [i])

    def mm(o, a, b, start=True, stop=True):
        op("t", lambda q: q.matmul_mx(ap(o), ap(a), ap(S(a)), ap(b), ap(S(b)), start, stop), [o], [a, S(a), b, S(b)])

    def snap(o, i):
        ts(o, i, SNAP, Op.add, SNAP, Op.subtract)

    partner = [T.cores[rank ^ (1 << b)] for b in range(L)]

    def route(b):
        rid, pid, _se = topo.addr(partner[b])
        e = topo.engines(core, partner[b])
        return pid, rid, sum(1 << x for x in e), len(e)

    def sent(sem, n):
        total["sent"] = total.get("sent", 0) + n
        total[sem] = total.get(sem, 0) + n

    gate = []

    def send(b, o, i, sem, raw=False):
        def run():
            waits("p", [], [i])
            pid, rid, mask, n = route(b)
            x, y = (ap(o), ap(i)) if raw else (ap(o).bitcast(dt.uint8), ap(i).bitcast(dt.uint8))
            g.remote_dma(x, y, T.sem[sem], T.sem["sent"], pid, rid, mask)
            sent(sem, n)
        return node("p", run, [], [i], gate)

    def arrive(sem, outs, after):
        node("x", lambda: note(sem, total[sem], "far", outs, []), outs, [], after)

    def send_codes(b, o, i, sem):
        arrive(sem, [o, S(o)], [send(b, o, i, sem), send(b, S(o), S(i), sem, True)])

    def send_set(b):
        send_codes(b, R("w%d" % b, B0, W1), R("w%d" % b, A0, B0), "ac%d" % b)

    UB, WU, WR, WY, WX = R("cu"), R("cw", 0, 128), R("cw", 2, 130), R("qwy", 16, 144), R("qwx", 16, 144)

    def E(t):
        return R("ce", 128 * t, 128 * t + 128)

    def pb(i, n=128, a=0):
        return R("p%d" % i, a, n)

    def Y(t):
        return R("ye", t, 512, 4)

    k = dma("a", ap(R("u4")), T.u[:, 0:4], [R("u4")], [])
    for q, (a, b) in enumerate(PLAN["loads"]):
        k = dma("a" if q % 2 else "s", ap(R("grt", a, b)), T.gr[:, a:b], [R("grt", a, b)], [], [k])
    dma("s", ap(R("wt")), T.w[:, 0:512], [R("wt")], [R("grt", 1536, 2048)])

    o128, o8, c8 = R("ones", 0, 128), R("ones", 0, 8), R("i128", 0, 128, 16)
    iota(C("p"), [[1, 1]], 1)
    iota(R("i128"), [[1, 128]], 0)
    iota(R("jq"), [[0, 8], [1, 16]], 0)
    memset(R("ones"), 1.0)
    quant(R("nl"), R("ones"))
    pid, rid, mask, nready = route(0)

    def ready():
        waits("p", [R("nl"), R("nls")], [])
        g.remote_sem_update(T.sem["ready"], T.sem["sent"], pid, rid, mask)
        sent("ready", nready)

    told = node("p", ready, [R("nl"), R("nls")], [])
    fill(R("et"), 0.0)
    line(C("pb"), C("p"), 1.0, -HALF, "v")
    ts(R("tri"), R("i128"), C("p"), Op.is_lt)
    ts(R("et", 3, 515, 4), R("i128"), C("p"), Op.is_equal)
    snap(C("ph"), C("pb"))
    line(R("f0"), R("tri"), -ULP, 1.0, "v")
    line(C("pl"), C("ph"), -1.0, C("p"), "v")
    fill(R("cc", 0, 2080, 520), -HALF)
    fill(R("ta0"), NONE)
    for t in range(4):
        line(R("iN", 128 * t, 128 * t + 128), R("i128"), 1.0, 128.0 * (t - 2))
    line(R("jf"), R("jq"), 1.0, -HALF - TOP)
    line(R("jm"), R("jq"), 1.0, -HALF)
    line(R("ct"), c8, 1.0, TOP)
    quant(R("qwv", 8, 136), R("ones", 0, 512))
    ts(R("lc"), o8, C("pl"), Op.mult, 16.0, Op.add)
    line(R("d0", 0, 4), R("ones", 0, 4), C("pl"), 0.0)
    line(R("d0", 4, 8), R("iN", 0, 512, 128), 1.0, C("ph"))
    ts(R("m8"), c8, C("ph"), Op.is_equal)
    for t in range(4):
        quant(E(t), R("et", 3 - t, 515 - t))
    for t in range(4):
        line(R("ut", t, 512, 4), o128, 0.0, R("u4", t, t + 1), "va"[t // 3])
    quant(R("cu"), R("ut"))

    def blk(q, n=1):
        return R("ar", 128 * q, 128 * (q + n))

    for q in range(4):
        a, b = 128 * q, 128 * q + 128
        quant(R("qg", a, b), R("grt", 4 * a, 4 * b))
        mm(pb(4 + q), R("qg", a, b), UB)
        mm(pb(q), UB, R("qg", a, b))
        act(C("a%d" % q), pb(4 + q, 1), Act.Abs, TINY)
        act(blk(q), pb(q), Act.Abs, TINY)
        line(R("t0", a, b), R("f0"), C("a%d" % q), 0.0)
    for q in range(4):
        n, size = PLAN["signs"][q], C("a%d" % q)
        if n:
            sg = R("sg", 384 * q, 384 * q + 128 * n)
            act(sg, blk(0, n), Act.Sign, size, -1.0)
            act(sg, sg, Act.Sign, 1.0, -1.0, acc=C("s%d" % q))
        for j in range(n, 4):
            a = 520 * q + 1 + 128 * (j - n)
            if j == q:
                tt(R("cc", a, a + 128), blk(q), R("t0", 128 * q, 128 * q + 128), Op.is_gt)
            else:
                ts(R("cc", a, a + 128), blk(j), size, Op.is_gt if j > q else Op.is_ge)
        m, a = 64 * (4 - n) + 1, 520 * q
        fill(R("cc", a + 2 * m - 1, a + 2 * m), 0.0)
        scan(R("rs", 260 * q + 260 - m, 260 * q + 260), R("cc", a, a + m), R("cc", a + m, a + 2 * m), C("s%d" % q) if n else 0.0)
        r, h = R("rs", 260 * q + 259, 260 * q + 260), R("hq", q, q + 1)
        snap(h, r)
        for k in range(2):
            ts(R("wy", 32 * k + q, 32 * k + 32, 4), c8, h, Op.is_equal, R("d0", 4 * k + q, 4 * k + q + 1), Op.mult)
        ts(R("wy", 64 + q, 576, 4), R("jm"), h, Op.add, r, Op.is_equal)
    quant(R("qwy"), R("wy"))
    gate.append(node("p", lambda: g.wait_ge(T.sem["ready"], nready), [], [], [told]))
    send_codes(0, R("nl", 0, 32), R("qwy", 0, 32), "an0")
    mm(pb(2), WY, R("qwy", 0, 128), True, False)
    mm(pb(2), WY, R("qwy", 8, 136), False, True)
    lw = R("lw0", 0, 8)
    ts(lw, pb(2, 8), 256.0, Op.add)
    pick(R("w0", A0, B0), R("qg"), lw)
    send_set(0)
    mine, wrapped = lw, pb(2, 8)

    fill(R("cwt"), 0.0)
    fill(R("wv", 1, 512, 2), 0.0)
    fill(R("wv", 64, 512, 2), 0.0)
    fill(Y(1), 1.0)
    fill(Y(3), 0.0)
    fill(R("wx", 1, 576, 2), 0.0)
    fill(R("wz", 1, 768, 2), 0.0)
    line(C("pd"), C("ph"), 1.0, -256.0, "v")
    line(C("pc"), C("ph"), 1.0, -128.0, "v")
    copy(R("dv", 0, 1), C("pl"))
    fill(R("cwt", 0, 512, 4), -1.0 / ULP)
    fill(R("cwt", 1, 512, 4), 2.0 ** -7 / ULP)
    fill(R("cwt", 512, 513), 256.0)
    line(R("cwt", 513, 514), R("tri", 0, 1), HALF, 1.0 - HALF)
    fill(R("cwt", 514, 515), 1.0)
    fill(R("cwt", 515, 517), -1.0)
    fill(R("cwt", 517, 518), 2.0 ** -7)
    quant(R("cw"), R("cwt"))
    fill(R("ta1"), NONE)
    fill(R("ta2"), NONE)
    ts(R("idn"), R("i128"), C("p"), Op.is_equal)
    quant(R("qw"), R("wt"))
    fill(R("tk"), 0.0)
    fill(R("nlt", 1, 512, 4), 0.0)
    fill(R("nlt", 512, 1024, 4), 0.0)
    line(R("nlt", 0, 512, 4), R("idn"), -240.0, 0.0)
    line(R("nlt", 513, 1024, 4), R("idn"), -240.0, 0.0)

    nac, nbc, umc, thr, ha, hb = [C(x) for x in ("nac", "nbc", "umc", "thr", "ha", "hb")]
    for b in range(L):
        w, nw, ta, nb, apn = ["%s%d" % (x, b) for x in ("w", "nw", "ta", "nb", "ap")]
        last = b == L - 1
        own, far, mrg = R(w, A0, B0), R(w, B0, W1), R(w, M0, A0)
        nar, nbr = R(nw, A0, B0), R(nw, B0, W1)
        slot = ((C("pl"), C("pc")), (C("pl"), C("sbh")) if last else (R("dv", 0, 1), R("dv", 1, 2)))
        number = ((C("la"), C("nahi")), (R("dv", 2, 3), R("dv", 3, 4)))
        tt(R("x8", 0, 8), wrapped, R("m8"), Op.mult)
        scatter(R(ta), mine, R("i128"))
        rsum(nac, R("x8", 0, 8))
        copy(nar, R("iN"), "a", mine)
        mm(pb(4), UB, own)
        act(R("absa"), pb(4), Act.Abs, TINY * ULP, ULP)
        if not last:
            line(C("nah"), nac, 1.0, -HALF)
            snap(number[0][1], C("nah"))
            line(number[0][0], number[0][1], -1.0, nac)
        else:
            ts(R("nlt", 2, 512, 4), nar, nac, Op.is_gt)
        if b == 0:
            pick(R("nx"), R("nl"), R("lc"))
            mm(pb(6), R("nx"), R("nl", 0, 128), True, False)
            mm(pb(6), R("nx"), R("nl", 8, 136), False, True)
            ts(R(nb), pb(6, 8), 256.0, Op.add)
            tt(R("x8", 8, 16), pb(6, 8), R("m8"), Op.mult)
            rsum(nbc, R("x8", 8, 16))
        else:
            tt(R("xp"), R("iN"), R("idn"), Op.mult, R(nb))
            if scalar("a"):
                act(R("xj"), R("xp"), Act.Copy, acc=nbc)
            else:
                rsum(nbc, R("xp"))
        pick(R(apn), R("wn%d" % b if b else "qg"), R(nb))
        if scalar("a"):
            act(R("mk"), R(ta), Act.Sign, NONE, -1.0, off=R(nb))
        else:
            ts(R("mk"), R(ta), NONE, Op.is_lt, off=R(nb))
        copy(nbr, R("iN"), "a", R(nb))
        for first in (True, False):
            for t in range(4):
                mm(pb(t), E(t), R(apn) if first == bool(PLAN["own_first"][b]) else far, first, not first)
        ts(Y(0), nar, nbc, Op.is_equal)
        ts(Y(2), nar, nbc, Op.is_gt, -1.0, Op.mult)
        if not last:
            line(C("nbh"), nbc, 1.0, -HALF)
            snap(number[1][1], C("nbh"))
            line(number[1][0], number[1][1], -1.0, nbc)
        quant(R("qe"), R("ye"))
        if last:
            ts(R("nlt", 514, 1024, 4), nbr, nac, Op.is_gt)
            ts(R("nlt", 3, 1024, 4), R(nw, A0, W1), nbc, Op.is_gt)
            quant(R("qlt", 0, 128), R("nlt", 0, 512))
            quant(R("qlt", 128, 256), R("nlt", 512, 1024))
            copy(R(nw, M0, A0), nbr)
        mm(pb(6), UB, far)
        mm(pb(7), far, UB)
        mm(pb(4), WU, R("qe"), True, False)
        mm(pb(4), E(2), R("qe"), False, True)
        mm(pb(5), R("qe"), WR)
        line(R("um"), R("mk"), -1.0, 1.0)
        act(R("yj"), Y(0), Act.Identity, 2.0 ** -7, -1.0, acc=umc)
        line(C("sbt"), pb(7, 1), umc, TINY)
        line(slot[1][1], umc, 256.0, C("pd"))
        for t in range(4):
            tt(R("hm", t, 512, 4), pb(t), R("mk"), Op.mult)
        tt(R("sbs"), pb(6), R("um"), Op.mult)
        quant(mrg, R("hm"))
        tt(R("za"), pb(4), R("absa"), Op.mult)
        ts(R("fb"), nbr, nbc, Op.is_ge, 1.0 - ULP, Op.max)
        ts(Y(2), R("i128"), C("p"), Op.is_gt, pb(5, 128, 127), Op.mult)
        if not last:
            ts(R("wz", 256, 768, 4), R("jq"), number[0][0], Op.is_equal, pb(5, 128, 127), Op.mult)
            ts(R("wz", 258, 768, 4), R("jq"), number[1][0], Op.is_equal)
            for sd in range(2):
                for k in range(2):
                    ts(R("wz", 128 * k + 2 * sd, 128 * k + 128, 4), R("iN", 0, 512, 16), number[sd][1], Op.is_equal, slot[sd][k], Op.mult)
            quant(R("qwz"), R("wz"))
            mm(pb(3), R("qwz", 64, 192), R("qwz", 0, 128), True, False)
            mm(pb(3), R("qwz", 64, 192), R("qwz", 32, 160), False, True)
            ts(R("lz"), pb(3, 32), 256.0, Op.add)
            n = 32 // PLAN["chunks"]
            for k in range(PLAN["chunks"]):
                pick(R("wn%d" % (b + 1), 16 * n * k, 16 * n * (k + 1)), R(w), R("lz", n * k, n * k + n))
        mm(pb(1), mrg, UB)
        mm(pb(0), UB, mrg)
        if last:
            mm(pb(3, W1), R("qw"), R(w))
            copy(R("yw"), pb(3, W1))
        act(thr, pb(1, 1), Act.Abs, C("sbt"))
        tt(R("xb"), pb(0), R("sbs"), Op.add)
        line(R("tb"), R("fb"), thr, 0.0)
        ts(Y(3), R("za"), thr, Op.is_ge)
        act(R("rowb"), R("xb"), Act.Abs, TINY)
        quant(R("ql"), R("ye"))
        bank = 5 if last else 7
        mm(pb(bank), R("ql"), WR)
        tt(R("cb"), R("rowb"), R("tb"), Op.is_gt)
        ra, rb, rh = pb(bank, 127, 126), R("rk", 127, 128), R("rk", 255, 256)

        def digits(tile, sd, cs, h, of):
            for k in range(2):
                ts(R(tile, 32 * k + 2 * sd, 32 * k + 32, 4), cs, h, Op.is_equal, of[sd][k], Op.mult)

        def rows(sd, jm, h, r):
            ts(R("wx", 64 + 2 * sd, 576, 4), jm, h, Op.add, r, Op.is_equal)

        scan(R("rk", 0, 128), Y(3), R("cb"), -HALF)
        if last:
            ts(R("tk", 8, 9), ra, 128.0 - 8, Op.is_lt, 31.0 / 32, Op.subtract)
            ts(R("tk", 10, 11), ra, 128.0 - 8, Op.is_lt)
            ts(R("tk", 9, 10), rb, 128.0 - 8, Op.is_lt, 31.0 / 32, Op.subtract)
            ts(R("tk", 11, 12), rb, 128.0 - 8, Op.is_lt)
            quant(R("qtk"), R("tk"))
            mm(pb(6), R("qlt", 0, 128), R("qtk", 2, 130))
            mm(pb(7), R("qlt", 128, 256), R("qtk", 2, 130))
            ra, rb = pb(6, 1), pb(7, 1)
            snap(ha, ra), snap(hb, rb), rows(0, R("jm"), ha, ra), rows(1, R("jm"), hb, rb)
            digits("wx", 0, c8, ha, slot), digits("wx", 1, c8, hb, slot)
        else:
            snap(ha, ra)
            scan(R("rk", 128, 256), Y(3), R("cb"), TOP - HALF)
            rows(0, R("jm"), ha, ra), rows(1, R("jf"), rh, rb)
            for tile, of in (("wx", slot), ("wv", number)):
                digits(tile, 0, c8, ha, of), digits(tile, 1, R("ct"), rh, of)
        quant(R("qwx"), R("wx"))
        mm(pb(2), WX, R("qwx", 0, 128), True, False)
        mm(pb(2), WX, R("qwx", 8, 136), False, True)
        ln = "lw%d" % (b + 1)
        lw, mine, wrapped = R(ln, 0, 8), R(ln, 8, 16), pb(6, 8)
        ts(lw, pb(2, 8), 256.0, Op.add)
        if not last:
            quant(R("qwv", 0, 128), R("wv"))
            mm(pb(6), WX, R("qwv", 0, 128), True, False)
            mm(pb(6), WX, R("qwv", 8, 136), False, True)
            ts(mine, wrapped, 256.0, Op.add)
            pick(R("w%d" % (b + 1), A0, B0), R(w), lw)
            arrive("an%d" % (b + 1), [R("nb%d" % (b + 1))], [send(b + 1, R("nb%d" % (b + 1)), mine, "an%d" % (b + 1), True)])
            send_set(b + 1)
        else:
            pick(R("w3"), R(w), lw)
            dma("a" if scalar("s") else "s", T.oc[:, 0:512], ap(R("w3")).bitcast(dt.uint8), [], [R("w3")])
            copy(R("yo"), R("yw"), "v", lw)
            if scalar("a"):
                act(R("nbo"), R(nw), Act.Identity, 256.0, off=lw)
            else:
                ts(R("nbo"), R(nw), 256.0, Op.add, off=lw)
            for k in range(4):
                dma("a" if scalar("a") else "s", T.osc[4 * k:4 * k + 4, 0:128], T["w3s"][32 * k:32 * k + 4, 0:128], [], [R("w3s")])
            dma("a" if scalar("s") else "s", T.y[:, 0:128], ap(R("yo")), [], [R("yo")])
            dma("a" if scalar("a") else "s", T.nb[0:1, 0:128], T.nbo[0:1, 0:128], [], [R("nbo")])

    PLAN.get("hook", lambda *a: 0)(nodes, either, Q, meet)
    for k in order or range(len(nodes)):
        nodes[k][1]()
    for s in sorted(total, key=lambda s: (s == "out", s)):
        g.wait_ge(T.sem[s], total[s])
